import numpy as np
import ml_dtypes


def mxq(x, axis, fmt="e4m3"):
    dtype, down = {"e4m3": (ml_dtypes.float8_e4m3fn, 7), "e5m2": (ml_dtypes.float8_e5m2, 14)}[fmt]
    v = np.moveaxis(np.asarray(x, np.float32).astype(ml_dtypes.bfloat16).astype(np.float64), axis, -1)
    blocks = v.reshape(v.shape[:-1] + (-1, 32))
    amax = np.abs(blocks).max(-1, keepdims=True)
    byte = np.maximum(np.where(amax > 0, np.frexp(amax)[1] - 1 + 127, 0) - down, 1)
    scale = np.exp2(byte - 127.0)
    codes = (blocks / scale).astype(np.float32).astype(dtype).astype(np.float64)
    return np.moveaxis((codes * scale).reshape(v.shape), -1, axis)


WIDE = False


def mx_kscale(k):
    if not WIDE:
        return np.ones(k)
    levels = np.array([18, -18])
    if k % 512:
        return np.exp2(np.random.permutation(np.resize(levels, k // 32))).repeat(32)
    a = np.empty((k // 512, 16))
    for p in range(k // 512):
        a[p, :8] = np.random.permutation(np.resize(levels, 8))
        for g in range(8):
            far = levels[np.abs(levels - a[p, g]) >= 10]
            a[p, g + 8] = far[np.random.randint(len(far))]
    return np.exp2(a.ravel()).repeat(32)


def f64(x):
    return np.asarray(x).astype(np.float64)


def striped(idx):
    return np.tile(np.asarray(idx).reshape(-1, 16).T, (8, 1)).astype(np.uint16)


def unstriped(offs):
    return offs[:16].T.reshape(-1).astype(np.int64)


B, N, T, D, R = 1, 512, 1024, 512, 1024
LR = 0.1
BETA = 0.5
RHO = 0.9
EPS = 0.001


def setup_inputs():
    n = np.random.standard_normal
    idx = np.random.permutation(T)[:B * N]
    s = mx_kscale(D)[:, None]
    z = mx_kscale(R)[:, None]
    x = n((B, D, R))
    return {
        "xT": (x * s).astype(np.float32),
        "wT": (n((D, T)) * (1.00 / np.sqrt(D)) / s).astype(np.float32),
        "y": (2 * np.random.randint(0, 2, (B, R, N)) - 1).astype(np.float32),
        "wt": (np.random.uniform(0.5, 1.5, (B, R, 1)) * 1.0 / np.sqrt(R) * z).astype(np.float32),
        "xm": (x.transpose(0, 2, 1) / z).astype(np.float32),
        "mT": (0.3 * n((D, T))).astype(np.float32),
        "vT": (np.random.uniform(0.1, 0.5, (D, T))).astype(np.float32),
        "offs": striped(idx),
    }


def reference(xT, wT, y, wt, xm, mT, vT, offs):
    idx = unstriped(offs)
    pick = lambda x: x[:, idx].reshape(x.shape[0], B, N).transpose(1, 0, 2)
    a = mxq(f64(xT), 1, "e4m3").transpose(0, 2, 1) @ mxq(pick(f64(wT)), 1, "e4m3")
    g = -f64(wt) * f64(y) * np.maximum(1.0 - f64(y) * a, 0.0)
    dw = mxq(f64(xm), 1, "e4m3").transpose(0, 2, 1) @ mxq(g, 1, "e5m2")
    nm = BETA * pick(f64(mT)) + (1.0 - BETA) * dw
    nv = RHO * pick(f64(vT)) + (1.0 - RHO) * dw * dw
    nw = -LR * nm / (np.sqrt(nv) + EPS)
    tables = []
    for old, new in ((wT, nw), (mT, nm), (vT, nv),):
        table = f64(old) if old is not wT else np.zeros((D, T))
        table[:, idx] = new.transpose(1, 0, 2).reshape(D, B * N)
        tables.append(table)
    return tuple(tables)

@@ -1,0 +1,250 @@
+import math
+from contextlib import ExitStack
+
+import concourse.mybir as mybir
+from concourse.masks import make_identity
+
+N, T, D, R = 512, 1024, 512, 1024
+LR, BETA, RHO, EPS = 0.1, 0.5, 0.9, 0.001
+FLOPS = 2 * 2 * R * N * D
+
+F32 = mybir.dt.float32
+BF16 = mybir.dt.bfloat16
+U32 = mybir.dt.uint32
+U16 = mybir.dt.uint16
+U8 = mybir.dt.uint8
+E4M3 = mybir.dt.float8_e4m3fn_x4
+E5M2 = mybir.dt.float8_e5m2_x4
+ALU = mybir.AluOpType
+ACT = mybir.ActivationFunctionType
+
+P = 128
+PACK = 4
+K_PASS = P * PACK
+PASSES = R // K_PASS
+D_TILES = D // P
+
+
+def tile_attend_gsqh_adam_kernel(tc, xT, wT, y, wt, xm, mT, vT, offs, out_0, out_1, out_2):
+    nc = tc.nc
+    with ExitStack() as ctx:
+        keep = ctx.enter_context(tc.tile_pool(name="keep", bufs=1))
+        ring = ctx.enter_context(tc.tile_pool(name="ring", bufs=2))
+        psum = ctx.enter_context(tc.psum_pool(name="psum", bufs=1))
+
+        def table_tile(tag):
+            return keep.tile([P, T], F32, name=tag, tag=tag, align_bytes=64)
+
+        def wide_tile(tag):
+            return keep.tile([P, PACK, K_PASS], F32, name=tag, tag=tag, align_bytes=64)
+
+        def woven_tile(tag):
+            return keep.tile([P, PACK * K_PASS], BF16, name=tag, tag=tag, align_bytes=64)
+
+        def weave_views(woven, planes):
+            return (woven[:].rearrange("p (c i t) -> p c t i", i=PACK, t=PACK),
+                    planes[:].rearrange("p t (c i) -> p c t i", i=PACK))
+
+        def deal_views(woven, planes):
+            return (woven[:].rearrange("p (t s j) -> p s j t", t=PACK, j=PACK),
+                    planes[:].rearrange("p j (s t) -> p s j t", t=PACK))
+
+        def quantize(tag, woven, fmt):
+            codes = keep.tile([P, K_PASS], U32, name=tag + "_codes", align_bytes=64)
+            scales = keep.tile([P, K_PASS], U8, name=tag + "_scales", align_bytes=64)
+            nc.vector.quantize_mx(out=codes[:].bitcast(fmt), scales=scales[:], in_=woven[:])
+            return codes, scales
+
+        offsets = keep.tile([P, N // 16], U16, name="offsets")
+        nc.sync.dma_start(offsets[:], offs)
+
+        w_rows = wT.rearrange("(p t) c -> t p c", t=PACK)
+        w_tab = [table_tile("tab_a%d" % t) for t in range(PACK)]
+        x_raw = [wide_tile("wide_x%d" % g) for g in range(PASSES)]
+        y_raw = [wide_tile("wide_y%d" % g) for g in range(PASSES)]
+        xm_raw = [wide_tile("wide_xm%d" % g) for g in range(PASSES)]
+        m_tab = [table_tile("m_tab%d" % j) for j in range(D_TILES)]
+        v_tab = [table_tile("v_tab%d" % j) for j in range(D_TILES)]
+        m_win = [table_tile("m_win%d" % j) for j in range(D_TILES)]
+        step_win = [table_tile("step_win%d" % j) for j in range(D_TILES)]
+        wt_sb = keep.tile([P, PASSES, PACK], F32, name="wt_sb")
+
+        def rows(g):
+            return slice(g * K_PASS, (g + 1) * K_PASS)
+
+        def feats(j):
+            return slice(j * P, (j + 1) * P)
+
+        def load_x(g):
+            nc.sync.dma_start(x_raw[g][:], xT[0, :, rows(g)].rearrange("(p j) r -> p j r", j=PACK))
+
+        def load_y(g):
+            src = y[0, rows(g), :].rearrange("(p t) n -> p t n", t=PACK)
+            for h in range(2):
+                nc.sync.dma_start(y_raw[g][:, 2 * h:2 * h + 2, :], src[:, 2 * h:2 * h + 2, :])
+
+        def load_xm(g):
+            nc.sync.dma_start(xm_raw[g][:], xm[0, rows(g), :].rearrange("(p t) d -> p t d", t=PACK))
+
+        def load_table(tile, table, j):
+            nc.sync.dma_start(tile[:], table[feats(j), :])
+
+        for t in range(PACK):
+            nc.sync.dma_start(w_tab[t][:], w_rows[t])
+        load_x(0)
+        nc.sync.dma_start(wt_sb[:], wt[0].rearrange("(g p t) o -> p g (t o)", p=P, t=PACK))
+        load_y(0)
+        load_x(1)
+        load_table(v_tab[0], vT, 0)
+        load_xm(0)
+        load_y(1)
+        load_table(v_tab[1], vT, 1)
+        load_xm(1)
+        load_table(v_tab[2], vT, 2)
+        load_table(v_tab[3], vT, 3)
+
+        for j in range(D_TILES):
+            (nc.vector if j == 0 else nc.gpsimd).memset(step_win[j][:], 0.0)
+        ident = keep.tile([P, P], F32, name="ident")
+        make_identity(nc, ident[:])
+        one = keep.tile([P, 1], F32, name="one")
+        nc.vector.memset(one[:], 1.0)
+        eps = keep.tile([P, 1], F32, name="eps")
+        nc.vector.tensor_scalar(eps[:], one[:], EPS, None, ALU.mult)
+        neg_wt = keep.tile([P, PASSES, PACK], F32, name="neg_wt")
+
+        w_got = wide_tile("w_got")
+        for t in range(PACK):
+            nc.vector.tensor_copy(w_got[:, t, :], w_tab[t][:].indirect(offsets[:]))
+        w_woven = woven_tile("w_woven")
+        nc.vector.tensor_copy(*weave_views(w_woven, w_got))
+        w_codes, w_scales = quantize("w", w_woven, E4M3)
+        nc.vector.tensor_scalar(neg_wt[:], wt_sb[:], -1.0, None, ALU.mult)
+
+        v_win = [table_tile("tab_a%d" % j) for j in range(D_TILES)]
+        for j in range(D_TILES):
+            load_table(m_tab[j], mT, j)
+        for j in range(D_TILES):
+            load_table(v_win[j], vT, j)
+        for j in range(D_TILES):
+            load_table(m_win[j], mT, j)
+
+        v_got = wide_tile("v_got")
+        v_decayed = wide_tile("v_decayed")
+        m_got = wide_tile("m_got")
+
+        def gather_v(j):
+            nc.vector.tensor_copy(v_got[:, j, :], v_tab[j][:].indirect(offsets[:]))
+
+        def gather_m(j):
+            nc.vector.tensor_copy(m_got[:, j, :], m_tab[j][:].indirect(offsets[:]))
+
+        def weave_x(g):
+            woven = woven_tile("x_woven%d" % g)
+            dst, src = deal_views(woven, x_raw[g])
+            if g == 0:
+                nc.scalar.copy(dst[:, :P // 2], src[:, :P // 2])
+                nc.vector.tensor_copy(dst[:, P // 2:], src[:, P // 2:])
+            else:
+                nc.scalar.copy(dst, src)
+            return woven
+
+        def gradient(g, x_codes, x_scales):
+            g_planes = keep.tile([P, PACK, N], BF16, name="g_planes%d" % g, align_bytes=64)
+            hinge = []
+
+            def margin(t):
+                scores = psum.tile([P, N], F32, name="bank_a%d" % t, tag="bank_a%d" % t)
+                nc.tensor.matmul_mx(out=scores[:], lhsT=x_codes[:, feats(t)].bitcast(E4M3), lhsT_scale=x_scales[:, feats(t)],
+                                    rhs=w_codes[:].bitcast(E4M3), rhs_scale=w_scales[:], start=True, stop=True)
+                ya = ring.tile([P, N], F32, name="ya")
+                nc.vector.tensor_tensor(ya[:], scores[:], y_raw[g][:, t, :], ALU.mult)
+                h = ring.tile([P, N], F32, name="h")
+                nc.scalar.activation(h[:], ya[:], ACT.Relu, bias=one[:], scale=-1.0)
+                hinge.append(h)
+
+            def weigh(t):
+                nc.vector.scalar_tensor_tensor(g_planes[:, t, :], hinge[t][:], neg_wt[:, g, t:t + 1], y_raw[g][:, t, :],
+                                               ALU.mult, ALU.mult)
+
+            margin(0)
+            for t in range(1, PACK):
+                margin(t)
+                weigh(t - 1)
+            weigh(PACK - 1)
+            return g_planes
+
+        def weave_plain(tag, planes):
+            woven = woven_tile(tag)
+            nc.scalar.copy(*weave_views(woven, planes))
+            return woven
+
+        dw = [psum.tile([P, N], F32, name="bank_d%d" % j, tag="bank_d%d" % j) for j in range(D_TILES)]
+
+        def dw_pass(g, xm_q, g_q):
+            for j in range(D_TILES):
+                nc.tensor.matmul_mx(out=dw[j][:], lhsT=xm_q[0][:, feats(j)].bitcast(E4M3), lhsT_scale=xm_q[1][:, feats(j)],
+                                    rhs=g_q[0][:].bitcast(E5M2), rhs_scale=g_q[1][:], start=(g == 0), stop=(g == PASSES - 1))
+
+        x_q0 = quantize("x0", weave_x(0), E4M3)
+        x_woven1 = weave_x(1)
+        g_planes0 = gradient(0, *x_q0)
+        x_q1 = quantize("x1", x_woven1, E4M3)
+        gather_v(0)
+        g_woven0 = weave_plain("g_woven0", g_planes0)
+        g_planes1 = gradient(1, *x_q1)
+        xm_woven0 = weave_plain("xm_woven0", xm_raw[0])
+        g_q0 = quantize("g0", g_woven0, E5M2)
+        xm_q0 = quantize("xm0", xm_woven0, E4M3)
+        dw_pass(0, xm_q0, g_q0)
+        g_woven1 = weave_plain("g_woven1", g_planes1)
+        xm_woven1 = weave_plain("xm_woven1", xm_raw[1])
+        g_q1 = quantize("g1", g_woven1, E5M2)
+        xm_q1 = quantize("xm1", xm_woven1, E4M3)
+        dw_pass(1, xm_q1, g_q1)
+        for j in range(1, D_TILES):
+            gather_v(j)
+        for j in range(D_TILES):
+            gather_m(j)
+
+        dw_sq = wide_tile("wide_x0")
+        dw_sb = wide_tile("wide_x1")
+        nm_t = wide_tile("wide_y0")
+        nm = wide_tile("wide_xm0")
+        root_t = wide_tile("wide_y1")
+        rate = wide_tile("wide_xm1")
+
+        def turned_sum(j, first, second):
+            bank = psum.tile([P, PACK, P], F32, name="bank_a%d" % j, tag="bank_a%d" % j)
+            for b in range(N // P):
+                nc.tensor.matmul(bank[:, b, :], first[:, j, feats(b)], ident[:], start=True, stop=False, is_transpose=True)
+                nc.tensor.matmul(bank[:, b, :], second[:, j, feats(b)], ident[:], start=False, stop=True, is_transpose=True)
+            return bank[:].rearrange("p b d -> p (b d)")
+
+        def turn_back(j, turned):
+            bank = psum.tile([P, N], F32, name="bank_d%d" % j, tag="bank_d%d" % j)
+            for b in range(N // P):
+                nc.tensor.transpose(bank[:, feats(b)], turned[:, j, feats(b)], ident[:])
+            return bank[:]
+
+        for j in range(D_TILES):
+            nc.scalar.activation(v_decayed[:, j, :], v_got[:, j, :], ACT.Copy, scale=RHO)
+            nc.scalar.activation(dw_sq[:, j, :], dw[j][:], ACT.Square, scale=math.sqrt(1.0 - RHO))
+            nc.vector.tensor_tensor(v_win[j][:].indirect(offsets[:]), v_decayed[:, j, :], dw_sq[:, j, :], ALU.add)
+            nc.sync.dma_start(out_2[feats(j), :], v_win[j][:])
+        for j in range(D_TILES):
+            nc.scalar.copy(dw_sb[:, j, :], dw[j][:])
+        for j in range(D_TILES):
+            nc.scalar.activation(nm_t[:, j, :], turned_sum(j, m_got, dw_sb), ACT.Copy, scale=BETA)
+        for j in range(D_TILES):
+            nc.scalar.copy(nm[:, j, :], turn_back(j, nm_t))
+            nc.vector.tensor_copy(m_win[j][:].indirect(offsets[:]), nm[:, j, :])
+            nc.sync.dma_start(out_1[feats(j), :], m_win[j][:])
+        for j in range(D_TILES):
+            nc.scalar.activation(root_t[:, j, :], turned_sum(j, v_decayed, dw_sq), ACT.Sqrt)
+        nc.scalar.activation(root_t[:], root_t[:], ACT.Square, bias=eps[:])
+        nc.scalar.activation(root_t[:], root_t[:], ACT.Abs_reciprocal_sqrt)
+        for j in range(D_TILES):
+            nc.scalar.activation(rate[:, j, :], turn_back(j, root_t), ACT.Copy, scale=-LR)
+            nc.vector.tensor_tensor(step_win[j][:].indirect(offsets[:]), nm[:, j, :], rate[:, j, :], ALU.mult)
+            nc.sync.dma_start(out_0[feats(j), :], step_win[j][:])

@@ -29,7 +29,7 @@ def tile_attend_gsqh_adam_kernel(tc, xT, wT, y, wt, xm, mT, vT, offs, out_0, out
     nc = tc.nc
     with ExitStack() as ctx:
         keep = ctx.enter_context(tc.tile_pool(name="keep", bufs=1))
-        ring = ctx.enter_context(tc.tile_pool(name="ring", bufs=2))
+        ring = ctx.enter_context(tc.tile_pool(name="ring", bufs=4))
         psum = ctx.enter_context(tc.psum_pool(name="psum", bufs=1))
 
         def table_tile(tag):
@@ -49,10 +49,11 @@ def tile_attend_gsqh_adam_kernel(tc, xT, wT, y, wt, xm, mT, vT, offs, out_0, out
             return (woven[:].rearrange("p (t s j) -> p s j t", t=PACK, j=PACK),
                     planes[:].rearrange("p j (s t) -> p s j t", t=PACK))
 
-        def quantize(tag, woven, fmt):
+        def quantize(tag, woven, fmt, cuts=(0, K_PASS)):
             codes = keep.tile([P, K_PASS], U32, name=tag + "_codes", align_bytes=64)
             scales = keep.tile([P, K_PASS], U8, name=tag + "_scales", align_bytes=64)
-            nc.vector.quantize_mx(out=codes[:].bitcast(fmt), scales=scales[:], in_=woven[:])
+            for lo, hi in zip(cuts, cuts[1:]):
+                nc.vector.quantize_mx(out=codes[:, lo:hi].bitcast(fmt), scales=scales[:, lo:hi], in_=woven[:, PACK * lo:PACK * hi])
             return codes, scales
 
         offsets = keep.tile([P, N // 16], U16, name="offsets")
@@ -75,8 +76,11 @@ def tile_attend_gsqh_adam_kernel(tc, xT, wT, y, wt, xm, mT, vT, offs, out_0, out
         def feats(j):
             return slice(j * P, (j + 1) * P)
 
-        def load_x(g):
-            nc.sync.dma_start(x_raw[g][:], xT[0, :, rows(g)].rearrange("(p j) r -> p j r", j=PACK))
+        def load_x(g, parts):
+            src = xT[0, :, rows(g)].rearrange("(p j) r -> p j r", j=PACK)
+            width = K_PASS // parts
+            for h in range(parts):
+                nc.sync.dma_start(x_raw[g][:, :, h * width:(h + 1) * width], src[:, :, h * width:(h + 1) * width])
 
         def load_y(g):
             src = y[0, rows(g), :].rearrange("(p t) n -> p t n", t=PACK)
@@ -91,35 +95,35 @@ def tile_attend_gsqh_adam_kernel(tc, xT, wT, y, wt, xm, mT, vT, offs, out_0, out
 
         for t in range(PACK):
             nc.sync.dma_start(w_tab[t][:], w_rows[t])
-        load_x(0)
+        load_x(0, 2)
         nc.sync.dma_start(wt_sb[:], wt[0].rearrange("(g p t) o -> p g (t o)", p=P, t=PACK))
         load_y(0)
-        load_x(1)
+        load_x(1, 1)
         load_table(v_tab[0], vT, 0)
-        load_xm(0)
         load_y(1)
         load_table(v_tab[1], vT, 1)
+        load_xm(0)
         load_xm(1)
-        load_table(v_tab[2], vT, 2)
-        load_table(v_tab[3], vT, 3)
+        for j in range(2, D_TILES):
+            load_table(v_tab[j], vT, j)
 
-        for j in range(D_TILES):
-            (nc.vector if j == 0 else nc.gpsimd).memset(step_win[j][:], 0.0)
-        ident = keep.tile([P, P], F32, name="ident")
-        make_identity(nc, ident[:])
         one = keep.tile([P, 1], F32, name="one")
         nc.vector.memset(one[:], 1.0)
+        for j in range(D_TILES):
+            (nc.gpsimd if j == D_TILES - 1 else nc.vector).memset(step_win[j][:], 0.0)
+        ident = keep.tile([P, P], F32, name="ident")
+        make_identity(nc, ident[:])
         eps = keep.tile([P, 1], F32, name="eps")
-        nc.vector.tensor_scalar(eps[:], one[:], EPS, None, ALU.mult)
+        nc.scalar.activation(eps[:], one[:], ACT.Copy, scale=EPS)
         neg_wt = keep.tile([P, PASSES, PACK], F32, name="neg_wt")
 
         w_got = wide_tile("w_got")
         for t in range(PACK):
             nc.vector.tensor_copy(w_got[:, t, :], w_tab[t][:].indirect(offsets[:]))
         w_woven = woven_tile("w_woven")
-        nc.vector.tensor_copy(*weave_views(w_woven, w_got))
-        w_codes, w_scales = quantize("w", w_woven, E4M3)
-        nc.vector.tensor_scalar(neg_wt[:], wt_sb[:], -1.0, None, ALU.mult)
+        dst, src = weave_views(w_woven, w_got)
+        nc.scalar.copy(dst[:, :, :2, :], src[:, :, :2, :])
+        nc.vector.tensor_copy(dst[:, :, 2:, :], src[:, :, 2:, :])
 
         v_win = [table_tile("tab_a%d" % j) for j in range(D_TILES)]
         for j in range(D_TILES):
@@ -129,22 +133,20 @@ def tile_attend_gsqh_adam_kernel(tc, xT, wT, y, wt, xm, mT, vT, offs, out_0, out
         for j in range(D_TILES):
             load_table(m_win[j], mT, j)
 
-        v_got = wide_tile("v_got")
         v_decayed = wide_tile("v_decayed")
-        m_got = wide_tile("m_got")
 
-        def gather_v(j):
-            nc.vector.tensor_copy(v_got[:, j, :], v_tab[j][:].indirect(offsets[:]))
-
-        def gather_m(j):
-            nc.vector.tensor_copy(m_got[:, j, :], m_tab[j][:].indirect(offsets[:]))
+        def gather(table, tag):
+            got = keep.tile([P, N], F32, name=tag, tag=tag, align_bytes=64)
+            nc.vector.tensor_copy(got[:], table[:].indirect(offsets[:]))
+            return got
 
         def weave_x(g):
             woven = woven_tile("x_woven%d" % g)
             dst, src = deal_views(woven, x_raw[g])
             if g == 0:
                 nc.scalar.copy(dst[:, :P // 2], src[:, :P // 2])
-                nc.vector.tensor_copy(dst[:, P // 2:], src[:, P // 2:])
+                nc.scalar.copy(dst[:, P // 2:3 * P // 4], src[:, P // 2:3 * P // 4])
+                nc.vector.tensor_copy(dst[:, 3 * P // 4:], src[:, 3 * P // 4:])
             else:
                 nc.scalar.copy(dst, src)
             return woven
@@ -167,11 +169,10 @@ def tile_attend_gsqh_adam_kernel(tc, xT, wT, y, wt, xm, mT, vT, offs, out_0, out
                 nc.vector.scalar_tensor_tensor(g_planes[:, t, :], hinge[t][:], neg_wt[:, g, t:t + 1], y_raw[g][:, t, :],
                                                ALU.mult, ALU.mult)
 
-            margin(0)
-            for t in range(1, PACK):
+            for t in range(PACK):
                 margin(t)
-                weigh(t - 1)
-            weigh(PACK - 1)
+            for t in range(PACK):
+                weigh(t)
             return g_planes
 
         def weave_plain(tag, planes):
@@ -186,26 +187,21 @@ def tile_attend_gsqh_adam_kernel(tc, xT, wT, y, wt, xm, mT, vT, offs, out_0, out
                 nc.tensor.matmul_mx(out=dw[j][:], lhsT=xm_q[0][:, feats(j)].bitcast(E4M3), lhsT_scale=xm_q[1][:, feats(j)],
                                     rhs=g_q[0][:].bitcast(E5M2), rhs_scale=g_q[1][:], start=(g == 0), stop=(g == PASSES - 1))
 
-        x_q0 = quantize("x0", weave_x(0), E4M3)
-        x_woven1 = weave_x(1)
+        x_woven0 = weave_x(0)
+        w_codes, w_scales = quantize("w", w_woven, E4M3)
+        x_q0 = quantize("x0", x_woven0, E4M3, cuts=(0, P, 2 * P, K_PASS))
+        nc.scalar.activation(neg_wt[:], wt_sb[:], ACT.Copy, scale=-1.0)
         g_planes0 = gradient(0, *x_q0)
-        x_q1 = quantize("x1", x_woven1, E4M3)
-        gather_v(0)
-        g_woven0 = weave_plain("g_woven0", g_planes0)
+        x_q1 = quantize("x1", weave_x(1), E4M3)
         g_planes1 = gradient(1, *x_q1)
-        xm_woven0 = weave_plain("xm_woven0", xm_raw[0])
-        g_q0 = quantize("g0", g_woven0, E5M2)
-        xm_q0 = quantize("xm0", xm_woven0, E4M3)
+        g_q0 = quantize("g0", weave_plain("g_woven0", g_planes0), E5M2)
+        xm_q0 = quantize("xm0", weave_plain("xm_woven0", xm_raw[0]), E4M3)
         dw_pass(0, xm_q0, g_q0)
-        g_woven1 = weave_plain("g_woven1", g_planes1)
-        xm_woven1 = weave_plain("xm_woven1", xm_raw[1])
-        g_q1 = quantize("g1", g_woven1, E5M2)
-        xm_q1 = quantize("xm1", xm_woven1, E4M3)
+        g_q1 = quantize("g1", weave_plain("g_woven1", g_planes1), E5M2)
+        xm_q1 = quantize("xm1", weave_plain("xm_woven1", xm_raw[1]), E4M3)
         dw_pass(1, xm_q1, g_q1)
-        for j in range(1, D_TILES):
-            gather_v(j)
-        for j in range(D_TILES):
-            gather_m(j)
+        v_got = [gather(v_tab[j], tag) for j, tag in enumerate(("v_got0", "x_woven1", "v_got2", "v_got3"))]
+        m_got = [gather(m_tab[j], tag) for j, tag in enumerate(("m_got0", "m_got1", "g_woven1", "xm_woven1"))]
 
         dw_sq = wide_tile("wide_x0")
         dw_sb = wide_tile("wide_x1")
@@ -217,8 +213,8 @@ def tile_attend_gsqh_adam_kernel(tc, xT, wT, y, wt, xm, mT, vT, offs, out_0, out
         def turned_sum(j, first, second):
             bank = psum.tile([P, PACK, P], F32, name="bank_a%d" % j, tag="bank_a%d" % j)
             for b in range(N // P):
-                nc.tensor.matmul(bank[:, b, :], first[:, j, feats(b)], ident[:], start=True, stop=False, is_transpose=True)
-                nc.tensor.matmul(bank[:, b, :], second[:, j, feats(b)], ident[:], start=False, stop=True, is_transpose=True)
+                nc.tensor.matmul(bank[:, b, :], first[:, feats(b)], ident[:], start=True, stop=False, is_transpose=True)
+                nc.tensor.matmul(bank[:, b, :], second[:, feats(b)], ident[:], start=False, stop=True, is_transpose=True)
             return bank[:].rearrange("p b d -> p (b d)")
 
         def turn_back(j, turned):
@@ -228,20 +224,20 @@ def tile_attend_gsqh_adam_kernel(tc, xT, wT, y, wt, xm, mT, vT, offs, out_0, out
             return bank[:]
 
         for j in range(D_TILES):
-            nc.scalar.activation(v_decayed[:, j, :], v_got[:, j, :], ACT.Copy, scale=RHO)
+            nc.scalar.activation(v_decayed[:, j, :], v_got[j][:], ACT.Copy, scale=RHO)
             nc.scalar.activation(dw_sq[:, j, :], dw[j][:], ACT.Square, scale=math.sqrt(1.0 - RHO))
             nc.vector.tensor_tensor(v_win[j][:].indirect(offsets[:]), v_decayed[:, j, :], dw_sq[:, j, :], ALU.add)
             nc.sync.dma_start(out_2[feats(j), :], v_win[j][:])
         for j in range(D_TILES):
             nc.scalar.copy(dw_sb[:, j, :], dw[j][:])
         for j in range(D_TILES):
-            nc.scalar.activation(nm_t[:, j, :], turned_sum(j, m_got, dw_sb), ACT.Copy, scale=BETA)
+            nc.scalar.activation(nm_t[:, j, :], turned_sum(j, m_got[j], dw_sb[:, j, :]), ACT.Copy, scale=BETA)
         for j in range(D_TILES):
             nc.scalar.copy(nm[:, j, :], turn_back(j, nm_t))
             nc.vector.tensor_copy(m_win[j][:].indirect(offsets[:]), nm[:, j, :])
             nc.sync.dma_start(out_1[feats(j), :], m_win[j][:])
         for j in range(D_TILES):
-            nc.scalar.activation(root_t[:, j, :], turned_sum(j, v_decayed, dw_sq), ACT.Sqrt)
+            nc.scalar.activation(root_t[:, j, :], turned_sum(j, v_decayed[:, j, :], dw_sq[:, j, :]), ACT.Sqrt)
         nc.scalar.activation(root_t[:], root_t[:], ACT.Square, bias=eps[:])
         nc.scalar.activation(root_t[:], root_t[:], ACT.Abs_reciprocal_sqrt)
         for j in range(D_TILES):

@@ -23,19 +23,23 @@ PACK = 4
 K_PASS = P * PACK
 PASSES = R // K_PASS
 D_TILES = D // P
+LIST_BAND = 16
+
+assert D == K_PASS and N == K_PASS and PASSES == 2
+assert BETA == 1.0 - BETA
 
 
 def tile_attend_gsqh_adam_kernel(tc, xT, wT, y, wt, xm, mT, vT, offs, out_0, out_1, out_2):
     nc = tc.nc
     with ExitStack() as ctx:
         keep = ctx.enter_context(tc.tile_pool(name="keep", bufs=1))
-        ring = ctx.enter_context(tc.tile_pool(name="ring", bufs=4))
+        ring = ctx.enter_context(tc.tile_pool(name="ring", bufs=PACK))
         psum = ctx.enter_context(tc.psum_pool(name="psum", bufs=1))
 
         def table_tile(tag):
             return keep.tile([P, T], F32, name=tag, tag=tag, align_bytes=64)
 
-        def wide_tile(tag):
+        def quad_tile(tag):
             return keep.tile([P, PACK, K_PASS], F32, name=tag, tag=tag, align_bytes=64)
 
         def woven_tile(tag):
@@ -53,52 +57,54 @@ def tile_attend_gsqh_adam_kernel(tc, xT, wT, y, wt, xm, mT, vT, offs, out_0, out
             codes = keep.tile([P, K_PASS], U32, name=tag + "_codes", align_bytes=64)
             scales = keep.tile([P, K_PASS], U8, name=tag + "_scales", align_bytes=64)
             for lo, hi in zip(cuts, cuts[1:]):
-                nc.vector.quantize_mx(out=codes[:, lo:hi].bitcast(fmt), scales=scales[:, lo:hi], in_=woven[:, PACK * lo:PACK * hi])
+                nc.vector.quantize_mx(out=codes[:, lo:hi].bitcast(fmt), scales=scales[:, lo:hi],
+                                      in_=woven[:, PACK * lo:PACK * hi])
             return codes, scales
 
-        offsets = keep.tile([P, N // 16], U16, name="offsets")
+        def pass_rows(g):
+            return slice(g * K_PASS, (g + 1) * K_PASS)
+
+        def block(n):
+            return slice(n * P, (n + 1) * P)
+
+        offsets = keep.tile([P, N // LIST_BAND], U16, name="offsets")
         nc.sync.dma_start(offsets[:], offs)
 
-        w_rows = wT.rearrange("(p t) c -> t p c", t=PACK)
-        w_tab = [table_tile("tab_a%d" % t) for t in range(PACK)]
-        x_raw = [wide_tile("wide_x%d" % g) for g in range(PASSES)]
-        y_raw = [wide_tile("wide_y%d" % g) for g in range(PASSES)]
-        xm_raw = [wide_tile("wide_xm%d" % g) for g in range(PASSES)]
+        w_planes = wT.rearrange("(p t) c -> t p c", t=PACK)
+        w_tab = [table_tile("w_tab%d" % t) for t in range(PACK)]
+        x_raw = [quad_tile("x_raw%d" % g) for g in range(PASSES)]
+        y_raw = [quad_tile("y_raw%d" % g) for g in range(PASSES)]
+        xm_raw = [quad_tile("xm_raw%d" % g) for g in range(PASSES)]
         m_tab = [table_tile("m_tab%d" % j) for j in range(D_TILES)]
         v_tab = [table_tile("v_tab%d" % j) for j in range(D_TILES)]
         m_win = [table_tile("m_win%d" % j) for j in range(D_TILES)]
         step_win = [table_tile("step_win%d" % j) for j in range(D_TILES)]
         wt_sb = keep.tile([P, PASSES, PACK], F32, name="wt_sb")
 
-        def rows(g):
-            return slice(g * K_PASS, (g + 1) * K_PASS)
-
-        def feats(j):
-            return slice(j * P, (j + 1) * P)
-
         def load_x(g, parts):
-            src = xT[0, :, rows(g)].rearrange("(p j) r -> p j r", j=PACK)
+            src = xT[0, :, pass_rows(g)].rearrange("(p j) r -> p j r", j=PACK)
             width = K_PASS // parts
-            for h in range(parts):
-                nc.sync.dma_start(x_raw[g][:, :, h * width:(h + 1) * width], src[:, :, h * width:(h + 1) * width])
+            for part in range(parts):
+                cols = slice(part * width, (part + 1) * width)
+                nc.sync.dma_start(x_raw[g][:, :, cols], src[:, :, cols])
 
         def load_y(g):
-            src = y[0, rows(g), :].rearrange("(p t) n -> p t n", t=PACK)
-            for h in range(2):
-                nc.sync.dma_start(y_raw[g][:, 2 * h:2 * h + 2, :], src[:, 2 * h:2 * h + 2, :])
+            src = y[0, pass_rows(g), :].rearrange("(p t) n -> p t n", t=PACK)
+            for t in range(0, PACK, 2):
+                nc.sync.dma_start(y_raw[g][:, t:t + 2, :], src[:, t:t + 2, :])
 
         def load_xm(g):
-            nc.sync.dma_start(xm_raw[g][:], xm[0, rows(g), :].rearrange("(p t) d -> p t d", t=PACK))
+            nc.sync.dma_start(xm_raw[g][:], xm[0, pass_rows(g), :].rearrange("(p t) d -> p t d", t=PACK))
 
         def load_table(tile, table, j):
-            nc.sync.dma_start(tile[:], table[feats(j), :])
+            nc.sync.dma_start(tile[:], table[block(j), :])
 
         for t in range(PACK):
-            nc.sync.dma_start(w_tab[t][:], w_rows[t])
-        load_x(0, 2)
+            nc.sync.dma_start(w_tab[t][:], w_planes[t])
+        load_x(0, parts=2)
         nc.sync.dma_start(wt_sb[:], wt[0].rearrange("(g p t) o -> p g (t o)", p=P, t=PACK))
         load_y(0)
-        load_x(1, 1)
+        load_x(1, parts=1)
         load_table(v_tab[0], vT, 0)
         load_y(1)
         load_table(v_tab[1], vT, 1)
@@ -117,15 +123,15 @@ def tile_attend_gsqh_adam_kernel(tc, xT, wT, y, wt, xm, mT, vT, offs, out_0, out
         nc.scalar.activation(eps[:], one[:], ACT.Copy, scale=EPS)
         neg_wt = keep.tile([P, PASSES, PACK], F32, name="neg_wt")
 
-        w_got = wide_tile("w_got")
+        w_got = quad_tile("w_got")
         for t in range(PACK):
             nc.vector.tensor_copy(w_got[:, t, :], w_tab[t][:].indirect(offsets[:]))
         w_woven = woven_tile("w_woven")
-        dst, src = weave_views(w_woven, w_got)
-        nc.scalar.copy(dst[:, :, :2, :], src[:, :, :2, :])
-        nc.vector.tensor_copy(dst[:, :, 2:, :], src[:, :, 2:, :])
+        w_dst, w_src = weave_views(w_woven, w_got)
+        nc.scalar.copy(w_dst[:, :, :2, :], w_src[:, :, :2, :])
+        nc.vector.tensor_copy(w_dst[:, :, 2:, :], w_src[:, :, 2:, :])
 
-        v_win = [table_tile("tab_a%d" % j) for j in range(D_TILES)]
+        v_win = [table_tile("w_tab%d" % j) for j in range(D_TILES)]
         for j in range(D_TILES):
             load_table(m_tab[j], mT, j)
         for j in range(D_TILES):
@@ -133,49 +139,43 @@ def tile_attend_gsqh_adam_kernel(tc, xT, wT, y, wt, xm, mT, vT, offs, out_0, out
         for j in range(D_TILES):
             load_table(m_win[j], mT, j)
 
-        v_decayed = wide_tile("v_decayed")
+        v_decayed = quad_tile("v_decayed")
 
         def gather(table, tag):
             got = keep.tile([P, N], F32, name=tag, tag=tag, align_bytes=64)
             nc.vector.tensor_copy(got[:], table[:].indirect(offsets[:]))
             return got
 
-        def weave_x(g):
+        def weave_x(g, scalar_cuts):
             woven = woven_tile("x_woven%d" % g)
             dst, src = deal_views(woven, x_raw[g])
-            if g == 0:
-                nc.scalar.copy(dst[:, :P // 2], src[:, :P // 2])
-                nc.scalar.copy(dst[:, P // 2:3 * P // 4], src[:, P // 2:3 * P // 4])
-                nc.vector.tensor_copy(dst[:, 3 * P // 4:], src[:, 3 * P // 4:])
-            else:
-                nc.scalar.copy(dst, src)
+            for lo, hi in zip(scalar_cuts, scalar_cuts[1:]):
+                nc.scalar.copy(dst[:, lo:hi], src[:, lo:hi])
+            if scalar_cuts[-1] < P:
+                nc.vector.tensor_copy(dst[:, scalar_cuts[-1]:], src[:, scalar_cuts[-1]:])
             return woven
 
         def gradient(g, x_codes, x_scales):
             g_planes = keep.tile([P, PACK, N], BF16, name="g_planes%d" % g, align_bytes=64)
-            hinge = []
-
-            def margin(t):
+            hinges = []
+            for t in range(PACK):
                 scores = psum.tile([P, N], F32, name="bank_a%d" % t, tag="bank_a%d" % t)
-                nc.tensor.matmul_mx(out=scores[:], lhsT=x_codes[:, feats(t)].bitcast(E4M3), lhsT_scale=x_scales[:, feats(t)],
+                nc.tensor.matmul_mx(out=scores[:], lhsT=x_codes[:, block(t)].bitcast(E4M3), lhsT_scale=x_scales[:, block(t)],
                                     rhs=w_codes[:].bitcast(E4M3), rhs_scale=w_scales[:], start=True, stop=True)
-                ya = ring.tile([P, N], F32, name="ya")
-                nc.vector.tensor_tensor(ya[:], scores[:], y_raw[g][:, t, :], ALU.mult)
-                h = ring.tile([P, N], F32, name="h")
-                nc.scalar.activation(h[:], ya[:], ACT.Relu, bias=one[:], scale=-1.0)
-                hinge.append(h)
-
-            def weigh(t):
-                nc.vector.scalar_tensor_tensor(g_planes[:, t, :], hinge[t][:], neg_wt[:, g, t:t + 1], y_raw[g][:, t, :],
+                margin = ring.tile([P, N], F32, name="margin")
+                nc.vector.tensor_tensor(margin[:], scores[:], y_raw[g][:, t, :], ALU.mult)
+                hinge = ring.tile([P, N], F32, name="hinge")
+                nc.scalar.activation(hinge[:], margin[:], ACT.Relu, bias=one[:], scale=-1.0)
+                hinges.append(hinge)
+            signed = ring.tile([P, N], F32, name="signed", bufs=PASSES)
+            nc.gpsimd.tensor_scalar(signed[:], y_raw[g][:, 0, :], neg_wt[:, g, 0:1], 0.0, ALU.mult, ALU.add)
+            nc.gpsimd.tensor_tensor(g_planes[:, 0, :], hinges[0][:], signed[:], ALU.mult)
+            for t in range(1, PACK):
+                nc.vector.scalar_tensor_tensor(g_planes[:, t, :], hinges[t][:], neg_wt[:, g, t:t + 1], y_raw[g][:, t, :],
                                                ALU.mult, ALU.mult)
-
-            for t in range(PACK):
-                margin(t)
-            for t in range(PACK):
-                weigh(t)
             return g_planes
 
-        def weave_plain(tag, planes):
+        def weave_on_scalar(tag, planes):
             woven = woven_tile(tag)
             nc.scalar.copy(*weave_views(woven, planes))
             return woven
@@ -184,50 +184,49 @@ def tile_attend_gsqh_adam_kernel(tc, xT, wT, y, wt, xm, mT, vT, offs, out_0, out
 
         def dw_pass(g, xm_q, g_q):
             for j in range(D_TILES):
-                nc.tensor.matmul_mx(out=dw[j][:], lhsT=xm_q[0][:, feats(j)].bitcast(E4M3), lhsT_scale=xm_q[1][:, feats(j)],
+                nc.tensor.matmul_mx(out=dw[j][:], lhsT=xm_q[0][:, block(j)].bitcast(E4M3), lhsT_scale=xm_q[1][:, block(j)],
                                     rhs=g_q[0][:].bitcast(E5M2), rhs_scale=g_q[1][:], start=(g == 0), stop=(g == PASSES - 1))
 
-        x_woven0 = weave_x(0)
+        x_woven0 = weave_x(0, scalar_cuts=(0, P // 2, 3 * P // 4))
         w_codes, w_scales = quantize("w", w_woven, E4M3)
         x_q0 = quantize("x0", x_woven0, E4M3, cuts=(0, P, 2 * P, K_PASS))
         nc.scalar.activation(neg_wt[:], wt_sb[:], ACT.Copy, scale=-1.0)
         g_planes0 = gradient(0, *x_q0)
-        x_q1 = quantize("x1", weave_x(1), E4M3)
+        x_q1 = quantize("x1", weave_x(1, scalar_cuts=(0, P)), E4M3)
         g_planes1 = gradient(1, *x_q1)
-        g_q0 = quantize("g0", weave_plain("g_woven0", g_planes0), E5M2)
-        xm_q0 = quantize("xm0", weave_plain("xm_woven0", xm_raw[0]), E4M3)
-        dw_pass(0, xm_q0, g_q0)
-        g_q1 = quantize("g1", weave_plain("g_woven1", g_planes1), E5M2)
-        xm_q1 = quantize("xm1", weave_plain("xm_woven1", xm_raw[1]), E4M3)
-        dw_pass(1, xm_q1, g_q1)
+        for g, g_planes in enumerate((g_planes0, g_planes1)):
+            g_q = quantize("g%d" % g, weave_on_scalar("g_woven%d" % g, g_planes), E5M2)
+            xm_q = quantize("xm%d" % g, weave_on_scalar("xm_woven%d" % g, xm_raw[g]), E4M3)
+            dw_pass(g, xm_q, g_q)
+
         v_got = [gather(v_tab[j], tag) for j, tag in enumerate(("v_got0", "x_woven1", "v_got2", "v_got3"))]
         m_got = [gather(m_tab[j], tag) for j, tag in enumerate(("m_got0", "m_got1", "g_woven1", "xm_woven1"))]
 
-        dw_sq = wide_tile("wide_x0")
-        dw_sb = wide_tile("wide_x1")
-        nm_t = wide_tile("wide_y0")
-        nm = wide_tile("wide_xm0")
-        root_t = wide_tile("wide_y1")
-        rate = wide_tile("wide_xm1")
+        dw_sq = quad_tile("x_raw0")
+        dw_sb = quad_tile("x_raw1")
+        nm_t = quad_tile("y_raw0")
+        nm = quad_tile("xm_raw0")
+        denom_t = quad_tile("y_raw1")
+        rate = quad_tile("xm_raw1")
 
         def turned_sum(j, first, second):
-            bank = psum.tile([P, PACK, P], F32, name="bank_a%d" % j, tag="bank_a%d" % j)
+            bank = psum.tile([P, N // P, P], F32, name="bank_a%d" % j, tag="bank_a%d" % j)
             for b in range(N // P):
-                nc.tensor.matmul(bank[:, b, :], first[:, feats(b)], ident[:], start=True, stop=False, is_transpose=True)
-                nc.tensor.matmul(bank[:, b, :], second[:, feats(b)], ident[:], start=False, stop=True, is_transpose=True)
+                nc.tensor.matmul(bank[:, b, :], first[:, block(b)], ident[:], start=True, stop=False, is_transpose=True)
+                nc.tensor.matmul(bank[:, b, :], second[:, block(b)], ident[:], start=False, stop=True, is_transpose=True)
             return bank[:].rearrange("p b d -> p (b d)")
 
         def turn_back(j, turned):
             bank = psum.tile([P, N], F32, name="bank_d%d" % j, tag="bank_d%d" % j)
             for b in range(N // P):
-                nc.tensor.transpose(bank[:, feats(b)], turned[:, j, feats(b)], ident[:])
+                nc.tensor.transpose(bank[:, block(b)], turned[:, j, block(b)], ident[:])
             return bank[:]
 
         for j in range(D_TILES):
             nc.scalar.activation(v_decayed[:, j, :], v_got[j][:], ACT.Copy, scale=RHO)
             nc.scalar.activation(dw_sq[:, j, :], dw[j][:], ACT.Square, scale=math.sqrt(1.0 - RHO))
             nc.vector.tensor_tensor(v_win[j][:].indirect(offsets[:]), v_decayed[:, j, :], dw_sq[:, j, :], ALU.add)
-            nc.sync.dma_start(out_2[feats(j), :], v_win[j][:])
+            nc.sync.dma_start(out_2[block(j), :], v_win[j][:])
         for j in range(D_TILES):
             nc.scalar.copy(dw_sb[:, j, :], dw[j][:])
         for j in range(D_TILES):
@@ -235,12 +234,12 @@ def tile_attend_gsqh_adam_kernel(tc, xT, wT, y, wt, xm, mT, vT, offs, out_0, out
         for j in range(D_TILES):
             nc.scalar.copy(nm[:, j, :], turn_back(j, nm_t))
             nc.vector.tensor_copy(m_win[j][:].indirect(offsets[:]), nm[:, j, :])
-            nc.sync.dma_start(out_1[feats(j), :], m_win[j][:])
+            nc.sync.dma_start(out_1[block(j), :], m_win[j][:])
         for j in range(D_TILES):
-            nc.scalar.activation(root_t[:, j, :], turned_sum(j, v_decayed[:, j, :], dw_sq[:, j, :]), ACT.Sqrt)
-        nc.scalar.activation(root_t[:], root_t[:], ACT.Square, bias=eps[:])
-        nc.scalar.activation(root_t[:], root_t[:], ACT.Abs_reciprocal_sqrt)
+            nc.scalar.activation(denom_t[:, j, :], turned_sum(j, v_decayed[:, j, :], dw_sq[:, j, :]), ACT.Sqrt)
+        nc.scalar.activation(denom_t[:], denom_t[:], ACT.Square, bias=eps[:])
+        nc.scalar.activation(denom_t[:], denom_t[:], ACT.Abs_reciprocal_sqrt)
         for j in range(D_TILES):
-            nc.scalar.activation(rate[:, j, :], turn_back(j, root_t), ACT.Copy, scale=-LR)
+            nc.scalar.activation(rate[:, j, :], turn_back(j, denom_t), ACT.Copy, scale=-LR)
             nc.vector.tensor_tensor(step_win[j][:].indirect(offsets[:]), nm[:, j, :], rate[:, j, :], ALU.mult)
-            nc.sync.dma_start(out_0[feats(j), :], step_win[j][:])
+            nc.sync.dma_start(out_0[block(j), :], step_win[j][:])

@@ -81,17 +81,15 @@ def tile_attend_gsqh_adam_kernel(tc, xT, wT, y, wt, xm, mT, vT, offs, out_0, out
         step_win = [table_tile("step_win%d" % j) for j in range(D_TILES)]
         wt_sb = keep.tile([P, PASSES, PACK], F32, name="wt_sb")
 
-        def load_x(g, parts):
+        def load_x(g, half):
             src = xT[0, :, pass_rows(g)].rearrange("(p j) r -> p j r", j=PACK)
-            width = K_PASS // parts
-            for part in range(parts):
-                cols = slice(part * width, (part + 1) * width)
-                nc.sync.dma_start(x_raw[g][:, :, cols], src[:, :, cols])
+            cols = slice(half * K_PASS // 2, (half + 1) * K_PASS // 2)
+            nc.sync.dma_start(x_raw[g][:, :, cols], src[:, :, cols])
 
-        def load_y(g):
+        def load_y(g, half):
             src = y[0, pass_rows(g), :].rearrange("(p t) n -> p t n", t=PACK)
-            for t in range(0, PACK, 2):
-                nc.sync.dma_start(y_raw[g][:, t:t + 2, :], src[:, t:t + 2, :])
+            planes = slice(half * PACK // 2, (half + 1) * PACK // 2)
+            nc.sync.dma_start(y_raw[g][:, planes, :], src[:, planes, :])
 
         def load_xm(g):
             nc.sync.dma_start(xm_raw[g][:], xm[0, pass_rows(g), :].rearrange("(p t) d -> p t d", t=PACK))
@@ -101,12 +99,16 @@ def tile_attend_gsqh_adam_kernel(tc, xT, wT, y, wt, xm, mT, vT, offs, out_0, out
 
         for t in range(PACK):
             nc.sync.dma_start(w_tab[t][:], w_planes[t])
-        load_x(0, parts=2)
+        load_x(0, 0)
+        load_x(0, 1)
         nc.sync.dma_start(wt_sb[:], wt[0].rearrange("(g p t) o -> p g (t o)", p=P, t=PACK))
-        load_y(0)
-        load_x(1, parts=1)
+        load_x(1, 0)
+        load_y(0, 0)
+        load_y(0, 1)
+        load_x(1, 1)
         load_table(v_tab[0], vT, 0)
-        load_y(1)
+        load_y(1, 0)
+        load_y(1, 1)
         load_table(v_tab[1], vT, 1)
         load_xm(0)
         load_xm(1)
@@ -167,10 +169,7 @@ def tile_attend_gsqh_adam_kernel(tc, xT, wT, y, wt, xm, mT, vT, offs, out_0, out
                 hinge = ring.tile([P, N], F32, name="hinge")
                 nc.scalar.activation(hinge[:], margin[:], ACT.Relu, bias=one[:], scale=-1.0)
                 hinges.append(hinge)
-            signed = ring.tile([P, N], F32, name="signed", bufs=PASSES)
-            nc.gpsimd.tensor_scalar(signed[:], y_raw[g][:, 0, :], neg_wt[:, g, 0:1], 0.0, ALU.mult, ALU.add)
-            nc.gpsimd.tensor_tensor(g_planes[:, 0, :], hinges[0][:], signed[:], ALU.mult)
-            for t in range(1, PACK):
+            for t in range(PACK):
                 nc.vector.scalar_tensor_tensor(g_planes[:, t, :], hinges[t][:], neg_wt[:, g, t:t + 1], y_raw[g][:, t, :],
                                                ALU.mult, ALU.mult)
             return g_planes
@@ -192,14 +191,14 @@ def tile_attend_gsqh_adam_kernel(tc, xT, wT, y, wt, xm, mT, vT, offs, out_0, out
         x_q0 = quantize("x0", x_woven0, E4M3, cuts=(0, P, 2 * P, K_PASS))
         nc.scalar.activation(neg_wt[:], wt_sb[:], ACT.Copy, scale=-1.0)
         g_planes0 = gradient(0, *x_q0)
-        x_q1 = quantize("x1", weave_x(1, scalar_cuts=(0, P)), E4M3)
+        x_q1 = quantize("x1", weave_x(1, scalar_cuts=(0, P // 2, P)), E4M3)
         g_planes1 = gradient(1, *x_q1)
         for g, g_planes in enumerate((g_planes0, g_planes1)):
             g_q = quantize("g%d" % g, weave_on_scalar("g_woven%d" % g, g_planes), E5M2)
             xm_q = quantize("xm%d" % g, weave_on_scalar("xm_woven%d" % g, xm_raw[g]), E4M3)
             dw_pass(g, xm_q, g_q)
 
-        v_got = [gather(v_tab[j], tag) for j, tag in enumerate(("v_got0", "x_woven1", "v_got2", "v_got3"))]
+        v_got = [gather(v_tab[j], tag) for j, tag in enumerate(("x_woven1", "v_got1", "v_got2", "v_got3"))]
         m_got = [gather(m_tab[j], tag) for j, tag in enumerate(("m_got0", "m_got1", "g_woven1", "xm_woven1"))]
 
         dw_sq = quad_tile("x_raw0")

@@ -33,7 +33,6 @@ def tile_attend_gsqh_adam_kernel(tc, xT, wT, y, wt, xm, mT, vT, offs, out_0, out
     nc = tc.nc
     with ExitStack() as ctx:
         keep = ctx.enter_context(tc.tile_pool(name="keep", bufs=1))
-        ring = ctx.enter_context(tc.tile_pool(name="ring", bufs=PACK))
         psum = ctx.enter_context(tc.psum_pool(name="psum", bufs=1))
 
         def table_tile(tag):
@@ -53,8 +52,8 @@ def tile_attend_gsqh_adam_kernel(tc, xT, wT, y, wt, xm, mT, vT, offs, out_0, out
             return (woven[:].rearrange("p (t s j) -> p s j t", t=PACK, j=PACK),
                     planes[:].rearrange("p j (s t) -> p s j t", t=PACK))
 
-        def quantize(tag, woven, fmt, cuts=(0, K_PASS)):
-            codes = keep.tile([P, K_PASS], U32, name=tag + "_codes", align_bytes=64)
+        def quantize(tag, woven, fmt, cuts=(0, K_PASS), place=None):
+            codes = keep.tile([P, K_PASS], U32, name=tag + "_codes", tag=place or tag + "_codes", align_bytes=64)
             scales = keep.tile([P, K_PASS], U8, name=tag + "_scales", align_bytes=64)
             for lo, hi in zip(cuts, cuts[1:]):
                 nc.vector.quantize_mx(out=codes[:, lo:hi].bitcast(fmt), scales=scales[:, lo:hi],
@@ -74,7 +73,8 @@ def tile_attend_gsqh_adam_kernel(tc, xT, wT, y, wt, xm, mT, vT, offs, out_0, out
         w_tab = [table_tile("w_tab%d" % t) for t in range(PACK)]
         x_raw = [quad_tile("x_raw%d" % g) for g in range(PASSES)]
         y_raw = [quad_tile("y_raw%d" % g) for g in range(PASSES)]
-        xm_raw = [quad_tile("xm_raw%d" % g) for g in range(PASSES)]
+        xm_raw = [[keep.tile([P, PACK, D // 2], F32, name="xm_raw%d_%d" % (g, h), align_bytes=64) for h in range(2)]
+                  for g in range(PASSES)]
         m_tab = [table_tile("m_tab%d" % j) for j in range(D_TILES)]
         v_tab = [table_tile("v_tab%d" % j) for j in range(D_TILES)]
         m_win = [table_tile("m_win%d" % j) for j in range(D_TILES)]
@@ -91,8 +91,9 @@ def tile_attend_gsqh_adam_kernel(tc, xT, wT, y, wt, xm, mT, vT, offs, out_0, out
             planes = slice(half * PACK // 2, (half + 1) * PACK // 2)
             nc.sync.dma_start(y_raw[g][:, planes, :], src[:, planes, :])
 
-        def load_xm(g):
-            nc.sync.dma_start(xm_raw[g][:], xm[0, pass_rows(g), :].rearrange("(p t) d -> p t d", t=PACK))
+        def load_xm(g, h):
+            src = xm[0, pass_rows(g), :].rearrange("(p t) d -> p t d", t=PACK)
+            nc.sync.dma_start(xm_raw[g][h][:], src[:, :, h * D // 2:(h + 1) * D // 2])
 
         def load_table(tile, table, j):
             nc.sync.dma_start(tile[:], table[block(j), :])
@@ -103,17 +104,17 @@ def tile_attend_gsqh_adam_kernel(tc, xT, wT, y, wt, xm, mT, vT, offs, out_0, out
         load_x(0, 1)
         nc.sync.dma_start(wt_sb[:], wt[0].rearrange("(g p t) o -> p g (t o)", p=P, t=PACK))
         load_x(1, 0)
+        load_x(1, 1)
         load_y(0, 0)
         load_y(0, 1)
-        load_x(1, 1)
-        load_table(v_tab[0], vT, 0)
         load_y(1, 0)
         load_y(1, 1)
+        load_table(v_tab[0], vT, 0)
         load_table(v_tab[1], vT, 1)
-        load_xm(0)
-        load_xm(1)
-        for j in range(2, D_TILES):
-            load_table(v_tab[j], vT, j)
+        load_table(v_tab[2], vT, 2)
+        load_xm(0, 0)
+        load_table(v_tab[3], vT, 3)
+        load_xm(1, 0)
 
         one = keep.tile([P, 1], F32, name="one")
         nc.vector.memset(one[:], 1.0)
@@ -136,15 +137,22 @@ def tile_attend_gsqh_adam_kernel(tc, xT, wT, y, wt, xm, mT, vT, offs, out_0, out
         v_win = [table_tile("w_tab%d" % j) for j in range(D_TILES)]
         for j in range(D_TILES):
             load_table(m_tab[j], mT, j)
-        for j in range(D_TILES):
-            load_table(v_win[j], vT, j)
-        for j in range(D_TILES):
-            load_table(m_win[j], mT, j)
+        load_table(v_win[0], vT, 0)
+        load_xm(0, 1)
+        load_xm(1, 1)
+        load_table(v_win[1], vT, 1)
+        load_table(m_win[0], mT, 0)
+        load_table(m_win[1], mT, 1)
+        load_table(v_win[2], vT, 2)
+        load_table(v_win[3], vT, 3)
+        load_table(m_win[2], mT, 2)
+        load_table(m_win[3], mT, 3)
 
-        v_decayed = quad_tile("v_decayed")
+        def row_tile(tag):
+            return keep.tile([P, N], F32, name=tag, tag=tag, align_bytes=64)
 
         def gather(table, tag):
-            got = keep.tile([P, N], F32, name=tag, tag=tag, align_bytes=64)
+            got = row_tile(tag)
             nc.vector.tensor_copy(got[:], table[:].indirect(offsets[:]))
             return got
 
@@ -158,55 +166,70 @@ def tile_attend_gsqh_adam_kernel(tc, xT, wT, y, wt, xm, mT, vT, offs, out_0, out
             return woven
 
         def gradient(g, x_codes, x_scales):
-            g_planes = keep.tile([P, PACK, N], BF16, name="g_planes%d" % g, align_bytes=64)
-            hinges = []
+            hinge = quad_tile(("hinge0", "w_got")[g])
+            weight = quad_tile("weight%d" % g)
+            if g == 1:
+                for t in range(PACK):
+                    nc.scalar.activation(weight[:, t, :], y_raw[g][:, t, :], ACT.Copy, scale=neg_wt[:, g, t:t + 1])
             for t in range(PACK):
-                scores = psum.tile([P, N], F32, name="bank_a%d" % t, tag="bank_a%d" % t)
+                bank = "bank_%s%d" % ("ad"[g], t)
+                scores = psum.tile([P, N], F32, name=bank, tag=bank)
                 nc.tensor.matmul_mx(out=scores[:], lhsT=x_codes[:, block(t)].bitcast(E4M3), lhsT_scale=x_scales[:, block(t)],
                                     rhs=w_codes[:].bitcast(E4M3), rhs_scale=w_scales[:], start=True, stop=True)
-                margin = ring.tile([P, N], F32, name="margin")
-                nc.vector.tensor_tensor(margin[:], scores[:], y_raw[g][:, t, :], ALU.mult)
-                hinge = ring.tile([P, N], F32, name="hinge")
-                nc.scalar.activation(hinge[:], margin[:], ACT.Relu, bias=one[:], scale=-1.0)
-                hinges.append(hinge)
-            for t in range(PACK):
-                nc.vector.scalar_tensor_tensor(g_planes[:, t, :], hinges[t][:], neg_wt[:, g, t:t + 1], y_raw[g][:, t, :],
-                                               ALU.mult, ALU.mult)
-            return g_planes
-
-        def weave_on_scalar(tag, planes):
-            woven = woven_tile(tag)
-            nc.scalar.copy(*weave_views(woven, planes))
+                nc.vector.tensor_tensor(hinge[:, t, :], scores[:], y_raw[g][:, t, :], ALU.mult)
+                nc.scalar.activation(hinge[:, t, :], hinge[:, t, :], ACT.Relu, bias=one[:], scale=-1.0)
+                if g == 0:
+                    nc.gpsimd.tensor_scalar(weight[:, t, :], y_raw[g][:, t, :], neg_wt[:, g, t:t + 1], 0.0, ALU.mult, ALU.add)
+            woven = woven_tile("g_woven%d" % g)
+            dst, hinge_view = weave_views(woven, hinge)
+            weight_view = weave_views(woven, weight)[1]
+            pieces = (8, 5)[g]
+            for q in range(pieces):
+                cols = slice(q * 16, (q + 1) * 16)
+                nc.gpsimd.tensor_tensor(dst[:, cols], hinge_view[:, cols], weight_view[:, cols], ALU.mult)
+            if pieces < 8:
+                cols = slice(pieces * 16, P)
+                nc.vector.tensor_tensor(dst[:, cols], hinge_view[:, cols], weight_view[:, cols], ALU.mult)
             return woven
 
-        dw = [psum.tile([P, N], F32, name="bank_d%d" % j, tag="bank_d%d" % j) for j in range(D_TILES)]
+        def quantize_xm(g, h):
+            tag = "xm_woven%d" % g if h == 0 else "xm_codes%d_0" % g
+            woven = keep.tile([P, PACK * D // 2], BF16, name=tag, tag=tag, align_bytes=64)
+            nc.scalar.copy(*weave_views(woven, xm_raw[g][h]))
+            codes = keep.tile([P, D // 2], U32, name="xm_codes%d_%d" % (g, h), tag="xm_codes%d_%d" % (g, h), align_bytes=64)
+            scales = keep.tile([P, D // 2], U8, name="xm_scales%d_%d" % (g, h), align_bytes=64)
+            nc.vector.quantize_mx(out=codes[:].bitcast(E4M3), scales=scales[:], in_=woven[:])
+            return codes, scales
 
-        def dw_pass(g, xm_q, g_q):
-            for j in range(D_TILES):
-                nc.tensor.matmul_mx(out=dw[j][:], lhsT=xm_q[0][:, block(j)].bitcast(E4M3), lhsT_scale=xm_q[1][:, block(j)],
-                                    rhs=g_q[0][:].bitcast(E5M2), rhs_scale=g_q[1][:], start=(g == 0), stop=(g == PASSES - 1))
+        def dw_half(h, g_q):
+            xm_q = [quantize_xm(g, h) for g in range(PASSES)]
+            for jj in range(2):
+                for g in (0, 1):
+                    nc.tensor.matmul_mx(out=dw[2 * h + jj][:], lhsT=xm_q[g][0][:, block(jj)].bitcast(E4M3),
+                                        lhsT_scale=xm_q[g][1][:, block(jj)],
+                                        rhs=g_q[g][0][:].bitcast(E5M2), rhs_scale=g_q[g][1][:],
+                                        start=(g == 0), stop=(g == 1))
 
         x_woven0 = weave_x(0, scalar_cuts=(0, P // 2, 3 * P // 4))
         w_codes, w_scales = quantize("w", w_woven, E4M3)
         x_q0 = quantize("x0", x_woven0, E4M3, cuts=(0, P, 2 * P, K_PASS))
         nc.scalar.activation(neg_wt[:], wt_sb[:], ACT.Copy, scale=-1.0)
-        g_planes0 = gradient(0, *x_q0)
         x_q1 = quantize("x1", weave_x(1, scalar_cuts=(0, P // 2, P)), E4M3)
-        g_planes1 = gradient(1, *x_q1)
-        for g, g_planes in enumerate((g_planes0, g_planes1)):
-            g_q = quantize("g%d" % g, weave_on_scalar("g_woven%d" % g, g_planes), E5M2)
-            xm_q = quantize("xm%d" % g, weave_on_scalar("xm_woven%d" % g, xm_raw[g]), E4M3)
-            dw_pass(g, xm_q, g_q)
+        g_woven0 = gradient(0, *x_q0)
+        g_woven1 = gradient(1, *x_q1)
+        v_got = [gather(v_tab[j], "v_got%d" % j) for j in range(D_TILES)]
+        m_got = [gather(m_tab[j], "m_got%d" % j) for j in range(D_TILES)]
+        g_q = [quantize("g0", g_woven0, E5M2, place="v_tab3"), quantize("g1", g_woven1, E5M2, place="m_tab1")]
 
-        v_got = [gather(v_tab[j], tag) for j, tag in enumerate(("x_woven1", "v_got1", "v_got2", "v_got3"))]
-        m_got = [gather(m_tab[j], tag) for j, tag in enumerate(("m_got0", "m_got1", "g_woven1", "xm_woven1"))]
+        dw = [psum.tile([P, N], F32, name="bank_d%d" % j, tag="bank_d%d" % j) for j in range(D_TILES)]
 
-        dw_sq = quad_tile("x_raw0")
+        v_decayed = [row_tile("v_decayed%d" % j) for j in range(D_TILES)]
+        dw_sq = [row_tile("dw_sq%d" % j) for j in range(D_TILES)]
         dw_sb = quad_tile("x_raw1")
         nm_t = quad_tile("y_raw0")
-        nm = quad_tile("xm_raw0")
+        nm = quad_tile("weight0")
         denom_t = quad_tile("y_raw1")
-        rate = quad_tile("xm_raw1")
+        rate = quad_tile("weight1")
 
         def turned_sum(j, first, second):
             bank = psum.tile([P, N // P, P], F32, name="bank_a%d" % j, tag="bank_a%d" % j)
@@ -221,21 +244,21 @@ def tile_attend_gsqh_adam_kernel(tc, xT, wT, y, wt, xm, mT, vT, offs, out_0, out
                 nc.tensor.transpose(bank[:, block(b)], turned[:, j, block(b)], ident[:])
             return bank[:]
 
+        for h in range(2):
+            dw_half(h, g_q)
+            for j in (2 * h, 2 * h + 1):
+                nc.scalar.activation(v_decayed[j][:], v_got[j][:], ACT.Copy, scale=RHO)
+                nc.scalar.activation(dw_sq[j][:], dw[j][:], ACT.Square, scale=math.sqrt(1.0 - RHO))
+                nc.vector.tensor_tensor(v_win[j][:].indirect(offsets[:]), v_decayed[j][:], dw_sq[j][:], ALU.add)
+                nc.sync.dma_start(out_2[block(j), :], v_win[j][:])
+            for j in (2 * h, 2 * h + 1):
+                nc.scalar.copy(dw_sb[:, j, :], dw[j][:])
+                nc.scalar.activation(nm_t[:, j, :], turned_sum(j, m_got[j], dw_sb[:, j, :]), ACT.Copy, scale=BETA)
+                nc.scalar.copy(nm[:, j, :], turn_back(j, nm_t))
+                nc.vector.tensor_copy(m_win[j][:].indirect(offsets[:]), nm[:, j, :])
+                nc.sync.dma_start(out_1[block(j), :], m_win[j][:])
         for j in range(D_TILES):
-            nc.scalar.activation(v_decayed[:, j, :], v_got[j][:], ACT.Copy, scale=RHO)
-            nc.scalar.activation(dw_sq[:, j, :], dw[j][:], ACT.Square, scale=math.sqrt(1.0 - RHO))
-            nc.vector.tensor_tensor(v_win[j][:].indirect(offsets[:]), v_decayed[:, j, :], dw_sq[:, j, :], ALU.add)
-            nc.sync.dma_start(out_2[block(j), :], v_win[j][:])
-        for j in range(D_TILES):
-            nc.scalar.copy(dw_sb[:, j, :], dw[j][:])
-        for j in range(D_TILES):
-            nc.scalar.activation(nm_t[:, j, :], turned_sum(j, m_got[j], dw_sb[:, j, :]), ACT.Copy, scale=BETA)
-        for j in range(D_TILES):
-            nc.scalar.copy(nm[:, j, :], turn_back(j, nm_t))
-            nc.vector.tensor_copy(m_win[j][:].indirect(offsets[:]), nm[:, j, :])
-            nc.sync.dma_start(out_1[block(j), :], m_win[j][:])
-        for j in range(D_TILES):
-            nc.scalar.activation(denom_t[:, j, :], turned_sum(j, v_decayed[:, j, :], dw_sq[:, j, :]), ACT.Sqrt)
+            nc.scalar.activation(denom_t[:, j, :], turned_sum(j, v_decayed[j], dw_sq[j]), ACT.Sqrt)
         nc.scalar.activation(denom_t[:], denom_t[:], ACT.Square, bias=eps[:])
         nc.scalar.activation(denom_t[:], denom_t[:], ACT.Abs_reciprocal_sqrt)
         for j in range(D_TILES):

@@ -104,17 +104,17 @@ def tile_attend_gsqh_adam_kernel(tc, xT, wT, y, wt, xm, mT, vT, offs, out_0, out
         load_x(0, 1)
         nc.sync.dma_start(wt_sb[:], wt[0].rearrange("(g p t) o -> p g (t o)", p=P, t=PACK))
         load_x(1, 0)
-        load_x(1, 1)
         load_y(0, 0)
         load_y(0, 1)
+        load_x(1, 1)
+        load_table(v_tab[0], vT, 0)
         load_y(1, 0)
         load_y(1, 1)
-        load_table(v_tab[0], vT, 0)
         load_table(v_tab[1], vT, 1)
-        load_table(v_tab[2], vT, 2)
         load_xm(0, 0)
-        load_table(v_tab[3], vT, 3)
         load_xm(1, 0)
+        load_table(v_tab[2], vT, 2)
+        load_table(v_tab[3], vT, 3)
 
         one = keep.tile([P, 1], F32, name="one")
         nc.vector.memset(one[:], 1.0)
@@ -167,10 +167,7 @@ def tile_attend_gsqh_adam_kernel(tc, xT, wT, y, wt, xm, mT, vT, offs, out_0, out
 
         def gradient(g, x_codes, x_scales):
             hinge = quad_tile(("hinge0", "w_got")[g])
-            weight = quad_tile("weight%d" % g)
-            if g == 1:
-                for t in range(PACK):
-                    nc.scalar.activation(weight[:, t, :], y_raw[g][:, t, :], ACT.Copy, scale=neg_wt[:, g, t:t + 1])
+            g_planes = keep.tile([P, PACK, N], BF16, name="g_planes%d" % g, align_bytes=64)
             for t in range(PACK):
                 bank = "bank_%s%d" % ("ad"[g], t)
                 scores = psum.tile([P, N], F32, name=bank, tag=bank)
@@ -178,18 +175,11 @@ def tile_attend_gsqh_adam_kernel(tc, xT, wT, y, wt, xm, mT, vT, offs, out_0, out
                                     rhs=w_codes[:].bitcast(E4M3), rhs_scale=w_scales[:], start=True, stop=True)
                 nc.vector.tensor_tensor(hinge[:, t, :], scores[:], y_raw[g][:, t, :], ALU.mult)
                 nc.scalar.activation(hinge[:, t, :], hinge[:, t, :], ACT.Relu, bias=one[:], scale=-1.0)
-                if g == 0:
-                    nc.gpsimd.tensor_scalar(weight[:, t, :], y_raw[g][:, t, :], neg_wt[:, g, t:t + 1], 0.0, ALU.mult, ALU.add)
+            for t in range(PACK):
+                nc.vector.scalar_tensor_tensor(g_planes[:, t, :], hinge[:, t, :], neg_wt[:, g, t:t + 1], y_raw[g][:, t, :],
+                                               ALU.mult, ALU.mult)
             woven = woven_tile("g_woven%d" % g)
-            dst, hinge_view = weave_views(woven, hinge)
-            weight_view = weave_views(woven, weight)[1]
-            pieces = (8, 5)[g]
-            for q in range(pieces):
-                cols = slice(q * 16, (q + 1) * 16)
-                nc.gpsimd.tensor_tensor(dst[:, cols], hinge_view[:, cols], weight_view[:, cols], ALU.mult)
-            if pieces < 8:
-                cols = slice(pieces * 16, P)
-                nc.vector.tensor_tensor(dst[:, cols], hinge_view[:, cols], weight_view[:, cols], ALU.mult)
+            nc.scalar.copy(*weave_views(woven, g_planes))
             return woven
 
         def quantize_xm(g, h):
@@ -214,12 +204,12 @@ def tile_attend_gsqh_adam_kernel(tc, xT, wT, y, wt, xm, mT, vT, offs, out_0, out
         w_codes, w_scales = quantize("w", w_woven, E4M3)
         x_q0 = quantize("x0", x_woven0, E4M3, cuts=(0, P, 2 * P, K_PASS))
         nc.scalar.activation(neg_wt[:], wt_sb[:], ACT.Copy, scale=-1.0)
-        x_q1 = quantize("x1", weave_x(1, scalar_cuts=(0, P // 2, P)), E4M3)
         g_woven0 = gradient(0, *x_q0)
+        x_q1 = quantize("x1", weave_x(1, scalar_cuts=(0, P // 2, P)), E4M3)
         g_woven1 = gradient(1, *x_q1)
-        v_got = [gather(v_tab[j], "v_got%d" % j) for j in range(D_TILES)]
-        m_got = [gather(m_tab[j], "m_got%d" % j) for j in range(D_TILES)]
-        g_q = [quantize("g0", g_woven0, E5M2, place="v_tab3"), quantize("g1", g_woven1, E5M2, place="m_tab1")]
+        g_q = [quantize("g0", g_woven0, E5M2), quantize("g1", g_woven1, E5M2)]
+        v_got = [gather(v_tab[j], tag) for j, tag in enumerate(("x_woven1", "v_got1", "v_got2", "v_got3"))]
+        m_got = [gather(m_tab[j], tag) for j, tag in enumerate(("m_got0", "g_woven1", "g1_late2", "g1_late3"))]
 
         dw = [psum.tile([P, N], F32, name="bank_d%d" % j, tag="bank_d%d" % j) for j in range(D_TILES)]
 
@@ -227,9 +217,9 @@ def tile_attend_gsqh_adam_kernel(tc, xT, wT, y, wt, xm, mT, vT, offs, out_0, out
         dw_sq = [row_tile("dw_sq%d" % j) for j in range(D_TILES)]
         dw_sb = quad_tile("x_raw1")
         nm_t = quad_tile("y_raw0")
-        nm = quad_tile("weight0")
+        nm = quad_tile("x_raw0")
         denom_t = quad_tile("y_raw1")
-        rate = quad_tile("weight1")
+        rate = quad_tile("hinge0")
 
         def turned_sum(j, first, second):
             bank = psum.tile([P, N // P, P], F32, name="bank_a%d" % j, tag="bank_a%d" % j)

@@ -23,6 +23,7 @@ PACK = 4
 K_PASS = P * PACK
 PASSES = R // K_PASS
 D_TILES = D // P
+GPSIMD_PLANES = 4
 LIST_BAND = 16
 
 assert D == K_PASS and N == K_PASS and PASSES == 2
@@ -73,8 +74,7 @@ def tile_attend_gsqh_adam_kernel(tc, xT, wT, y, wt, xm, mT, vT, offs, out_0, out
         w_tab = [table_tile("w_tab%d" % t) for t in range(PACK)]
         x_raw = [quad_tile("x_raw%d" % g) for g in range(PASSES)]
         y_raw = [quad_tile("y_raw%d" % g) for g in range(PASSES)]
-        xm_raw = [[keep.tile([P, PACK, D // 2], F32, name="xm_raw%d_%d" % (g, h), align_bytes=64) for h in range(2)]
-                  for g in range(PASSES)]
+        xm_raw = [quad_tile("xm_raw%d" % g) for g in range(PASSES)]
         m_tab = [table_tile("m_tab%d" % j) for j in range(D_TILES)]
         v_tab = [table_tile("v_tab%d" % j) for j in range(D_TILES)]
         m_win = [table_tile("m_win%d" % j) for j in range(D_TILES)]
@@ -91,9 +91,8 @@ def tile_attend_gsqh_adam_kernel(tc, xT, wT, y, wt, xm, mT, vT, offs, out_0, out
             planes = slice(half * PACK // 2, (half + 1) * PACK // 2)
             nc.sync.dma_start(y_raw[g][:, planes, :], src[:, planes, :])
 
-        def load_xm(g, h):
-            src = xm[0, pass_rows(g), :].rearrange("(p t) d -> p t d", t=PACK)
-            nc.sync.dma_start(xm_raw[g][h][:], src[:, :, h * D // 2:(h + 1) * D // 2])
+        def load_xm(g):
+            nc.sync.dma_start(xm_raw[g][:], xm[0, pass_rows(g), :].rearrange("(p t) d -> p t d", t=PACK))
 
         def load_table(tile, table, j):
             nc.sync.dma_start(tile[:], table[block(j), :])
@@ -104,17 +103,17 @@ def tile_attend_gsqh_adam_kernel(tc, xT, wT, y, wt, xm, mT, vT, offs, out_0, out
         load_x(0, 1)
         nc.sync.dma_start(wt_sb[:], wt[0].rearrange("(g p t) o -> p g (t o)", p=P, t=PACK))
         load_x(1, 0)
+        load_x(1, 1)
         load_y(0, 0)
         load_y(0, 1)
-        load_x(1, 1)
-        load_table(v_tab[0], vT, 0)
         load_y(1, 0)
         load_y(1, 1)
+        load_table(v_tab[0], vT, 0)
         load_table(v_tab[1], vT, 1)
-        load_xm(0, 0)
-        load_xm(1, 0)
+        load_xm(0)
         load_table(v_tab[2], vT, 2)
         load_table(v_tab[3], vT, 3)
+        load_xm(1)
 
         one = keep.tile([P, 1], F32, name="one")
         nc.vector.memset(one[:], 1.0)
@@ -137,16 +136,10 @@ def tile_attend_gsqh_adam_kernel(tc, xT, wT, y, wt, xm, mT, vT, offs, out_0, out
         v_win = [table_tile("w_tab%d" % j) for j in range(D_TILES)]
         for j in range(D_TILES):
             load_table(m_tab[j], mT, j)
-        load_table(v_win[0], vT, 0)
-        load_xm(0, 1)
-        load_xm(1, 1)
-        load_table(v_win[1], vT, 1)
-        load_table(m_win[0], mT, 0)
-        load_table(m_win[1], mT, 1)
-        load_table(v_win[2], vT, 2)
-        load_table(v_win[3], vT, 3)
-        load_table(m_win[2], mT, 2)
-        load_table(m_win[3], mT, 3)
+        for j in range(D_TILES):
+            load_table(v_win[j], vT, j)
+        for j in range(D_TILES):
+            load_table(m_win[j], mT, j)
 
         def row_tile(tag):
             return keep.tile([P, N], F32, name=tag, tag=tag, align_bytes=64)
@@ -167,51 +160,60 @@ def tile_attend_gsqh_adam_kernel(tc, xT, wT, y, wt, xm, mT, vT, offs, out_0, out
 
         def gradient(g, x_codes, x_scales):
             hinge = quad_tile(("hinge0", "w_got")[g])
-            g_planes = keep.tile([P, PACK, N], BF16, name="g_planes%d" % g, align_bytes=64)
+            g_planes = keep.tile([P, PACK, N], BF16, name="g_planes%d" % g, tag=("g_planes0", "v_tab1")[g], align_bytes=64)
+            on_gpsimd = GPSIMD_PLANES if g == 0 else 0
+            weight = keep.tile([P, GPSIMD_PLANES, N], F32, name="weight", align_bytes=64) if on_gpsimd else None
             for t in range(PACK):
+                if t < on_gpsimd:
+                    nc.scalar.activation(weight[:, t, :], y_raw[g][:, t, :], ACT.Copy, scale=neg_wt[:, g, t:t + 1])
                 bank = "bank_%s%d" % ("ad"[g], t)
                 scores = psum.tile([P, N], F32, name=bank, tag=bank)
                 nc.tensor.matmul_mx(out=scores[:], lhsT=x_codes[:, block(t)].bitcast(E4M3), lhsT_scale=x_scales[:, block(t)],
                                     rhs=w_codes[:].bitcast(E4M3), rhs_scale=w_scales[:], start=True, stop=True)
                 nc.vector.tensor_tensor(hinge[:, t, :], scores[:], y_raw[g][:, t, :], ALU.mult)
                 nc.scalar.activation(hinge[:, t, :], hinge[:, t, :], ACT.Relu, bias=one[:], scale=-1.0)
-            for t in range(PACK):
+            return hinge, weight, g_planes, on_gpsimd
+
+        def weigh(g, hinge, weight, g_planes, on_gpsimd):
+            for t in range(on_gpsimd):
+                nc.gpsimd.tensor_tensor(g_planes[:, t, :], hinge[:, t, :], weight[:, t, :], ALU.mult)
+            for t in range(on_gpsimd, PACK):
                 nc.vector.scalar_tensor_tensor(g_planes[:, t, :], hinge[:, t, :], neg_wt[:, g, t:t + 1], y_raw[g][:, t, :],
                                                ALU.mult, ALU.mult)
             woven = woven_tile("g_woven%d" % g)
             nc.scalar.copy(*weave_views(woven, g_planes))
             return woven
 
-        def quantize_xm(g, h):
-            tag = "xm_woven%d" % g if h == 0 else "xm_codes%d_0" % g
-            woven = keep.tile([P, PACK * D // 2], BF16, name=tag, tag=tag, align_bytes=64)
-            nc.scalar.copy(*weave_views(woven, xm_raw[g][h]))
-            codes = keep.tile([P, D // 2], U32, name="xm_codes%d_%d" % (g, h), tag="xm_codes%d_%d" % (g, h), align_bytes=64)
-            scales = keep.tile([P, D // 2], U8, name="xm_scales%d_%d" % (g, h), align_bytes=64)
-            nc.vector.quantize_mx(out=codes[:].bitcast(E4M3), scales=scales[:], in_=woven[:])
-            return codes, scales
-
-        def dw_half(h, g_q):
-            xm_q = [quantize_xm(g, h) for g in range(PASSES)]
-            for jj in range(2):
-                for g in (0, 1):
-                    nc.tensor.matmul_mx(out=dw[2 * h + jj][:], lhsT=xm_q[g][0][:, block(jj)].bitcast(E4M3),
-                                        lhsT_scale=xm_q[g][1][:, block(jj)],
-                                        rhs=g_q[g][0][:].bitcast(E5M2), rhs_scale=g_q[g][1][:],
-                                        start=(g == 0), stop=(g == 1))
+        def weave_on_scalar(tag, planes):
+            woven = woven_tile(tag)
+            nc.scalar.copy(*weave_views(woven, planes))
+            return woven
 
         x_woven0 = weave_x(0, scalar_cuts=(0, P // 2, 3 * P // 4))
         w_codes, w_scales = quantize("w", w_woven, E4M3)
         x_q0 = quantize("x0", x_woven0, E4M3, cuts=(0, P, 2 * P, K_PASS))
         nc.scalar.activation(neg_wt[:], wt_sb[:], ACT.Copy, scale=-1.0)
-        g_woven0 = gradient(0, *x_q0)
-        x_q1 = quantize("x1", weave_x(1, scalar_cuts=(0, P // 2, P)), E4M3)
-        g_woven1 = gradient(1, *x_q1)
+        x_q1 = quantize("x1", weave_x(1, scalar_cuts=(0, P // 2)), E4M3)
+        hinges = [gradient(0, *x_q0), gradient(1, *x_q1)]
+        v_got = [gather(v_tab[j], "v_got%d" % j) for j in range(2)]
+        g_woven0 = weigh(0, *hinges[0])
+        xm_woven0 = weave_on_scalar("xm_woven0", xm_raw[0])
+        g_woven1 = weigh(1, *hinges[1])
+        xm_woven1 = weave_on_scalar("xm_woven1", xm_raw[1])
         g_q = [quantize("g0", g_woven0, E5M2), quantize("g1", g_woven1, E5M2)]
-        v_got = [gather(v_tab[j], tag) for j, tag in enumerate(("x_woven1", "v_got1", "v_got2", "v_got3"))]
-        m_got = [gather(m_tab[j], tag) for j, tag in enumerate(("m_got0", "g_woven1", "g1_late2", "g1_late3"))]
+        xm_q = [quantize("xm0", xm_woven0, E4M3), quantize("xm1", xm_woven1, E4M3)]
+        v_got.extend([gather(v_tab[j], "v_got%d" % j) for j in range(2, D_TILES)])
+        m_got = [gather(m_tab[j], "m_got%d" % j)[:] for j in range(2)]
+        m_late = keep.tile([P, 2, N], F32, name="m_late", tag="xm_woven1", align_bytes=64)
+        for j in range(2):
+            nc.vector.tensor_copy(m_late[:, j, :], m_tab[2 + j][:].indirect(offsets[:]))
+            m_got.append(m_late[:, j, :])
 
         dw = [psum.tile([P, N], F32, name="bank_d%d" % j, tag="bank_d%d" % j) for j in range(D_TILES)]
+        for g in range(PASSES):
+            for j in range(D_TILES):
+                nc.tensor.matmul_mx(out=dw[j][:], lhsT=xm_q[g][0][:, block(j)].bitcast(E4M3), lhsT_scale=xm_q[g][1][:, block(j)],
+                                    rhs=g_q[g][0][:].bitcast(E5M2), rhs_scale=g_q[g][1][:], start=(g == 0), stop=(g == PASSES - 1))
 
         v_decayed = [row_tile("v_decayed%d" % j) for j in range(D_TILES)]
         dw_sq = [row_tile("dw_sq%d" % j) for j in range(D_TILES)]
@@ -234,19 +236,17 @@ def tile_attend_gsqh_adam_kernel(tc, xT, wT, y, wt, xm, mT, vT, offs, out_0, out
                 nc.tensor.transpose(bank[:, block(b)], turned[:, j, block(b)], ident[:])
             return bank[:]
 
-        for h in range(2):
-            dw_half(h, g_q)
-            for j in (2 * h, 2 * h + 1):
-                nc.scalar.activation(v_decayed[j][:], v_got[j][:], ACT.Copy, scale=RHO)
-                nc.scalar.activation(dw_sq[j][:], dw[j][:], ACT.Square, scale=math.sqrt(1.0 - RHO))
-                nc.vector.tensor_tensor(v_win[j][:].indirect(offsets[:]), v_decayed[j][:], dw_sq[j][:], ALU.add)
-                nc.sync.dma_start(out_2[block(j), :], v_win[j][:])
-            for j in (2 * h, 2 * h + 1):
-                nc.scalar.copy(dw_sb[:, j, :], dw[j][:])
-                nc.scalar.activation(nm_t[:, j, :], turned_sum(j, m_got[j], dw_sb[:, j, :]), ACT.Copy, scale=BETA)
-                nc.scalar.copy(nm[:, j, :], turn_back(j, nm_t))
-                nc.vector.tensor_copy(m_win[j][:].indirect(offsets[:]), nm[:, j, :])
-                nc.sync.dma_start(out_1[block(j), :], m_win[j][:])
+        for j in range(D_TILES):
+            nc.scalar.activation(v_decayed[j][:], v_got[j][:], ACT.Copy, scale=RHO)
+            nc.scalar.activation(dw_sq[j][:], dw[j][:], ACT.Square, scale=math.sqrt(1.0 - RHO))
+            nc.vector.tensor_tensor(v_win[j][:].indirect(offsets[:]), v_decayed[j][:], dw_sq[j][:], ALU.add)
+            nc.sync.dma_start(out_2[block(j), :], v_win[j][:])
+        for j in range(D_TILES):
+            nc.scalar.copy(dw_sb[:, j, :], dw[j][:])
+            nc.scalar.activation(nm_t[:, j, :], turned_sum(j, m_got[j], dw_sb[:, j, :]), ACT.Copy, scale=BETA)
+            nc.scalar.copy(nm[:, j, :], turn_back(j, nm_t))
+            nc.vector.tensor_copy(m_win[j][:].indirect(offsets[:]), nm[:, j, :])
+            nc.sync.dma_start(out_1[block(j), :], m_win[j][:])
         for j in range(D_TILES):
             nc.scalar.activation(denom_t[:, j, :], turned_sum(j, v_decayed[j], dw_sq[j]), ACT.Sqrt)
         nc.scalar.activation(denom_t[:], denom_t[:], ACT.Square, bias=eps[:])

@@ -74,7 +74,9 @@ def tile_attend_gsqh_adam_kernel(tc, xT, wT, y, wt, xm, mT, vT, offs, out_0, out
         w_tab = [table_tile("w_tab%d" % t) for t in range(PACK)]
         x_raw = [quad_tile("x_raw%d" % g) for g in range(PASSES)]
         y_raw = [quad_tile("y_raw%d" % g) for g in range(PASSES)]
-        xm_raw = [quad_tile("xm_raw%d" % g) for g in range(PASSES)]
+        xm_parts = [keep.tile([P, PACK, D // 2], F32, name="xm_part%d" % h, tag="xm_part%d" % h, align_bytes=64)
+                    for h in range(2)]
+        xm_raw1 = quad_tile("xm_raw1")
         m_tab = [table_tile("m_tab%d" % j) for j in range(D_TILES)]
         v_tab = [table_tile("v_tab%d" % j) for j in range(D_TILES)]
         m_win = [table_tile("m_win%d" % j) for j in range(D_TILES)]
@@ -91,8 +93,9 @@ def tile_attend_gsqh_adam_kernel(tc, xT, wT, y, wt, xm, mT, vT, offs, out_0, out
             planes = slice(half * PACK // 2, (half + 1) * PACK // 2)
             nc.sync.dma_start(y_raw[g][:, planes, :], src[:, planes, :])
 
-        def load_xm(g):
-            nc.sync.dma_start(xm_raw[g][:], xm[0, pass_rows(g), :].rearrange("(p t) d -> p t d", t=PACK))
+        def load_xm(tile, g, lo, hi):
+            src = xm[0, pass_rows(g), :].rearrange("(p t) d -> p t d", t=PACK)
+            nc.sync.dma_start(tile[:], src[:, :, lo:hi])
 
         def load_table(tile, table, j):
             nc.sync.dma_start(tile[:], table[block(j), :])
@@ -110,10 +113,11 @@ def tile_attend_gsqh_adam_kernel(tc, xT, wT, y, wt, xm, mT, vT, offs, out_0, out
         load_y(1, 1)
         load_table(v_tab[0], vT, 0)
         load_table(v_tab[1], vT, 1)
-        load_xm(0)
+        load_xm(xm_parts[0], 0, 0, D // 2)
+        load_xm(xm_parts[1], 0, D // 2, D)
         load_table(v_tab[2], vT, 2)
         load_table(v_tab[3], vT, 3)
-        load_xm(1)
+        load_xm(xm_raw1, 1, 0, D)
 
         one = keep.tile([P, 1], F32, name="one")
         nc.vector.memset(one[:], 1.0)
@@ -165,7 +169,10 @@ def tile_attend_gsqh_adam_kernel(tc, xT, wT, y, wt, xm, mT, vT, offs, out_0, out
             weight = keep.tile([P, GPSIMD_PLANES, N], F32, name="weight", align_bytes=64) if on_gpsimd else None
             for t in range(PACK):
                 if t < on_gpsimd:
-                    nc.scalar.activation(weight[:, t, :], y_raw[g][:, t, :], ACT.Copy, scale=neg_wt[:, g, t:t + 1])
+                    if t < PACK // 2:
+                        nc.scalar.activation(weight[:, t, :], y_raw[g][:, t, :], ACT.Copy, scale=neg_wt[:, g, t:t + 1])
+                    else:
+                        nc.gpsimd.tensor_scalar(weight[:, t, :], y_raw[g][:, t, :], neg_wt[:, g, t:t + 1], 0.0, ALU.mult, ALU.add)
                 bank = "bank_%s%d" % ("ad"[g], t)
                 scores = psum.tile([P, N], F32, name=bank, tag=bank)
                 nc.tensor.matmul_mx(out=scores[:], lhsT=x_codes[:, block(t)].bitcast(E4M3), lhsT_scale=x_scales[:, block(t)],
@@ -180,13 +187,8 @@ def tile_attend_gsqh_adam_kernel(tc, xT, wT, y, wt, xm, mT, vT, offs, out_0, out
             for t in range(on_gpsimd, PACK):
                 nc.vector.scalar_tensor_tensor(g_planes[:, t, :], hinge[:, t, :], neg_wt[:, g, t:t + 1], y_raw[g][:, t, :],
                                                ALU.mult, ALU.mult)
-            woven = woven_tile("g_woven%d" % g)
+            woven = woven_tile(("xm_part0", "g_woven1")[g])
             nc.scalar.copy(*weave_views(woven, g_planes))
-            return woven
-
-        def weave_on_scalar(tag, planes):
-            woven = woven_tile(tag)
-            nc.scalar.copy(*weave_views(woven, planes))
             return woven
 
         x_woven0 = weave_x(0, scalar_cuts=(0, P // 2, 3 * P // 4))
@@ -196,10 +198,15 @@ def tile_attend_gsqh_adam_kernel(tc, xT, wT, y, wt, xm, mT, vT, offs, out_0, out
         x_q1 = quantize("x1", weave_x(1, scalar_cuts=(0, P // 2)), E4M3)
         hinges = [gradient(0, *x_q0), gradient(1, *x_q1)]
         v_got = [gather(v_tab[j], "v_got%d" % j) for j in range(2)]
-        g_woven0 = weigh(0, *hinges[0])
-        xm_woven0 = weave_on_scalar("xm_woven0", xm_raw[0])
+        xm_woven0 = woven_tile("xm_woven0")
+        for h in range(2):
+            dst = xm_woven0[:, h * PACK * D // 2:(h + 1) * PACK * D // 2].rearrange("p (c i t) -> p c t i", i=PACK, t=PACK)
+            nc.scalar.copy(dst, xm_parts[h][:].rearrange("p t (c i) -> p c t i", i=PACK))
+            if h == 0:
+                g_woven0 = weigh(0, *hinges[0])
         g_woven1 = weigh(1, *hinges[1])
-        xm_woven1 = weave_on_scalar("xm_woven1", xm_raw[1])
+        xm_woven1 = woven_tile("xm_woven1")
+        nc.scalar.copy(*weave_views(xm_woven1, xm_raw1))
         g_q = [quantize("g0", g_woven0, E5M2), quantize("g1", g_woven1, E5M2)]
         xm_q = [quantize("xm0", xm_woven0, E4M3), quantize("xm1", xm_woven1, E4M3)]
         v_got.extend([gather(v_tab[j], "v_got%d" % j) for j in range(2, D_TILES)])
@@ -215,7 +222,8 @@ def tile_attend_gsqh_adam_kernel(tc, xT, wT, y, wt, xm, mT, vT, offs, out_0, out
                 nc.tensor.matmul_mx(out=dw[j][:], lhsT=xm_q[g][0][:, block(j)].bitcast(E4M3), lhsT_scale=xm_q[g][1][:, block(j)],
                                     rhs=g_q[g][0][:].bitcast(E5M2), rhs_scale=g_q[g][1][:], start=(g == 0), stop=(g == PASSES - 1))
 
-        v_decayed = [row_tile("v_decayed%d" % j) for j in range(D_TILES)]
+        decayed = quad_tile("xm_raw1")
+        v_decayed = [decayed[:, j, :] for j in range(D_TILES)]
         dw_sq = [row_tile("dw_sq%d" % j) for j in range(D_TILES)]
         dw_sb = quad_tile("x_raw1")
         nm_t = quad_tile("y_raw0")
@@ -237,9 +245,9 @@ def tile_attend_gsqh_adam_kernel(tc, xT, wT, y, wt, xm, mT, vT, offs, out_0, out
             return bank[:]
 
         for j in range(D_TILES):
-            nc.scalar.activation(v_decayed[j][:], v_got[j][:], ACT.Copy, scale=RHO)
+            nc.scalar.activation(v_decayed[j], v_got[j][:], ACT.Copy, scale=RHO)
             nc.scalar.activation(dw_sq[j][:], dw[j][:], ACT.Square, scale=math.sqrt(1.0 - RHO))
-            nc.vector.tensor_tensor(v_win[j][:].indirect(offsets[:]), v_decayed[j][:], dw_sq[j][:], ALU.add)
+            nc.vector.tensor_tensor(v_win[j][:].indirect(offsets[:]), v_decayed[j], dw_sq[j][:], ALU.add)
             nc.sync.dma_start(out_2[block(j), :], v_win[j][:])
         for j in range(D_TILES):
             nc.scalar.copy(dw_sb[:, j, :], dw[j][:])

@@ -74,50 +74,41 @@ def tile_attend_gsqh_adam_kernel(tc, xT, wT, y, wt, xm, mT, vT, offs, out_0, out
         w_tab = [table_tile("w_tab%d" % t) for t in range(PACK)]
         x_raw = [quad_tile("x_raw%d" % g) for g in range(PASSES)]
         y_raw = [quad_tile("y_raw%d" % g) for g in range(PASSES)]
-        xm_parts = [keep.tile([P, PACK, D // 2], F32, name="xm_part%d" % h, tag="xm_part%d" % h, align_bytes=64)
-                    for h in range(2)]
-        xm_raw1 = quad_tile("xm_raw1")
+        xm_raw = [[keep.tile([P, PACK, D // 2], F32, name="xm_raw%d_%d" % (g, h), tag="xm_raw%d_%d" % (g, h), align_bytes=64)
+                   for h in range(2)] for g in range(PASSES)]
         m_tab = [table_tile("m_tab%d" % j) for j in range(D_TILES)]
         v_tab = [table_tile("v_tab%d" % j) for j in range(D_TILES)]
         m_win = [table_tile("m_win%d" % j) for j in range(D_TILES)]
         step_win = [table_tile("step_win%d" % j) for j in range(D_TILES)]
         wt_sb = keep.tile([P, PASSES, PACK], F32, name="wt_sb")
 
-        def load_x(g, half):
-            src = xT[0, :, pass_rows(g)].rearrange("(p j) r -> p j r", j=PACK)
-            cols = slice(half * K_PASS // 2, (half + 1) * K_PASS // 2)
-            nc.sync.dma_start(x_raw[g][:, :, cols], src[:, :, cols])
+        def load_x(g):
+            nc.sync.dma_start(x_raw[g][:], xT[0, :, pass_rows(g)].rearrange("(p j) r -> p j r", j=PACK))
 
         def load_y(g, half):
             src = y[0, pass_rows(g), :].rearrange("(p t) n -> p t n", t=PACK)
             planes = slice(half * PACK // 2, (half + 1) * PACK // 2)
             nc.sync.dma_start(y_raw[g][:, planes, :], src[:, planes, :])
 
-        def load_xm(tile, g, lo, hi):
+        def load_xm(g, h):
             src = xm[0, pass_rows(g), :].rearrange("(p t) d -> p t d", t=PACK)
-            nc.sync.dma_start(tile[:], src[:, :, lo:hi])
+            nc.sync.dma_start(xm_raw[g][h][:], src[:, :, h * D // 2:(h + 1) * D // 2])
 
         def load_table(tile, table, j):
             nc.sync.dma_start(tile[:], table[block(j), :])
 
+        nc.scalar.dma_start(wt_sb[:], wt[0].rearrange("(g p t) o -> p g (t o)", p=P, t=PACK))
         for t in range(PACK):
             nc.sync.dma_start(w_tab[t][:], w_planes[t])
-        load_x(0, 0)
-        load_x(0, 1)
-        nc.sync.dma_start(wt_sb[:], wt[0].rearrange("(g p t) o -> p g (t o)", p=P, t=PACK))
-        load_x(1, 0)
-        load_x(1, 1)
-        load_y(0, 0)
-        load_y(0, 1)
-        load_y(1, 0)
-        load_y(1, 1)
+        for g in range(PASSES):
+            load_x(g)
+        for g in range(PASSES):
+            load_y(g, 0)
+            load_y(g, 1)
         load_table(v_tab[0], vT, 0)
         load_table(v_tab[1], vT, 1)
-        load_xm(xm_parts[0], 0, 0, D // 2)
-        load_xm(xm_parts[1], 0, D // 2, D)
-        load_table(v_tab[2], vT, 2)
-        load_table(v_tab[3], vT, 3)
-        load_xm(xm_raw1, 1, 0, D)
+        load_xm(0, 0)
+        load_xm(1, 0)
 
         one = keep.tile([P, 1], F32, name="one")
         nc.vector.memset(one[:], 1.0)
@@ -138,10 +129,18 @@ def tile_attend_gsqh_adam_kernel(tc, xT, wT, y, wt, xm, mT, vT, offs, out_0, out
         nc.vector.tensor_copy(w_dst[:, :, 2:, :], w_src[:, :, 2:, :])
 
         v_win = [table_tile("w_tab%d" % j) for j in range(D_TILES)]
-        for j in range(D_TILES):
-            load_table(m_tab[j], mT, j)
-        for j in range(D_TILES):
-            load_table(v_win[j], vT, j)
+        load_table(v_tab[2], vT, 2)
+        load_table(v_tab[3], vT, 3)
+        load_table(m_tab[0], mT, 0)
+        load_table(m_tab[1], mT, 1)
+        load_table(m_tab[2], mT, 2)
+        load_table(v_win[0], vT, 0)
+        load_xm(0, 1)
+        load_xm(1, 1)
+        load_table(v_win[1], vT, 1)
+        load_table(m_tab[3], mT, 3)
+        load_table(v_win[2], vT, 2)
+        load_table(v_win[3], vT, 3)
         for j in range(D_TILES):
             load_table(m_win[j], mT, j)
 
@@ -187,48 +186,60 @@ def tile_attend_gsqh_adam_kernel(tc, xT, wT, y, wt, xm, mT, vT, offs, out_0, out
             for t in range(on_gpsimd, PACK):
                 nc.vector.scalar_tensor_tensor(g_planes[:, t, :], hinge[:, t, :], neg_wt[:, g, t:t + 1], y_raw[g][:, t, :],
                                                ALU.mult, ALU.mult)
-            woven = woven_tile(("xm_part0", "g_woven1")[g])
+            woven = woven_tile(("xm_raw0_0", "g_woven1")[g])
             nc.scalar.copy(*weave_views(woven, g_planes))
             return woven
 
-        x_woven0 = weave_x(0, scalar_cuts=(0, P // 2, 3 * P // 4))
+        def weave_xm(g, h, woven):
+            nc.scalar.copy(woven.rearrange("p (c i t) -> p c t i", i=PACK, t=PACK),
+                           xm_raw[g][h][:].rearrange("p t (c i) -> p c t i", i=PACK))
+            return woven
+
+        def gather_pair(tag, first, second):
+            pair = keep.tile([P, 2, N], F32, name=tag, tag=tag, align_bytes=64)
+            for k, table in enumerate((first, second)):
+                nc.vector.tensor_copy(pair[:, k, :], table[:].indirect(offsets[:]))
+            return pair[:, 0, :], pair[:, 1, :]
+
+        def quantize_xm(g, h, woven):
+            codes = keep.tile([P, D // 2], U32, name="xm_codes%d_%d" % (g, h), tag="xm_codes%d_%d" % (g, h), align_bytes=64)
+            scales = keep.tile([P, D // 2], U8, name="xm_scales%d_%d" % (g, h), align_bytes=64)
+            nc.vector.quantize_mx(out=codes[:].bitcast(E4M3), scales=scales[:], in_=woven)
+            return codes, scales
+
+        def dw_half(h, xm_q):
+            for jj in range(2):
+                for g in range(PASSES):
+                    nc.tensor.matmul_mx(out=dw[2 * h + jj][:], lhsT=xm_q[g][0][:, block(jj)].bitcast(E4M3),
+                                        lhsT_scale=xm_q[g][1][:, block(jj)],
+                                        rhs=g_q[g][0][:].bitcast(E5M2), rhs_scale=g_q[g][1][:],
+                                        start=(g == 0), stop=(g == PASSES - 1))
+
+        x_woven0 = weave_x(0, scalar_cuts=(0, P // 2))
         w_codes, w_scales = quantize("w", w_woven, E4M3)
-        x_q0 = quantize("x0", x_woven0, E4M3, cuts=(0, P, 2 * P, K_PASS))
+        x_q0 = quantize("x0", x_woven0, E4M3)
         nc.scalar.activation(neg_wt[:], wt_sb[:], ACT.Copy, scale=-1.0)
-        x_q1 = quantize("x1", weave_x(1, scalar_cuts=(0, P // 2)), E4M3)
+        x_q1 = quantize("x1", weave_x(1, scalar_cuts=(0, 44)), E4M3)
         hinges = [gradient(0, *x_q0), gradient(1, *x_q1)]
-        v_got = [gather(v_tab[j], "v_got%d" % j) for j in range(2)]
-        xm_woven0 = woven_tile("xm_woven0")
-        for h in range(2):
-            dst = xm_woven0[:, h * PACK * D // 2:(h + 1) * PACK * D // 2].rearrange("p (c i t) -> p c t i", i=PACK, t=PACK)
-            nc.scalar.copy(dst, xm_parts[h][:].rearrange("p t (c i) -> p c t i", i=PACK))
-            if h == 0:
-                g_woven0 = weigh(0, *hinges[0])
+        v_got = [gather(v_tab[j], "v_got%d" % j)[:] for j in (0, 1)]
+        early = keep.tile([P, PASSES, PACK * D // 2], BF16, name="xm_early", tag="xm_early", align_bytes=64)
+        xm_woven = [weave_xm(0, 0, early[:, 0, :])]
+        g_woven0 = weigh(0, *hinges[0])
         g_woven1 = weigh(1, *hinges[1])
-        xm_woven1 = woven_tile("xm_woven1")
-        nc.scalar.copy(*weave_views(xm_woven1, xm_raw1))
+        xm_woven.append(weave_xm(1, 0, early[:, 1, :]))
         g_q = [quantize("g0", g_woven0, E5M2), quantize("g1", g_woven1, E5M2)]
-        xm_q = [quantize("xm0", xm_woven0, E4M3), quantize("xm1", xm_woven1, E4M3)]
-        v_got.extend([gather(v_tab[j], "v_got%d" % j) for j in range(2, D_TILES)])
-        m_got = [gather(m_tab[j], "m_got%d" % j)[:] for j in range(2)]
-        m_late = keep.tile([P, 2, N], F32, name="m_late", tag="xm_woven1", align_bytes=64)
-        for j in range(2):
-            nc.vector.tensor_copy(m_late[:, j, :], m_tab[2 + j][:].indirect(offsets[:]))
-            m_got.append(m_late[:, j, :])
-
+        xm_q_first = [quantize_xm(g, 0, xm_woven[g]) for g in range(PASSES)]
+        v_got.extend([gather(v_tab[j], "v_got%d" % j)[:] for j in (2, 3)])
+        m_got = [gather(m_tab[0], "m_got0")[:]]
+        m_got.extend(gather_pair("g_woven1", m_tab[1], m_tab[2]))
         dw = [psum.tile([P, N], F32, name="bank_d%d" % j, tag="bank_d%d" % j) for j in range(D_TILES)]
-        for g in range(PASSES):
-            for j in range(D_TILES):
-                nc.tensor.matmul_mx(out=dw[j][:], lhsT=xm_q[g][0][:, block(j)].bitcast(E4M3), lhsT_scale=xm_q[g][1][:, block(j)],
-                                    rhs=g_q[g][0][:].bitcast(E5M2), rhs_scale=g_q[g][1][:], start=(g == 0), stop=(g == PASSES - 1))
 
-        decayed = quad_tile("xm_raw1")
+        decayed = quad_tile("v_tab1")
         v_decayed = [decayed[:, j, :] for j in range(D_TILES)]
-        dw_sq = [row_tile("dw_sq%d" % j) for j in range(D_TILES)]
-        dw_sb = quad_tile("x_raw1")
+        dw_sq = [row_tile(tag) for tag in ("dw_sq0", "xm_raw1_1", "dw_sq2", "dw_sq3")]
+        dw_sb = quad_tile("xm_raw0_1")
         nm_t = quad_tile("y_raw0")
         nm = quad_tile("x_raw0")
-        denom_t = quad_tile("y_raw1")
         rate = quad_tile("hinge0")
 
         def turned_sum(j, first, second):
@@ -245,7 +256,15 @@ def tile_attend_gsqh_adam_kernel(tc, xT, wT, y, wt, xm, mT, vT, offs, out_0, out
             return bank[:]
 
         for j in range(D_TILES):
-            nc.scalar.activation(v_decayed[j], v_got[j][:], ACT.Copy, scale=RHO)
+            if j == 0:
+                dw_half(0, xm_q_first)
+            if j == 1:
+                late = keep.tile([P, PASSES, PACK * D // 2], BF16, name="xm_late", tag="xm_codes1_0", align_bytes=64)
+                late_woven = [weave_xm(g, 1, late[:, g, :]) for g in range(PASSES)]
+            if j == 2:
+                dw_half(1, [quantize_xm(g, 1, late_woven[g]) for g in range(PASSES)])
+                m_got.append(gather(m_tab[3], "m_got3")[:])
+            nc.scalar.activation(v_decayed[j], v_got[j], ACT.Copy, scale=RHO)
             nc.scalar.activation(dw_sq[j][:], dw[j][:], ACT.Square, scale=math.sqrt(1.0 - RHO))
             nc.vector.tensor_tensor(v_win[j][:].indirect(offsets[:]), v_decayed[j], dw_sq[j][:], ALU.add)
             nc.sync.dma_start(out_2[block(j), :], v_win[j][:])
@@ -255,6 +274,7 @@ def tile_attend_gsqh_adam_kernel(tc, xT, wT, y, wt, xm, mT, vT, offs, out_0, out
             nc.scalar.copy(nm[:, j, :], turn_back(j, nm_t))
             nc.vector.tensor_copy(m_win[j][:].indirect(offsets[:]), nm[:, j, :])
             nc.sync.dma_start(out_1[block(j), :], m_win[j][:])
+        denom_t = quad_tile("xm_codes1_0")
         for j in range(D_TILES):
             nc.scalar.activation(denom_t[:, j, :], turned_sum(j, v_decayed[j], dw_sq[j]), ACT.Sqrt)
         nc.scalar.activation(denom_t[:], denom_t[:], ACT.Square, bias=eps[:])

@@ -23,43 +23,37 @@ PACK = 4
 K_PASS = P * PACK
 PASSES = R // K_PASS
 D_TILES = D // P
-GPSIMD_PLANES = 4
 LIST_BAND = 16
 
 assert D == K_PASS and N == K_PASS and PASSES == 2
 assert BETA == 1.0 - BETA
 
 
+X_ON_SCALAR = (88, 76)
+HALF = N // 2
+
+
 def tile_attend_gsqh_adam_kernel(tc, xT, wT, y, wt, xm, mT, vT, offs, out_0, out_1, out_2):
     nc = tc.nc
     with ExitStack() as ctx:
         keep = ctx.enter_context(tc.tile_pool(name="keep", bufs=1))
+        laid = ctx.enter_context(tc.tile_pool(name="laid", bufs=1))
         psum = ctx.enter_context(tc.psum_pool(name="psum", bufs=1))
 
-        def table_tile(tag):
-            return keep.tile([P, T], F32, name=tag, tag=tag, align_bytes=64)
+        def sbuf(shape, dtype, name, place=None):
+            return keep.tile([P] + shape, dtype, name=name, tag=place or name, align_bytes=64)
 
-        def quad_tile(tag):
-            return keep.tile([P, PACK, K_PASS], F32, name=tag, tag=tag, align_bytes=64)
+        def woven_view(woven):
+            return woven.rearrange("p (c i t) -> p c t i", i=PACK, t=PACK)
 
-        def woven_tile(tag):
-            return keep.tile([P, PACK * K_PASS], BF16, name=tag, tag=tag, align_bytes=64)
+        def planes_view(planes):
+            return planes.rearrange("p t (c i) -> p c t i", i=PACK)
 
-        def weave_views(woven, planes):
-            return (woven[:].rearrange("p (c i t) -> p c t i", i=PACK, t=PACK),
-                    planes[:].rearrange("p t (c i) -> p c t i", i=PACK))
+        def quantize(codes, scales, woven, fmt):
+            nc.vector.quantize_mx(out=codes.bitcast(fmt), scales=scales, in_=woven)
 
-        def deal_views(woven, planes):
-            return (woven[:].rearrange("p (t s j) -> p s j t", t=PACK, j=PACK),
-                    planes[:].rearrange("p j (s t) -> p s j t", t=PACK))
-
-        def quantize(tag, woven, fmt, cuts=(0, K_PASS), place=None):
-            codes = keep.tile([P, K_PASS], U32, name=tag + "_codes", tag=place or tag + "_codes", align_bytes=64)
-            scales = keep.tile([P, K_PASS], U8, name=tag + "_scales", align_bytes=64)
-            for lo, hi in zip(cuts, cuts[1:]):
-                nc.vector.quantize_mx(out=codes[:, lo:hi].bitcast(fmt), scales=scales[:, lo:hi],
-                                      in_=woven[:, PACK * lo:PACK * hi])
-            return codes, scales
+        def mx_tiles(name, width):
+            return sbuf([width], U32, name + "_codes"), sbuf([width], U8, name + "_scales")
 
         def pass_rows(g):
             return slice(g * K_PASS, (g + 1) * K_PASS)
@@ -67,28 +61,33 @@ def tile_attend_gsqh_adam_kernel(tc, xT, wT, y, wt, xm, mT, vT, offs, out_0, out
         def block(n):
             return slice(n * P, (n + 1) * P)
 
+        def half(h):
+            return slice(h * HALF, (h + 1) * HALF)
+
         offsets = keep.tile([P, N // LIST_BAND], U16, name="offsets")
         nc.sync.dma_start(offsets[:], offs)
 
         w_planes = wT.rearrange("(p t) c -> t p c", t=PACK)
-        w_tab = [table_tile("w_tab%d" % t) for t in range(PACK)]
-        x_raw = [quad_tile("x_raw%d" % g) for g in range(PASSES)]
-        y_raw = [quad_tile("y_raw%d" % g) for g in range(PASSES)]
-        xm_raw = [[keep.tile([P, PACK, D // 2], F32, name="xm_raw%d_%d" % (g, h), tag="xm_raw%d_%d" % (g, h), align_bytes=64)
-                   for h in range(2)] for g in range(PASSES)]
-        m_tab = [table_tile("m_tab%d" % j) for j in range(D_TILES)]
-        v_tab = [table_tile("v_tab%d" % j) for j in range(D_TILES)]
-        m_win = [table_tile("m_win%d" % j) for j in range(D_TILES)]
-        step_win = [table_tile("step_win%d" % j) for j in range(D_TILES)]
+        w_tab = [sbuf([T], F32, "w_tab%d" % t) for t in range(PACK)]
+        x_raw = [sbuf([PACK, K_PASS], F32, "x_raw%d" % g) for g in range(PASSES)]
+        y_raw = [[sbuf([2, N], F32, "y_raw%d_%d" % (g, pair)) for pair in range(2)] for g in range(PASSES)]
+        xm_raw = [[sbuf([PACK, D // 2], F32, "xm_raw%d_%d" % (g, h)) for h in range(2)] for g in range(PASSES)]
+        m_tab = [laid.tile([P, T], F32, name="m_tab0", offset=0, align_bytes=64)]
+        m_tab.extend(sbuf([T], F32, "m_tab%d" % j) for j in range(1, D_TILES))
+        v_tab = [sbuf([T], F32, "v_tab%d" % j) for j in range(D_TILES)]
+        step_win = [sbuf([T], F32, "step_win%d" % j) for j in range(D_TILES)]
         wt_sb = keep.tile([P, PASSES, PACK], F32, name="wt_sb")
 
         def load_x(g):
             nc.sync.dma_start(x_raw[g][:], xT[0, :, pass_rows(g)].rearrange("(p j) r -> p j r", j=PACK))
 
-        def load_y(g, half):
+        def load_y(g, pair):
             src = y[0, pass_rows(g), :].rearrange("(p t) n -> p t n", t=PACK)
-            planes = slice(half * PACK // 2, (half + 1) * PACK // 2)
-            nc.sync.dma_start(y_raw[g][:, planes, :], src[:, planes, :])
+            planes = slice(2 * pair, 2 * pair + 2)
+            nc.sync.dma_start(y_raw[g][pair][:], src[:, planes, :])
+
+        def y_plane(g, t):
+            return y_raw[g][t // 2][:, t % 2, :]
 
         def load_xm(g, h):
             src = xm[0, pass_rows(g), :].rearrange("(p t) d -> p t d", t=PACK)
@@ -105,142 +104,144 @@ def tile_attend_gsqh_adam_kernel(tc, xT, wT, y, wt, xm, mT, vT, offs, out_0, out
         for g in range(PASSES):
             load_y(g, 0)
             load_y(g, 1)
-        load_table(v_tab[0], vT, 0)
-        load_table(v_tab[1], vT, 1)
+        for j in range(D_TILES):
+            load_table(v_tab[j], vT, j)
+        load_table(m_tab[0], mT, 0)
         load_xm(0, 0)
         load_xm(1, 0)
+        load_table(m_tab[1], mT, 1)
 
         one = keep.tile([P, 1], F32, name="one")
         nc.vector.memset(one[:], 1.0)
         for j in range(D_TILES):
-            (nc.gpsimd if j == D_TILES - 1 else nc.vector).memset(step_win[j][:], 0.0)
+            (nc.gpsimd if j % 2 else nc.vector).memset(step_win[j][:], 0.0)
         ident = keep.tile([P, P], F32, name="ident")
         make_identity(nc, ident[:])
         eps = keep.tile([P, 1], F32, name="eps")
         nc.scalar.activation(eps[:], one[:], ACT.Copy, scale=EPS)
         neg_wt = keep.tile([P, PASSES, PACK], F32, name="neg_wt")
+        nc.scalar.activation(neg_wt[:], wt_sb[:], ACT.Copy, scale=-1.0)
 
-        w_got = quad_tile("w_got")
-        for t in range(PACK):
+        w_got = sbuf([PACK, N], F32, "w_got")
+        for t in range(PACK - 1):
             nc.vector.tensor_copy(w_got[:, t, :], w_tab[t][:].indirect(offsets[:]))
-        w_woven = woven_tile("w_woven")
-        w_dst, w_src = weave_views(w_woven, w_got)
-        nc.scalar.copy(w_dst[:, :, :2, :], w_src[:, :, :2, :])
-        nc.vector.tensor_copy(w_dst[:, :, 2:, :], w_src[:, :, 2:, :])
+        for h in range(2):
+            listed = offsets[:, h * HALF // LIST_BAND:(h + 1) * HALF // LIST_BAND]
+            nc.vector.tensor_copy(w_got[:, PACK - 1, half(h)], w_tab[PACK - 1][:].indirect(listed))
+        w_woven = sbuf([PACK * N], BF16, "w_woven")
+        nc.scalar.copy(woven_view(w_woven[:, :PACK * HALF]), planes_view(w_got[:, :, half(0)]))
+        nc.vector.tensor_copy(woven_view(w_woven[:, PACK * HALF:]), planes_view(w_got[:, :, half(1)]))
+        w_codes, w_scales = mx_tiles("w", N)
+        quantize(w_codes[:], w_scales[:], w_woven[:], E4M3)
 
-        v_win = [table_tile("w_tab%d" % j) for j in range(D_TILES)]
-        load_table(v_tab[2], vT, 2)
-        load_table(v_tab[3], vT, 3)
-        load_table(m_tab[0], mT, 0)
-        load_table(m_tab[1], mT, 1)
-        load_table(m_tab[2], mT, 2)
+        v_win = [sbuf([T], F32, "v_win%d" % j, "w_tab%d" % j) for j in range(D_TILES)]
         load_table(v_win[0], vT, 0)
+        load_table(m_tab[2], mT, 2)
         load_xm(0, 1)
         load_xm(1, 1)
         load_table(v_win[1], vT, 1)
         load_table(m_tab[3], mT, 3)
-        load_table(v_win[2], vT, 2)
-        load_table(v_win[3], vT, 3)
-        for j in range(D_TILES):
-            load_table(m_win[j], mT, j)
+        for j in range(2, D_TILES):
+            load_table(v_win[j], vT, j)
 
-        def row_tile(tag):
-            return keep.tile([P, N], F32, name=tag, tag=tag, align_bytes=64)
-
-        def gather(table, tag):
-            got = row_tile(tag)
+        def gather(table, name, place=None):
+            got = sbuf([N], F32, name, place)
             nc.vector.tensor_copy(got[:], table[:].indirect(offsets[:]))
-            return got
+            return got[:]
 
-        def weave_x(g, scalar_cuts):
-            woven = woven_tile("x_woven%d" % g)
-            dst, src = deal_views(woven, x_raw[g])
-            for lo, hi in zip(scalar_cuts, scalar_cuts[1:]):
-                nc.scalar.copy(dst[:, lo:hi], src[:, lo:hi])
-            if scalar_cuts[-1] < P:
-                nc.vector.tensor_copy(dst[:, scalar_cuts[-1]:], src[:, scalar_cuts[-1]:])
+        def weave_x(g, place=None):
+            woven = sbuf([PACK * K_PASS], BF16, "x_woven%d" % g, place)
+            dst = woven[:].rearrange("p (t s j) -> p s j t", t=PACK, j=PACK)
+            src = x_raw[g][:].rearrange("p j (s t) -> p s j t", t=PACK)
+            nc.scalar.copy(dst[:, :X_ON_SCALAR[g]], src[:, :X_ON_SCALAR[g]])
+            if X_ON_SCALAR[g] < P:
+                nc.vector.tensor_copy(dst[:, X_ON_SCALAR[g]:], src[:, X_ON_SCALAR[g]:])
             return woven
 
-        def gradient(g, x_codes, x_scales):
-            hinge = quad_tile(("hinge0", "w_got")[g])
-            g_planes = keep.tile([P, PACK, N], BF16, name="g_planes%d" % g, tag=("g_planes0", "v_tab1")[g], align_bytes=64)
-            on_gpsimd = GPSIMD_PLANES if g == 0 else 0
-            weight = keep.tile([P, GPSIMD_PLANES, N], F32, name="weight", align_bytes=64) if on_gpsimd else None
+        def quantize_x(g, woven):
+            codes, scales = mx_tiles("x%d" % g, K_PASS)
+            quantize(codes[:], scales[:], woven[:], E4M3)
+            return codes, scales
+
+        def hinges(g, x_codes, x_scales, hinge):
             for t in range(PACK):
-                if t < on_gpsimd:
-                    if t < PACK // 2:
-                        nc.scalar.activation(weight[:, t, :], y_raw[g][:, t, :], ACT.Copy, scale=neg_wt[:, g, t:t + 1])
-                    else:
-                        nc.gpsimd.tensor_scalar(weight[:, t, :], y_raw[g][:, t, :], neg_wt[:, g, t:t + 1], 0.0, ALU.mult, ALU.add)
                 bank = "bank_%s%d" % ("ad"[g], t)
                 scores = psum.tile([P, N], F32, name=bank, tag=bank)
                 nc.tensor.matmul_mx(out=scores[:], lhsT=x_codes[:, block(t)].bitcast(E4M3), lhsT_scale=x_scales[:, block(t)],
                                     rhs=w_codes[:].bitcast(E4M3), rhs_scale=w_scales[:], start=True, stop=True)
-                nc.vector.tensor_tensor(hinge[:, t, :], scores[:], y_raw[g][:, t, :], ALU.mult)
+                nc.vector.tensor_tensor(hinge[:, t, :], scores[:], y_plane(g, t), ALU.mult)
                 nc.scalar.activation(hinge[:, t, :], hinge[:, t, :], ACT.Relu, bias=one[:], scale=-1.0)
-            return hinge, weight, g_planes, on_gpsimd
 
-        def weigh(g, hinge, weight, g_planes, on_gpsimd):
-            for t in range(on_gpsimd):
-                nc.gpsimd.tensor_tensor(g_planes[:, t, :], hinge[:, t, :], weight[:, t, :], ALU.mult)
-            for t in range(on_gpsimd, PACK):
-                nc.vector.scalar_tensor_tensor(g_planes[:, t, :], hinge[:, t, :], neg_wt[:, g, t:t + 1], y_raw[g][:, t, :],
-                                               ALU.mult, ALU.mult)
-            woven = woven_tile(("xm_raw0_0", "g_woven1")[g])
-            nc.scalar.copy(*weave_views(woven, g_planes))
+        def weave_xm(name, place, h, columns):
+            width = columns.stop - columns.start
+            woven = sbuf([PASSES, PACK * width], BF16, name, place)
+            for g in range(PASSES):
+                nc.scalar.copy(woven_view(woven[:, g, :]), planes_view(xm_raw[g][h][:, :, columns]))
             return woven
 
-        def weave_xm(g, h, woven):
-            nc.scalar.copy(woven.rearrange("p (c i t) -> p c t i", i=PACK, t=PACK),
-                           xm_raw[g][h][:].rearrange("p t (c i) -> p c t i", i=PACK))
-            return woven
-
-        def gather_pair(tag, first, second):
-            pair = keep.tile([P, 2, N], F32, name=tag, tag=tag, align_bytes=64)
-            for k, table in enumerate((first, second)):
-                nc.vector.tensor_copy(pair[:, k, :], table[:].indirect(offsets[:]))
-            return pair[:, 0, :], pair[:, 1, :]
-
-        def quantize_xm(g, h, woven):
-            codes = keep.tile([P, D // 2], U32, name="xm_codes%d_%d" % (g, h), tag="xm_codes%d_%d" % (g, h), align_bytes=64)
-            scales = keep.tile([P, D // 2], U8, name="xm_scales%d_%d" % (g, h), align_bytes=64)
-            nc.vector.quantize_mx(out=codes[:].bitcast(E4M3), scales=scales[:], in_=woven)
+        def quantize_xm(name, woven):
+            width = woven.shape[2] // PACK
+            codes = sbuf([PASSES, width], U32, name + "_codes")
+            scales = sbuf([PASSES, width], U8, name + "_scales")
+            quantize(codes[:].rearrange("p g c -> p (g c)"), scales[:].rearrange("p g c -> p (g c)"),
+                     woven[:].rearrange("p g c -> p (g c)"), E4M3)
             return codes, scales
 
-        def dw_half(h, xm_q):
-            for jj in range(2):
+        x_q0 = quantize_x(0, weave_x(0))
+        x_woven1 = weave_x(1)
+        hinge = [sbuf([PACK, N], F32, "hinge0"), sbuf([PACK, N], F32, "hinge1", "w_got")]
+        hinges(0, *x_q0, hinge[0])
+        hinges(1, *quantize_x(1, x_woven1), hinge[1])
+
+        weight0 = sbuf([PACK, N], F32, "weight0")
+        g_planes0 = sbuf([PACK, N], BF16, "g_planes0")
+        for t in range(PACK):
+            nc.gpsimd.tensor_scalar(weight0[:, t, :], y_plane(0, t), neg_wt[:, 0, t:t + 1], 0.0, ALU.mult, ALU.add)
+            nc.gpsimd.tensor_tensor(g_planes0[:, t, :], hinge[0][:, t, :], weight0[:, t, :], ALU.mult)
+        weight1 = [sbuf([PACK, HALF], F32, "weight1%d" % h, "x_raw%d" % h) for h in range(2)]
+        for h in (1, 0):
+            for t in range(PACK):
+                nc.scalar.activation(weight1[h][:, t, :], y_plane(1, t)[:, half(h)], ACT.Copy, scale=neg_wt[:, 1, t:t + 1])
+        g_planes1 = sbuf([PACK, HALF], BF16, "g_planes1")
+        for t in range(PACK):
+            nc.gpsimd.tensor_tensor(g_planes1[:, t, :], hinge[1][:, t, half(1)], weight1[1][:, t, :], ALU.mult)
+        v_got = [gather(v_tab[j], "v_got%d" % j) for j in range(D_TILES)]
+        m_got = [gather(m_tab[0], "m_got0")]
+        g_woven0 = sbuf([PACK * N], BF16, "g_woven0")
+        nc.scalar.copy(woven_view(g_woven0[:]), planes_view(g_planes0[:]))
+        xm_woven = weave_xm("xm_first", None, 0, block(0))
+        g_woven1 = [laid.tile([P, PACK * HALF], BF16, name="g_woven10", offset=0, align_bytes=64), sbuf([PACK * HALF], BF16, "g_woven11")]
+        nc.scalar.copy(woven_view(g_woven1[1][:]), planes_view(g_planes1[:]))
+        nc.vector.tensor_tensor(woven_view(g_woven1[0][:]), planes_view(hinge[1][:, :, half(0)]),
+                                planes_view(weight1[0][:]), ALU.mult)
+        g_q = [(laid.tile([P, N], U32, name="g0_codes", offset=4 * N, align_bytes=64), sbuf([N], U8, "g0_scales")), mx_tiles("g1", N)]
+        quantize(g_q[0][0][:], g_q[0][1][:], g_woven0[:], E5M2)
+        xm_q = quantize_xm("xm_first", xm_woven)
+        for h in range(2):
+            quantize(g_q[1][0][:, half(h)], g_q[1][1][:, half(h)], g_woven1[h][:], E5M2)
+        first = sbuf([2, N], F32, "first", "g_planes1")
+        nc.vector.tensor_copy(first[:, 1, :], m_tab[1][:].indirect(offsets[:]))
+        m_got.append(first[:, 1, :])
+        later = sbuf([D_TILES - 1, N], F32, "later", "xm_first_scales")
+        v_decayed = [first[:, 0, :]] + [later[:, j, :] for j in range(D_TILES - 1)]
+        m_win = [sbuf([T], F32, "m_win%d" % j, "v_tab%d" % j) for j in range(D_TILES)]
+        for j in range(D_TILES):
+            load_table(m_win[j], mT, j)
+        dw = [psum.tile([P, N], F32, name="bank_d%d" % j, tag="bank_d%d" % j) for j in range(D_TILES)]
+
+        def make_dw(tiles, codes, scales):
+            for jj, j in enumerate(tiles):
                 for g in range(PASSES):
-                    nc.tensor.matmul_mx(out=dw[2 * h + jj][:], lhsT=xm_q[g][0][:, block(jj)].bitcast(E4M3),
-                                        lhsT_scale=xm_q[g][1][:, block(jj)],
+                    nc.tensor.matmul_mx(out=dw[j][:], lhsT=codes[:, g, block(jj)].bitcast(E4M3),
+                                        lhsT_scale=scales[:, g, block(jj)],
                                         rhs=g_q[g][0][:].bitcast(E5M2), rhs_scale=g_q[g][1][:],
                                         start=(g == 0), stop=(g == PASSES - 1))
 
-        x_woven0 = weave_x(0, scalar_cuts=(0, P // 2))
-        w_codes, w_scales = quantize("w", w_woven, E4M3)
-        x_q0 = quantize("x0", x_woven0, E4M3)
-        nc.scalar.activation(neg_wt[:], wt_sb[:], ACT.Copy, scale=-1.0)
-        x_q1 = quantize("x1", weave_x(1, scalar_cuts=(0, 44)), E4M3)
-        hinges = [gradient(0, *x_q0), gradient(1, *x_q1)]
-        v_got = [gather(v_tab[j], "v_got%d" % j)[:] for j in (0, 1)]
-        early = keep.tile([P, PASSES, PACK * D // 2], BF16, name="xm_early", tag="xm_early", align_bytes=64)
-        xm_woven = [weave_xm(0, 0, early[:, 0, :])]
-        g_woven0 = weigh(0, *hinges[0])
-        g_woven1 = weigh(1, *hinges[1])
-        xm_woven.append(weave_xm(1, 0, early[:, 1, :]))
-        g_q = [quantize("g0", g_woven0, E5M2), quantize("g1", g_woven1, E5M2)]
-        xm_q_first = [quantize_xm(g, 0, xm_woven[g]) for g in range(PASSES)]
-        v_got.extend([gather(v_tab[j], "v_got%d" % j)[:] for j in (2, 3)])
-        m_got = [gather(m_tab[0], "m_got0")[:]]
-        m_got.extend(gather_pair("g_woven1", m_tab[1], m_tab[2]))
-        dw = [psum.tile([P, N], F32, name="bank_d%d" % j, tag="bank_d%d" % j) for j in range(D_TILES)]
-
-        decayed = quad_tile("v_tab1")
-        v_decayed = [decayed[:, j, :] for j in range(D_TILES)]
-        dw_sq = [row_tile(tag) for tag in ("dw_sq0", "xm_raw1_1", "dw_sq2", "dw_sq3")]
-        dw_sb = quad_tile("xm_raw0_1")
-        nm_t = quad_tile("y_raw0")
-        nm = quad_tile("x_raw0")
-        rate = quad_tile("hinge0")
+        dw_sq = [sbuf([N], F32, "dw_sq%d" % j, place) for j, place in enumerate((None, "xm_raw1_1", None, None))]
+        dw_sb = sbuf([D_TILES, N], F32, "dw_sb", "xm_raw0_1")
+        nm_t = sbuf([D_TILES, N], F32, "nm_t", "x_raw1")
+        nm = sbuf([D_TILES, N], F32, "nm", "x_raw0")
+        rate = sbuf([D_TILES, N], F32, "rate", "hinge0")
 
         def turned_sum(j, first, second):
             bank = psum.tile([P, N // P, P], F32, name="bank_a%d" % j, tag="bank_a%d" % j)
@@ -257,13 +258,12 @@ def tile_attend_gsqh_adam_kernel(tc, xT, wT, y, wt, xm, mT, vT, offs, out_0, out
 
         for j in range(D_TILES):
             if j == 0:
-                dw_half(0, xm_q_first)
+                make_dw([0], *xm_q)
+                make_dw([1], *quantize_xm("xm_second", weave_xm("xm_second", "xm_first", 0, block(1))))
+                m_got.append(gather(m_tab[2], "m_got2", "xm_raw1_0"))
             if j == 1:
-                late = keep.tile([P, PASSES, PACK * D // 2], BF16, name="xm_late", tag="xm_codes1_0", align_bytes=64)
-                late_woven = [weave_xm(g, 1, late[:, g, :]) for g in range(PASSES)]
-            if j == 2:
-                dw_half(1, [quantize_xm(g, 1, late_woven[g]) for g in range(PASSES)])
-                m_got.append(gather(m_tab[3], "m_got3")[:])
+                make_dw([2, 3], *quantize_xm("xm_late", weave_xm("xm_late", "xm_first_codes", 1, slice(0, D // 2))))
+                m_got.append(gather(m_tab[3], "m_got3"))
             nc.scalar.activation(v_decayed[j], v_got[j], ACT.Copy, scale=RHO)
             nc.scalar.activation(dw_sq[j][:], dw[j][:], ACT.Square, scale=math.sqrt(1.0 - RHO))
             nc.vector.tensor_tensor(v_win[j][:].indirect(offsets[:]), v_decayed[j], dw_sq[j][:], ALU.add)
@@ -274,7 +274,7 @@ def tile_attend_gsqh_adam_kernel(tc, xT, wT, y, wt, xm, mT, vT, offs, out_0, out
             nc.scalar.copy(nm[:, j, :], turn_back(j, nm_t))
             nc.vector.tensor_copy(m_win[j][:].indirect(offsets[:]), nm[:, j, :])
             nc.sync.dma_start(out_1[block(j), :], m_win[j][:])
-        denom_t = quad_tile("xm_codes1_0")
+        denom_t = sbuf([D_TILES, N], F32, "denom_t", "xm_first_codes")
         for j in range(D_TILES):
             nc.scalar.activation(denom_t[:, j, :], turned_sum(j, v_decayed[j], dw_sq[j]), ACT.Sqrt)
         nc.scalar.activation(denom_t[:], denom_t[:], ACT.Square, bias=eps[:])

@@ -172,9 +172,7 @@ def tile_attend_gsqh_adam_kernel(tc, xT, wT, y, wt, xm, mT, vT, offs, out_0, out
                 nc.vector.tensor_tensor(hinge[:, t, :], scores[:], y_plane(g, t), ALU.mult)
                 nc.scalar.activation(hinge[:, t, :], hinge[:, t, :], ACT.Relu, bias=one[:], scale=-1.0)
 
-        def weave_xm(name, place, h, columns):
-            width = columns.stop - columns.start
-            woven = sbuf([PASSES, PACK * width], BF16, name, place)
+        def weave_xm(woven, h, columns):
             for g in range(PASSES):
                 nc.scalar.copy(woven_view(woven[:, g, :]), planes_view(xm_raw[g][h][:, :, columns]))
             return woven
@@ -209,8 +207,8 @@ def tile_attend_gsqh_adam_kernel(tc, xT, wT, y, wt, xm, mT, vT, offs, out_0, out
         m_got = [gather(m_tab[0], "m_got0")]
         g_woven0 = sbuf([PACK * N], BF16, "g_woven0")
         nc.scalar.copy(woven_view(g_woven0[:]), planes_view(g_planes0[:]))
-        xm_woven = weave_xm("xm_first", None, 0, block(0))
-        g_woven1 = [laid.tile([P, PACK * HALF], BF16, name="g_woven10", offset=0, align_bytes=64), sbuf([PACK * HALF], BF16, "g_woven11")]
+        xm_woven = weave_xm(sbuf([PASSES, PACK * D // 2], BF16, "xm_first"), 0, slice(0, D // 2))
+        g_woven1 = [laid.tile([P, PACK * HALF], BF16, name="g_woven10", offset=0, align_bytes=64), sbuf([PACK * HALF], BF16, "g_woven11", "xm_raw1_0")]
         nc.scalar.copy(woven_view(g_woven1[1][:]), planes_view(g_planes1[:]))
         nc.vector.tensor_tensor(woven_view(g_woven1[0][:]), planes_view(hinge[1][:, :, half(0)]),
                                 planes_view(weight1[0][:]), ALU.mult)
@@ -219,11 +217,9 @@ def tile_attend_gsqh_adam_kernel(tc, xT, wT, y, wt, xm, mT, vT, offs, out_0, out
         xm_q = quantize_xm("xm_first", xm_woven)
         for h in range(2):
             quantize(g_q[1][0][:, half(h)], g_q[1][1][:, half(h)], g_woven1[h][:], E5M2)
-        first = sbuf([2, N], F32, "first", "g_planes1")
-        nc.vector.tensor_copy(first[:, 1, :], m_tab[1][:].indirect(offsets[:]))
-        m_got.append(first[:, 1, :])
-        later = sbuf([D_TILES - 1, N], F32, "later", "xm_first_scales")
-        v_decayed = [first[:, 0, :]] + [later[:, j, :] for j in range(D_TILES - 1)]
+        first = sbuf([N], F32, "first", "g_planes1")
+        m_got.append(gather(m_tab[1], "m_got1", "xm_raw1_0"))
+        v_decayed = [first[:]]
         m_win = [sbuf([T], F32, "m_win%d" % j, "v_tab%d" % j) for j in range(D_TILES)]
         for j in range(D_TILES):
             load_table(m_win[j], mT, j)
@@ -258,12 +254,13 @@ def tile_attend_gsqh_adam_kernel(tc, xT, wT, y, wt, xm, mT, vT, offs, out_0, out
 
         for j in range(D_TILES):
             if j == 0:
-                make_dw([0], *xm_q)
-                make_dw([1], *quantize_xm("xm_second", weave_xm("xm_second", "xm_first", 0, block(1))))
-                m_got.append(gather(m_tab[2], "m_got2", "xm_raw1_0"))
+                make_dw([0, 1], *xm_q)
             if j == 1:
-                make_dw([2, 3], *quantize_xm("xm_late", weave_xm("xm_late", "xm_first_codes", 1, slice(0, D // 2))))
-                m_got.append(gather(m_tab[3], "m_got3"))
+                later = sbuf([D_TILES - 1, N], F32, "later", "xm_first_scales")
+                v_decayed.extend(later[:, k, :] for k in range(D_TILES - 1))
+                late = sbuf([PASSES, PACK * D // 2], BF16, "xm_late", "xm_first_codes")
+                make_dw([2, 3], *quantize_xm("xm_late", weave_xm(late, 1, slice(0, D // 2))))
+                m_got.extend(gather(m_tab[k], "m_got%d" % k) for k in (2, 3))
             nc.scalar.activation(v_decayed[j], v_got[j], ACT.Copy, scale=RHO)
             nc.scalar.activation(dw_sq[j][:], dw[j][:], ACT.Square, scale=math.sqrt(1.0 - RHO))
             nc.vector.tensor_tensor(v_win[j][:].indirect(offsets[:]), v_decayed[j], dw_sq[j][:], ALU.add)

@@ -71,7 +71,9 @@ def tile_attend_gsqh_adam_kernel(tc, xT, wT, y, wt, xm, mT, vT, offs, out_0, out
         w_tab = [sbuf([T], F32, "w_tab%d" % t) for t in range(PACK)]
         x_raw = [sbuf([PACK, K_PASS], F32, "x_raw%d" % g) for g in range(PASSES)]
         y_raw = [[sbuf([2, N], F32, "y_raw%d_%d" % (g, pair)) for pair in range(2)] for g in range(PASSES)]
-        xm_raw = [[sbuf([PACK, D // 2], F32, "xm_raw%d_%d" % (g, h)) for h in range(2)] for g in range(PASSES)]
+        xm_parts = (slice(0, P), slice(P, D))
+        xm_raw = [[sbuf([PACK, part.stop - part.start], F32, "xm_raw%d_%d" % (g, h)) for h, part in enumerate(xm_parts)]
+                  for g in range(PASSES)]
         m_tab = [laid.tile([P, T], F32, name="m_tab0", offset=0, align_bytes=64)]
         m_tab.extend(sbuf([T], F32, "m_tab%d" % j) for j in range(1, D_TILES))
         v_tab = [sbuf([T], F32, "v_tab%d" % j) for j in range(D_TILES)]
@@ -91,7 +93,7 @@ def tile_attend_gsqh_adam_kernel(tc, xT, wT, y, wt, xm, mT, vT, offs, out_0, out
 
         def load_xm(g, h):
             src = xm[0, pass_rows(g), :].rearrange("(p t) d -> p t d", t=PACK)
-            nc.sync.dma_start(xm_raw[g][h][:], src[:, :, h * D // 2:(h + 1) * D // 2])
+            nc.sync.dma_start(xm_raw[g][h][:], src[:, :, xm_parts[h]])
 
         def load_table(tile, table, j):
             nc.sync.dma_start(tile[:], table[block(j), :])
@@ -136,9 +138,9 @@ def tile_attend_gsqh_adam_kernel(tc, xT, wT, y, wt, xm, mT, vT, offs, out_0, out
 
         v_win = [sbuf([T], F32, "v_win%d" % j, "w_tab%d" % j) for j in range(D_TILES)]
         load_table(v_win[0], vT, 0)
-        load_table(m_tab[2], mT, 2)
         load_xm(0, 1)
         load_xm(1, 1)
+        load_table(m_tab[2], mT, 2)
         load_table(v_win[1], vT, 1)
         load_table(m_tab[3], mT, 3)
         for j in range(2, D_TILES):
@@ -172,17 +174,17 @@ def tile_attend_gsqh_adam_kernel(tc, xT, wT, y, wt, xm, mT, vT, offs, out_0, out
                 nc.vector.tensor_tensor(hinge[:, t, :], scores[:], y_plane(g, t), ALU.mult)
                 nc.scalar.activation(hinge[:, t, :], hinge[:, t, :], ACT.Relu, bias=one[:], scale=-1.0)
 
-        def weave_xm(woven, h, columns):
-            for g in range(PASSES):
-                nc.scalar.copy(woven_view(woven[:, g, :]), planes_view(xm_raw[g][h][:, :, columns]))
+        def weave_xm(name, h, tiles):
+            woven = sbuf([len(tiles) * PASSES, PACK * P], BF16, name)
+            for k, j in enumerate(tiles):
+                for g in range(PASSES):
+                    nc.scalar.copy(woven_view(woven[:, k * PASSES + g, :]), planes_view(xm_raw[g][h][:, :, block(j - h)]))
             return woven
 
         def quantize_xm(name, woven):
-            width = woven.shape[2] // PACK
-            codes = sbuf([PASSES, width], U32, name + "_codes")
-            scales = sbuf([PASSES, width], U8, name + "_scales")
-            quantize(codes[:].rearrange("p g c -> p (g c)"), scales[:].rearrange("p g c -> p (g c)"),
-                     woven[:].rearrange("p g c -> p (g c)"), E4M3)
+            codes = sbuf([woven.shape[1], P], U32, name + "_codes")
+            scales = sbuf([woven.shape[1], P], U8, name + "_scales")
+            quantize(*(tile[:].rearrange("p k c -> p (k c)") for tile in (codes, scales, woven)), E4M3)
             return codes, scales
 
         x_q0 = quantize_x(0, weave_x(0))
@@ -196,22 +198,20 @@ def tile_attend_gsqh_adam_kernel(tc, xT, wT, y, wt, xm, mT, vT, offs, out_0, out
         for t in range(PACK):
             nc.gpsimd.tensor_scalar(weight0[:, t, :], y_plane(0, t), neg_wt[:, 0, t:t + 1], 0.0, ALU.mult, ALU.add)
             nc.gpsimd.tensor_tensor(g_planes0[:, t, :], hinge[0][:, t, :], weight0[:, t, :], ALU.mult)
-        weight1 = [sbuf([PACK, HALF], F32, "weight1%d" % h, "x_raw%d" % h) for h in range(2)]
-        for h in (1, 0):
-            for t in range(PACK):
-                nc.scalar.activation(weight1[h][:, t, :], y_plane(1, t)[:, half(h)], ACT.Copy, scale=neg_wt[:, 1, t:t + 1])
+        weight1 = sbuf([PACK, N], F32, "weight1", "x_raw1")
         g_planes1 = sbuf([PACK, HALF], BF16, "g_planes1")
         for t in range(PACK):
-            nc.gpsimd.tensor_tensor(g_planes1[:, t, :], hinge[1][:, t, half(1)], weight1[1][:, t, :], ALU.mult)
+            nc.scalar.activation(weight1[:, t, :], y_plane(1, t), ACT.Copy, scale=neg_wt[:, 1, t:t + 1])
+            nc.gpsimd.tensor_tensor(g_planes1[:, t, :], hinge[1][:, t, half(1)], weight1[:, t, half(1)], ALU.mult)
         v_got = [gather(v_tab[j], "v_got%d" % j) for j in range(D_TILES)]
         m_got = [gather(m_tab[0], "m_got0")]
         g_woven0 = sbuf([PACK * N], BF16, "g_woven0")
         nc.scalar.copy(woven_view(g_woven0[:]), planes_view(g_planes0[:]))
-        xm_woven = weave_xm(sbuf([PASSES, PACK * D // 2], BF16, "xm_first"), 0, slice(0, D // 2))
+        xm_woven = weave_xm("xm_first", 0, [0])
         g_woven1 = [laid.tile([P, PACK * HALF], BF16, name="g_woven10", offset=0, align_bytes=64), sbuf([PACK * HALF], BF16, "g_woven11", "xm_raw1_0")]
         nc.scalar.copy(woven_view(g_woven1[1][:]), planes_view(g_planes1[:]))
         nc.vector.tensor_tensor(woven_view(g_woven1[0][:]), planes_view(hinge[1][:, :, half(0)]),
-                                planes_view(weight1[0][:]), ALU.mult)
+                                planes_view(weight1[:, :, half(0)]), ALU.mult)
         g_q = [(laid.tile([P, N], U32, name="g0_codes", offset=4 * N, align_bytes=64), sbuf([N], U8, "g0_scales")), mx_tiles("g1", N)]
         quantize(g_q[0][0][:], g_q[0][1][:], g_woven0[:], E5M2)
         xm_q = quantize_xm("xm_first", xm_woven)
@@ -228,12 +228,12 @@ def tile_attend_gsqh_adam_kernel(tc, xT, wT, y, wt, xm, mT, vT, offs, out_0, out
         def make_dw(tiles, codes, scales):
             for jj, j in enumerate(tiles):
                 for g in range(PASSES):
-                    nc.tensor.matmul_mx(out=dw[j][:], lhsT=codes[:, g, block(jj)].bitcast(E4M3),
-                                        lhsT_scale=scales[:, g, block(jj)],
+                    nc.tensor.matmul_mx(out=dw[j][:], lhsT=codes[:, jj * PASSES + g, :].bitcast(E4M3),
+                                        lhsT_scale=scales[:, jj * PASSES + g, :],
                                         rhs=g_q[g][0][:].bitcast(E5M2), rhs_scale=g_q[g][1][:],
                                         start=(g == 0), stop=(g == PASSES - 1))
 
-        dw_sq = [sbuf([N], F32, "dw_sq%d" % j, place) for j, place in enumerate((None, "xm_raw1_1", None, None))]
+        dw_sq = [sbuf([N], F32, "dw_sq%d" % j) for j in range(D_TILES)]
         dw_sb = sbuf([D_TILES, N], F32, "dw_sb", "xm_raw0_1")
         nm_t = sbuf([D_TILES, N], F32, "nm_t", "x_raw1")
         nm = sbuf([D_TILES, N], F32, "nm", "x_raw0")
@@ -254,13 +254,15 @@ def tile_attend_gsqh_adam_kernel(tc, xT, wT, y, wt, xm, mT, vT, offs, out_0, out
 
         for j in range(D_TILES):
             if j == 0:
-                make_dw([0, 1], *xm_q)
+                make_dw([0], *xm_q)
             if j == 1:
-                later = sbuf([D_TILES - 1, N], F32, "later", "xm_first_scales")
+                later = sbuf([D_TILES - 1, N], F32, "later", "xm_raw1_1")
                 v_decayed.extend(later[:, k, :] for k in range(D_TILES - 1))
-                late = sbuf([PASSES, PACK * D // 2], BF16, "xm_late", "xm_first_codes")
-                make_dw([2, 3], *quantize_xm("xm_late", weave_xm(late, 1, slice(0, D // 2))))
-                m_got.extend(gather(m_tab[k], "m_got%d" % k) for k in (2, 3))
+                make_dw([1], *quantize_xm("xm_second", weave_xm("xm_second", 1, [1])))
+                m_got.append(gather(m_tab[2], "m_got2"))
+                make_dw([2, 3], *quantize_xm("xm_late", weave_xm("xm_late", 1, [2, 3])))
+            if j == 2:
+                m_got.append(gather(m_tab[3], "m_got3"))
             nc.scalar.activation(v_decayed[j], v_got[j], ACT.Copy, scale=RHO)
             nc.scalar.activation(dw_sq[j][:], dw[j][:], ACT.Square, scale=math.sqrt(1.0 - RHO))
             nc.vector.tensor_tensor(v_win[j][:].indirect(offsets[:]), v_decayed[j], dw_sq[j][:], ALU.add)
@@ -271,7 +273,7 @@ def tile_attend_gsqh_adam_kernel(tc, xT, wT, y, wt, xm, mT, vT, offs, out_0, out
             nc.scalar.copy(nm[:, j, :], turn_back(j, nm_t))
             nc.vector.tensor_copy(m_win[j][:].indirect(offsets[:]), nm[:, j, :])
             nc.sync.dma_start(out_1[block(j), :], m_win[j][:])
-        denom_t = sbuf([D_TILES, N], F32, "denom_t", "xm_first_codes")
+        denom_t = sbuf([D_TILES, N], F32, "denom_t", "xm_late")
         for j in range(D_TILES):
             nc.scalar.activation(denom_t[:, j, :], turned_sum(j, v_decayed[j], dw_sq[j]), ACT.Sqrt)
         nc.scalar.activation(denom_t[:], denom_t[:], ACT.Square, bias=eps[:])

@@ -195,14 +195,18 @@ def tile_attend_gsqh_adam_kernel(tc, xT, wT, y, wt, xm, mT, vT, offs, out_0, out
 
         weight0 = sbuf([PACK, N], F32, "weight0")
         g_planes0 = sbuf([PACK, N], BF16, "g_planes0")
-        for t in range(PACK):
+        for t in (0, 1):
+            nc.scalar.activation(weight0[:, t, :], y_plane(0, t), ACT.Copy, scale=neg_wt[:, 0, t:t + 1])
+        for t in (2, 3):
             nc.gpsimd.tensor_scalar(weight0[:, t, :], y_plane(0, t), neg_wt[:, 0, t:t + 1], 0.0, ALU.mult, ALU.add)
-            nc.gpsimd.tensor_tensor(g_planes0[:, t, :], hinge[0][:, t, :], weight0[:, t, :], ALU.mult)
+        for planes in (slice(0, 2), slice(2, 4)):
+            nc.gpsimd.tensor_tensor(g_planes0[:, planes, :], hinge[0][:, planes, :], weight0[:, planes, :], ALU.mult)
         weight1 = sbuf([PACK, N], F32, "weight1", "x_raw1")
         g_planes1 = sbuf([PACK, HALF], BF16, "g_planes1")
-        for t in range(PACK):
-            nc.scalar.activation(weight1[:, t, :], y_plane(1, t), ACT.Copy, scale=neg_wt[:, 1, t:t + 1])
-            nc.gpsimd.tensor_tensor(g_planes1[:, t, :], hinge[1][:, t, half(1)], weight1[:, t, half(1)], ALU.mult)
+        for h in (1, 0):
+            for t in range(PACK):
+                nc.scalar.activation(weight1[:, t, half(h)], y_plane(1, t)[:, half(h)], ACT.Copy, scale=neg_wt[:, 1, t:t + 1])
+        nc.gpsimd.tensor_tensor(g_planes1[:], hinge[1][:, :, half(1)], weight1[:, :, half(1)], ALU.mult)
         v_got = [gather(v_tab[j], "v_got%d" % j) for j in range(D_TILES)]
         m_got = [gather(m_tab[0], "m_got0")]
         g_woven0 = sbuf([PACK * N], BF16, "g_woven0")

@@ -74,9 +74,9 @@ def tile_attend_gsqh_adam_kernel(tc, xT, wT, y, wt, xm, mT, vT, offs, out_0, out
         xm_parts = (slice(0, P), slice(P, D))
         xm_raw = [[sbuf([PACK, part.stop - part.start], F32, "xm_raw%d_%d" % (g, h)) for h, part in enumerate(xm_parts)]
                   for g in range(PASSES)]
-        m_tab = [laid.tile([P, T], F32, name="m_tab0", offset=0, align_bytes=64)]
-        m_tab.extend(sbuf([T], F32, "m_tab%d" % j) for j in range(1, D_TILES))
-        v_tab = [sbuf([T], F32, "v_tab%d" % j) for j in range(D_TILES)]
+        m_tab = [sbuf([T], F32, "m_tab%d" % j) for j in range(D_TILES)]
+        v_tab = [sbuf([T], F32, "v_tab%d" % j) for j in range(D_TILES - 1)]
+        v_tab.append(laid.tile([P, T], F32, name="v_tab3", offset=0, align_bytes=64))
         step_win = [sbuf([T], F32, "step_win%d" % j) for j in range(D_TILES)]
         wt_sb = keep.tile([P, PASSES, PACK], F32, name="wt_sb")
 
@@ -108,9 +108,9 @@ def tile_attend_gsqh_adam_kernel(tc, xT, wT, y, wt, xm, mT, vT, offs, out_0, out
             load_y(g, 1)
         for j in range(D_TILES):
             load_table(v_tab[j], vT, j)
-        load_table(m_tab[0], mT, 0)
         load_xm(0, 0)
         load_xm(1, 0)
+        load_table(m_tab[0], mT, 0)
         load_table(m_tab[1], mT, 1)
 
         one = keep.tile([P, 1], F32, name="one")
@@ -208,7 +208,6 @@ def tile_attend_gsqh_adam_kernel(tc, xT, wT, y, wt, xm, mT, vT, offs, out_0, out
                 nc.scalar.activation(weight1[:, t, half(h)], y_plane(1, t)[:, half(h)], ACT.Copy, scale=neg_wt[:, 1, t:t + 1])
         nc.gpsimd.tensor_tensor(g_planes1[:], hinge[1][:, :, half(1)], weight1[:, :, half(1)], ALU.mult)
         v_got = [gather(v_tab[j], "v_got%d" % j) for j in range(D_TILES)]
-        m_got = [gather(m_tab[0], "m_got0")]
         g_woven0 = sbuf([PACK * N], BF16, "g_woven0")
         nc.scalar.copy(woven_view(g_woven0[:]), planes_view(g_planes0[:]))
         xm_woven = weave_xm("xm_first", 0, [0])
@@ -218,13 +217,14 @@ def tile_attend_gsqh_adam_kernel(tc, xT, wT, y, wt, xm, mT, vT, offs, out_0, out
                                 planes_view(weight1[:, :, half(0)]), ALU.mult)
         g_q = [(laid.tile([P, N], U32, name="g0_codes", offset=4 * N, align_bytes=64), sbuf([N], U8, "g0_scales")), mx_tiles("g1", N)]
         quantize(g_q[0][0][:], g_q[0][1][:], g_woven0[:], E5M2)
+        quantize(g_q[1][0][:, half(0)], g_q[1][1][:, half(0)], g_woven1[0][:], E5M2)
+        m_got = [gather(m_tab[0], "m_got0")]
         xm_q = quantize_xm("xm_first", xm_woven)
-        for h in range(2):
-            quantize(g_q[1][0][:, half(h)], g_q[1][1][:, half(h)], g_woven1[h][:], E5M2)
+        quantize(g_q[1][0][:, half(1)], g_q[1][1][:, half(1)], g_woven1[1][:], E5M2)
         first = sbuf([N], F32, "first", "g_planes1")
         m_got.append(gather(m_tab[1], "m_got1", "xm_raw1_0"))
         v_decayed = [first[:]]
-        m_win = [sbuf([T], F32, "m_win%d" % j, "v_tab%d" % j) for j in range(D_TILES)]
+        m_win = [sbuf([T], F32, "m_win%d" % j, place) for j, place in enumerate(("v_tab0", "v_tab1", "v_tab2", "m_tab0"))]
         for j in range(D_TILES):
             load_table(m_win[j], mT, j)
         dw = [psum.tile([P, N], F32, name="bank_d%d" % j, tag="bank_d%d" % j) for j in range(D_TILES)]

@@ -117,6 +117,8 @@ def tile_attend_gsqh_adam_kernel(tc, xT, wT, y, wt, xm, mT, vT, offs, out_0, out
         nc.vector.memset(one[:], 1.0)
         for j in range(D_TILES):
             (nc.gpsimd if j % 2 else nc.vector).memset(step_win[j][:], 0.0)
+        minus_one = sbuf([N], F32, "minus_one")
+        nc.vector.memset(minus_one[:], -1.0)
         ident = keep.tile([P, P], F32, name="ident")
         make_identity(nc, ident[:])
         eps = keep.tile([P, 1], F32, name="eps")
@@ -273,16 +275,15 @@ def tile_attend_gsqh_adam_kernel(tc, xT, wT, y, wt, xm, mT, vT, offs, out_0, out
             nc.sync.dma_start(out_2[block(j), :], v_win[j][:])
         for j in range(D_TILES):
             nc.scalar.copy(dw_sb[:, j, :], dw[j][:])
-            nc.scalar.activation(nm_t[:, j, :], turned_sum(j, m_got[j], dw_sb[:, j, :]), ACT.Copy, scale=BETA)
+            nc.scalar.activation(nm_t[:, j, :], turned_sum(j, m_got[j], dw_sb[:, j, :]), ACT.Copy, scale=-BETA)
             nc.scalar.copy(nm[:, j, :], turn_back(j, nm_t))
-            nc.vector.tensor_copy(m_win[j][:].indirect(offsets[:]), nm[:, j, :])
+            nc.vector.tensor_tensor(m_win[j][:].indirect(offsets[:]), nm[:, j, :], minus_one[:], ALU.mult)
             nc.sync.dma_start(out_1[block(j), :], m_win[j][:])
         denom_t = sbuf([D_TILES, N], F32, "denom_t", "xm_late")
         for j in range(D_TILES):
             nc.scalar.activation(denom_t[:, j, :], turned_sum(j, v_decayed[j], dw_sq[j]), ACT.Sqrt)
         nc.scalar.activation(denom_t[:], denom_t[:], ACT.Square, bias=eps[:])
-        nc.scalar.activation(denom_t[:], denom_t[:], ACT.Abs_reciprocal_sqrt)
         for j in range(D_TILES):
-            nc.scalar.activation(rate[:, j, :], turn_back(j, denom_t), ACT.Copy, scale=-LR)
+            nc.scalar.activation(rate[:, j, :], turn_back(j, denom_t), ACT.Abs_reciprocal_sqrt, scale=1.0 / (LR * LR))
             nc.vector.tensor_tensor(step_win[j][:].indirect(offsets[:]), nm[:, j, :], rate[:, j, :], ALU.mult)
             nc.sync.dma_start(out_0[block(j), :], step_win[j][:])

@@ -29,7 +29,7 @@ assert D == K_PASS and N == K_PASS and PASSES == 2
 assert BETA == 1.0 - BETA
 
 
-X_ON_SCALAR = (88, 76)
+X_ON_SCALAR = (88, 56)
 HALF = N // 2
 
 
@@ -65,7 +65,6 @@ def tile_attend_gsqh_adam_kernel(tc, xT, wT, y, wt, xm, mT, vT, offs, out_0, out
             return slice(h * HALF, (h + 1) * HALF)
 
         offsets = keep.tile([P, N // LIST_BAND], U16, name="offsets")
-        nc.sync.dma_start(offsets[:], offs)
 
         w_planes = wT.rearrange("(p t) c -> t p c", t=PACK)
         w_tab = [sbuf([T], F32, "w_tab%d" % t) for t in range(PACK)]
@@ -99,7 +98,9 @@ def tile_attend_gsqh_adam_kernel(tc, xT, wT, y, wt, xm, mT, vT, offs, out_0, out
             nc.sync.dma_start(tile[:], table[block(j), :])
 
         nc.scalar.dma_start(wt_sb[:], wt[0].rearrange("(g p t) o -> p g (t o)", p=P, t=PACK))
-        for t in range(PACK):
+        nc.sync.dma_start(w_tab[0][:], w_planes[0])
+        nc.sync.dma_start(offsets[:], offs)
+        for t in range(1, PACK):
             nc.sync.dma_start(w_tab[t][:], w_planes[t])
         for g in range(PASSES):
             load_x(g)
@@ -191,9 +192,10 @@ def tile_attend_gsqh_adam_kernel(tc, xT, wT, y, wt, xm, mT, vT, offs, out_0, out
 
         x_q0 = quantize_x(0, weave_x(0))
         x_woven1 = weave_x(1)
-        hinge = [sbuf([PACK, N], F32, "hinge0"), sbuf([PACK, N], F32, "hinge1", "w_got")]
+        x_q1 = quantize_x(1, x_woven1)
+        hinge = [sbuf([PACK, N], F32, "hinge0", "x_woven1"), sbuf([PACK, N], F32, "hinge1", "w_got")]
         hinges(0, *x_q0, hinge[0])
-        hinges(1, *quantize_x(1, x_woven1), hinge[1])
+        hinges(1, *x_q1, hinge[1])
 
         weight0 = sbuf([PACK, N], F32, "weight0")
         g_planes0 = sbuf([PACK, N], BF16, "g_planes0")
@@ -243,7 +245,7 @@ def tile_attend_gsqh_adam_kernel(tc, xT, wT, y, wt, xm, mT, vT, offs, out_0, out
         dw_sb = sbuf([D_TILES, N], F32, "dw_sb", "xm_raw0_1")
         nm_t = sbuf([D_TILES, N], F32, "nm_t", "x_raw1")
         nm = sbuf([D_TILES, N], F32, "nm", "x_raw0")
-        rate = sbuf([D_TILES, N], F32, "rate", "hinge0")
+        rate = sbuf([D_TILES, N], F32, "rate", "x_woven1")
 
         def turned_sum(j, first, second):
             bank = psum.tile([P, N // P, P], F32, name="bank_a%d" % j, tag="bank_a%d" % j)

@@ -73,9 +73,9 @@ def tile_attend_gsqh_adam_kernel(tc, xT, wT, y, wt, xm, mT, vT, offs, out_0, out
         xm_parts = (slice(0, P), slice(P, D))
         xm_raw = [[sbuf([PACK, part.stop - part.start], F32, "xm_raw%d_%d" % (g, h)) for h, part in enumerate(xm_parts)]
                   for g in range(PASSES)]
-        m_tab = [sbuf([T], F32, "m_tab%d" % j) for j in range(D_TILES)]
-        v_tab = [sbuf([T], F32, "v_tab%d" % j) for j in range(D_TILES - 1)]
-        v_tab.append(laid.tile([P, T], F32, name="v_tab3", offset=0, align_bytes=64))
+        m_tab = [laid.tile([P, T], F32, name="m_tab0", offset=0, align_bytes=64)]
+        m_tab.extend(sbuf([T], F32, "m_tab%d" % j) for j in range(1, D_TILES))
+        v_tab = [sbuf([T], F32, "v_tab%d" % j) for j in range(D_TILES)]
         step_win = [sbuf([T], F32, "step_win%d" % j) for j in range(D_TILES)]
         wt_sb = keep.tile([P, PASSES, PACK], F32, name="wt_sb")
 
@@ -102,17 +102,19 @@ def tile_attend_gsqh_adam_kernel(tc, xT, wT, y, wt, xm, mT, vT, offs, out_0, out
         nc.sync.dma_start(offsets[:], offs)
         for t in range(1, PACK):
             nc.sync.dma_start(w_tab[t][:], w_planes[t])
+        load_table(v_tab[0], vT, 0)
         for g in range(PASSES):
             load_x(g)
         for g in range(PASSES):
             load_y(g, 0)
             load_y(g, 1)
-        for j in range(D_TILES):
+        for j in range(1, D_TILES):
             load_table(v_tab[j], vT, j)
+        load_table(m_tab[0], mT, 0)
         load_xm(0, 0)
         load_xm(1, 0)
-        load_table(m_tab[0], mT, 0)
         load_table(m_tab[1], mT, 1)
+        load_table(m_tab[2], mT, 2)
 
         one = keep.tile([P, 1], F32, name="one")
         nc.vector.memset(one[:], 1.0)
@@ -139,12 +141,11 @@ def tile_attend_gsqh_adam_kernel(tc, xT, wT, y, wt, xm, mT, vT, offs, out_0, out
         w_codes, w_scales = mx_tiles("w", N)
         quantize(w_codes[:], w_scales[:], w_woven[:], E4M3)
 
-        v_win = [sbuf([T], F32, "v_win%d" % j, "w_tab%d" % j) for j in range(D_TILES)]
-        load_table(v_win[0], vT, 0)
+        v_win = [sbuf([T], F32, "v_win%d" % j, "w_tab%d" % (D_TILES - 1 - j)) for j in range(D_TILES)]
+        nc.scalar.activation(v_win[0][:], v_tab[0][:], ACT.Copy)
+        load_table(v_win[1], vT, 1)
         load_xm(0, 1)
         load_xm(1, 1)
-        load_table(m_tab[2], mT, 2)
-        load_table(v_win[1], vT, 1)
         load_table(m_tab[3], mT, 3)
         for j in range(2, D_TILES):
             load_table(v_win[j], vT, j)
@@ -190,6 +191,7 @@ def tile_attend_gsqh_adam_kernel(tc, xT, wT, y, wt, xm, mT, vT, offs, out_0, out
             quantize(*(tile[:].rearrange("p k c -> p (k c)") for tile in (codes, scales, woven)), E4M3)
             return codes, scales
 
+        v_got = [gather(v_tab[0], "v_got0", "w_woven")]
         x_q0 = quantize_x(0, weave_x(0))
         x_woven1 = weave_x(1)
         x_q1 = quantize_x(1, x_woven1)
@@ -211,7 +213,8 @@ def tile_attend_gsqh_adam_kernel(tc, xT, wT, y, wt, xm, mT, vT, offs, out_0, out
             for t in range(PACK):
                 nc.scalar.activation(weight1[:, t, half(h)], y_plane(1, t)[:, half(h)], ACT.Copy, scale=neg_wt[:, 1, t:t + 1])
         nc.gpsimd.tensor_tensor(g_planes1[:], hinge[1][:, :, half(1)], weight1[:, :, half(1)], ALU.mult)
-        v_got = [gather(v_tab[j], "v_got%d" % j) for j in range(D_TILES)]
+        v_got.extend(gather(v_tab[j], "v_got%d" % j) for j in range(1, D_TILES))
+        m_got = [gather(m_tab[0], "m_got0")]
         g_woven0 = sbuf([PACK * N], BF16, "g_woven0")
         nc.scalar.copy(woven_view(g_woven0[:]), planes_view(g_planes0[:]))
         xm_woven = weave_xm("xm_first", 0, [0])
@@ -222,13 +225,13 @@ def tile_attend_gsqh_adam_kernel(tc, xT, wT, y, wt, xm, mT, vT, offs, out_0, out
         g_q = [(laid.tile([P, N], U32, name="g0_codes", offset=4 * N, align_bytes=64), sbuf([N], U8, "g0_scales")), mx_tiles("g1", N)]
         quantize(g_q[0][0][:], g_q[0][1][:], g_woven0[:], E5M2)
         quantize(g_q[1][0][:, half(0)], g_q[1][1][:, half(0)], g_woven1[0][:], E5M2)
-        m_got = [gather(m_tab[0], "m_got0")]
+        m_got.append(gather(m_tab[1], "m_got1"))
         xm_q = quantize_xm("xm_first", xm_woven)
         quantize(g_q[1][0][:, half(1)], g_q[1][1][:, half(1)], g_woven1[1][:], E5M2)
         first = sbuf([N], F32, "first", "g_planes1")
-        m_got.append(gather(m_tab[1], "m_got1", "xm_raw1_0"))
+        m_got.append(gather(m_tab[2], "m_got2", "xm_raw1_0"))
         v_decayed = [first[:]]
-        m_win = [sbuf([T], F32, "m_win%d" % j, place) for j, place in enumerate(("v_tab0", "v_tab1", "v_tab2", "m_tab0"))]
+        m_win = [sbuf([T], F32, "m_win%d" % j, place) for j, place in enumerate(("v_tab0", "v_tab1", "v_tab2", "v_tab3"))]
         for j in range(D_TILES):
             load_table(m_win[j], mT, j)
         dw = [psum.tile([P, N], F32, name="bank_d%d" % j, tag="bank_d%d" % j) for j in range(D_TILES)]
@@ -267,10 +270,8 @@ def tile_attend_gsqh_adam_kernel(tc, xT, wT, y, wt, xm, mT, vT, offs, out_0, out
                 later = sbuf([D_TILES - 1, N], F32, "later", "xm_raw1_1")
                 v_decayed.extend(later[:, k, :] for k in range(D_TILES - 1))
                 make_dw([1], *quantize_xm("xm_second", weave_xm("xm_second", 1, [1])))
-                m_got.append(gather(m_tab[2], "m_got2"))
+                m_got.append(gather(m_tab[3], "m_got3", "xm_second"))
                 make_dw([2, 3], *quantize_xm("xm_late", weave_xm("xm_late", 1, [2, 3])))
-            if j == 2:
-                m_got.append(gather(m_tab[3], "m_got3"))
             nc.scalar.activation(v_decayed[j], v_got[j], ACT.Copy, scale=RHO)
             nc.scalar.activation(dw_sq[j][:], dw[j][:], ACT.Square, scale=math.sqrt(1.0 - RHO))
             nc.vector.tensor_tensor(v_win[j][:].indirect(offsets[:]), v_decayed[j], dw_sq[j][:], ALU.add)

@@ -29,7 +29,7 @@ assert D == K_PASS and N == K_PASS and PASSES == 2
 assert BETA == 1.0 - BETA
 
 
-X_ON_SCALAR = (88, 56)
+X_ON_SCALAR = (88, 76)
 HALF = N // 2
 
 
@@ -43,11 +43,11 @@ def tile_attend_gsqh_adam_kernel(tc, xT, wT, y, wt, xm, mT, vT, offs, out_0, out
         def sbuf(shape, dtype, name, place=None):
             return keep.tile([P] + shape, dtype, name=name, tag=place or name, align_bytes=64)
 
-        def woven_view(woven):
-            return woven.rearrange("p (c i t) -> p c t i", i=PACK, t=PACK)
+        def woven_view(woven, run=PACK):
+            return woven.rearrange("p (c i t) -> p c t i", i=run, t=PACK)
 
-        def planes_view(planes):
-            return planes.rearrange("p t (c i) -> p c t i", i=PACK)
+        def planes_view(planes, run=PACK):
+            return planes.rearrange("p t (c i) -> p c t i", i=run)
 
         def quantize(codes, scales, woven, fmt):
             nc.vector.quantize_mx(out=codes.bitcast(fmt), scales=scales, in_=woven)
@@ -191,13 +191,12 @@ def tile_attend_gsqh_adam_kernel(tc, xT, wT, y, wt, xm, mT, vT, offs, out_0, out
             quantize(*(tile[:].rearrange("p k c -> p (k c)") for tile in (codes, scales, woven)), E4M3)
             return codes, scales
 
-        v_got = [gather(v_tab[0], "v_got0", "w_woven")]
+        v_got = [gather(v_tab[0], "v_got0")]
         x_q0 = quantize_x(0, weave_x(0))
         x_woven1 = weave_x(1)
-        x_q1 = quantize_x(1, x_woven1)
-        hinge = [sbuf([PACK, N], F32, "hinge0", "x_woven1"), sbuf([PACK, N], F32, "hinge1", "w_got")]
+        hinge = [sbuf([PACK, N], F32, "hinge0"), sbuf([PACK, N], F32, "hinge1", "w_got")]
         hinges(0, *x_q0, hinge[0])
-        hinges(1, *x_q1, hinge[1])
+        hinges(1, *quantize_x(1, x_woven1), hinge[1])
 
         weight0 = sbuf([PACK, N], F32, "weight0")
         g_planes0 = sbuf([PACK, N], BF16, "g_planes0")
@@ -220,8 +219,8 @@ def tile_attend_gsqh_adam_kernel(tc, xT, wT, y, wt, xm, mT, vT, offs, out_0, out
         xm_woven = weave_xm("xm_first", 0, [0])
         g_woven1 = [laid.tile([P, PACK * HALF], BF16, name="g_woven10", offset=0, align_bytes=64), sbuf([PACK * HALF], BF16, "g_woven11", "xm_raw1_0")]
         nc.scalar.copy(woven_view(g_woven1[1][:]), planes_view(g_planes1[:]))
-        nc.vector.tensor_tensor(woven_view(g_woven1[0][:]), planes_view(hinge[1][:, :, half(0)]),
-                                planes_view(weight1[:, :, half(0)]), ALU.mult)
+        nc.vector.tensor_tensor(woven_view(g_woven1[0][:], 2), planes_view(hinge[1][:, :, half(0)], 2),
+                                planes_view(weight1[:, :, half(0)], 2), ALU.mult)
         g_q = [(laid.tile([P, N], U32, name="g0_codes", offset=4 * N, align_bytes=64), sbuf([N], U8, "g0_scales")), mx_tiles("g1", N)]
         quantize(g_q[0][0][:], g_q[0][1][:], g_woven0[:], E5M2)
         quantize(g_q[1][0][:, half(0)], g_q[1][1][:, half(0)], g_woven1[0][:], E5M2)
@@ -248,7 +247,7 @@ def tile_attend_gsqh_adam_kernel(tc, xT, wT, y, wt, xm, mT, vT, offs, out_0, out
         dw_sb = sbuf([D_TILES, N], F32, "dw_sb", "xm_raw0_1")
         nm_t = sbuf([D_TILES, N], F32, "nm_t", "x_raw1")
         nm = sbuf([D_TILES, N], F32, "nm", "x_raw0")
-        rate = sbuf([D_TILES, N], F32, "rate", "x_woven1")
+        rate = sbuf([D_TILES, N], F32, "rate", "hinge0")
 
         def turned_sum(j, first, second):
             bank = psum.tile([P, N // P, P], F32, name="bank_a%d" % j, tag="bank_a%d" % j)
@@ -267,11 +266,13 @@ def tile_attend_gsqh_adam_kernel(tc, xT, wT, y, wt, xm, mT, vT, offs, out_0, out
             if j == 0:
                 make_dw([0], *xm_q)
             if j == 1:
-                later = sbuf([D_TILES - 1, N], F32, "later", "xm_raw1_1")
-                v_decayed.extend(later[:, k, :] for k in range(D_TILES - 1))
+                v_decayed.append(sbuf([N], F32, "v_decayed1", "xm_raw1_1")[:])
                 make_dw([1], *quantize_xm("xm_second", weave_xm("xm_second", 1, [1])))
-                m_got.append(gather(m_tab[3], "m_got3", "xm_second"))
+                m_got.append(gather(m_tab[3], "m_got3"))
                 make_dw([2, 3], *quantize_xm("xm_late", weave_xm("xm_late", 1, [2, 3])))
+            if j == 2:
+                later = sbuf([2, N], F32, "later", "xm_late_codes")
+                v_decayed.extend(later[:, k, :] for k in range(2))
             nc.scalar.activation(v_decayed[j], v_got[j], ACT.Copy, scale=RHO)
             nc.scalar.activation(dw_sq[j][:], dw[j][:], ACT.Square, scale=math.sqrt(1.0 - RHO))
             nc.vector.tensor_tensor(v_win[j][:].indirect(offsets[:]), v_decayed[j], dw_sq[j][:], ALU.add)

@@ -29,7 +29,7 @@ assert D == K_PASS and N == K_PASS and PASSES == 2
 assert BETA == 1.0 - BETA
 
 
-X_ON_SCALAR = (88, 76)
+X_ON_SCALAR = (72, 64)
 HALF = N // 2
 
 
@@ -70,7 +70,7 @@ def tile_attend_gsqh_adam_kernel(tc, xT, wT, y, wt, xm, mT, vT, offs, out_0, out
         w_tab = [sbuf([T], F32, "w_tab%d" % t) for t in range(PACK)]
         x_raw = [sbuf([PACK, K_PASS], F32, "x_raw%d" % g) for g in range(PASSES)]
         y_raw = [[sbuf([2, N], F32, "y_raw%d_%d" % (g, pair)) for pair in range(2)] for g in range(PASSES)]
-        xm_parts = (slice(0, P), slice(P, D))
+        xm_parts = (slice(0, P), slice(P, 2 * P), slice(2 * P, D))
         xm_raw = [[sbuf([PACK, part.stop - part.start], F32, "xm_raw%d_%d" % (g, h)) for h, part in enumerate(xm_parts)]
                   for g in range(PASSES)]
         m_tab = [laid.tile([P, T], F32, name="m_tab0", offset=0, align_bytes=64)]
@@ -114,6 +114,8 @@ def tile_attend_gsqh_adam_kernel(tc, xT, wT, y, wt, xm, mT, vT, offs, out_0, out
         load_xm(0, 0)
         load_xm(1, 0)
         load_table(m_tab[1], mT, 1)
+        load_xm(0, 1)
+        load_xm(1, 1)
         load_table(m_tab[2], mT, 2)
 
         one = keep.tile([P, 1], F32, name="one")
@@ -144,8 +146,8 @@ def tile_attend_gsqh_adam_kernel(tc, xT, wT, y, wt, xm, mT, vT, offs, out_0, out
         v_win = [sbuf([T], F32, "v_win%d" % j, "w_tab%d" % (D_TILES - 1 - j)) for j in range(D_TILES)]
         nc.scalar.activation(v_win[0][:], v_tab[0][:], ACT.Copy)
         load_table(v_win[1], vT, 1)
-        load_xm(0, 1)
-        load_xm(1, 1)
+        load_xm(0, 2)
+        load_xm(1, 2)
         load_table(m_tab[3], mT, 3)
         for j in range(2, D_TILES):
             load_table(v_win[j], vT, j)
@@ -178,8 +180,7 @@ def tile_attend_gsqh_adam_kernel(tc, xT, wT, y, wt, xm, mT, vT, offs, out_0, out
                 nc.vector.tensor_tensor(hinge[:, t, :], scores[:], y_plane(g, t), ALU.mult)
                 nc.scalar.activation(hinge[:, t, :], hinge[:, t, :], ACT.Relu, bias=one[:], scale=-1.0)
 
-        def weave_xm(name, h, tiles):
-            woven = sbuf([len(tiles) * PASSES, PACK * P], BF16, name)
+        def weave_xm(woven, h, tiles):
             for k, j in enumerate(tiles):
                 for g in range(PASSES):
                     nc.scalar.copy(woven_view(woven[:, k * PASSES + g, :]), planes_view(xm_raw[g][h][:, :, block(j - h)]))
@@ -207,7 +208,7 @@ def tile_attend_gsqh_adam_kernel(tc, xT, wT, y, wt, xm, mT, vT, offs, out_0, out
         for planes in (slice(0, 2), slice(2, 4)):
             nc.gpsimd.tensor_tensor(g_planes0[:, planes, :], hinge[0][:, planes, :], weight0[:, planes, :], ALU.mult)
         weight1 = sbuf([PACK, N], F32, "weight1", "x_raw1")
-        g_planes1 = sbuf([PACK, HALF], BF16, "g_planes1")
+        g_planes1 = laid.tile([P, PACK, HALF], BF16, name="g_planes1", offset=10 * N, align_bytes=64)
         for h in (1, 0):
             for t in range(PACK):
                 nc.scalar.activation(weight1[:, t, half(h)], y_plane(1, t)[:, half(h)], ACT.Copy, scale=neg_wt[:, 1, t:t + 1])
@@ -216,7 +217,7 @@ def tile_attend_gsqh_adam_kernel(tc, xT, wT, y, wt, xm, mT, vT, offs, out_0, out
         m_got = [gather(m_tab[0], "m_got0")]
         g_woven0 = sbuf([PACK * N], BF16, "g_woven0")
         nc.scalar.copy(woven_view(g_woven0[:]), planes_view(g_planes0[:]))
-        xm_woven = weave_xm("xm_first", 0, [0])
+        xm_woven = weave_xm(sbuf([PASSES, PACK * P], BF16, "xm_first"), 0, [0])
         g_woven1 = [laid.tile([P, PACK * HALF], BF16, name="g_woven10", offset=0, align_bytes=64), sbuf([PACK * HALF], BF16, "g_woven11", "xm_raw1_0")]
         nc.scalar.copy(woven_view(g_woven1[1][:]), planes_view(g_planes1[:]))
         nc.vector.tensor_tensor(woven_view(g_woven1[0][:], 2), planes_view(hinge[1][:, :, half(0)], 2),
@@ -227,7 +228,7 @@ def tile_attend_gsqh_adam_kernel(tc, xT, wT, y, wt, xm, mT, vT, offs, out_0, out
         m_got.append(gather(m_tab[1], "m_got1"))
         xm_q = quantize_xm("xm_first", xm_woven)
         quantize(g_q[1][0][:, half(1)], g_q[1][1][:, half(1)], g_woven1[1][:], E5M2)
-        first = sbuf([N], F32, "first", "g_planes1")
+        first = laid.tile([P, N], F32, name="first", offset=8 * N, align_bytes=64)
         m_got.append(gather(m_tab[2], "m_got2", "xm_raw1_0"))
         v_decayed = [first[:]]
         m_win = [sbuf([T], F32, "m_win%d" % j, place) for j, place in enumerate(("v_tab0", "v_tab1", "v_tab2", "v_tab3"))]
@@ -243,8 +244,8 @@ def tile_attend_gsqh_adam_kernel(tc, xT, wT, y, wt, xm, mT, vT, offs, out_0, out
                                         rhs=g_q[g][0][:].bitcast(E5M2), rhs_scale=g_q[g][1][:],
                                         start=(g == 0), stop=(g == PASSES - 1))
 
-        dw_sq = [sbuf([N], F32, "dw_sq%d" % j) for j in range(D_TILES)]
-        dw_sb = sbuf([D_TILES, N], F32, "dw_sb", "xm_raw0_1")
+        dw_sq = [sbuf([N], F32, "dw_sq%d" % j, "xm_raw1_2" if j == 1 else None) for j in range(D_TILES)]
+        dw_sb = sbuf([D_TILES, N], F32, "dw_sb", "xm_raw0_2")
         nm_t = sbuf([D_TILES, N], F32, "nm_t", "x_raw1")
         nm = sbuf([D_TILES, N], F32, "nm", "x_raw0")
         rate = sbuf([D_TILES, N], F32, "rate", "hinge0")
@@ -265,15 +266,19 @@ def tile_attend_gsqh_adam_kernel(tc, xT, wT, y, wt, xm, mT, vT, offs, out_0, out
         for j in range(D_TILES):
             if j == 0:
                 make_dw([0], *xm_q)
+                nc.scalar.activation(v_decayed[0], v_got[0], ACT.Copy, scale=RHO)
+                second = laid.tile([P, PASSES, PACK * P], BF16, name="xm_second", offset=12 * N, align_bytes=64)
+                make_dw([1], *quantize_xm("xm_second", weave_xm(second, 1, [1])))
             if j == 1:
-                v_decayed.append(sbuf([N], F32, "v_decayed1", "xm_raw1_1")[:])
-                make_dw([1], *quantize_xm("xm_second", weave_xm("xm_second", 1, [1])))
+                v_decayed.append(sbuf([N], F32, "v_decayed1", "xm_second_codes")[:])
+                late = sbuf([2 * PASSES, PACK * P], BF16, "xm_late")
+                make_dw([2, 3], *quantize_xm("xm_late", weave_xm(late, 2, [2, 3])))
                 m_got.append(gather(m_tab[3], "m_got3"))
-                make_dw([2, 3], *quantize_xm("xm_late", weave_xm("xm_late", 1, [2, 3])))
             if j == 2:
                 later = sbuf([2, N], F32, "later", "xm_late_codes")
                 v_decayed.extend(later[:, k, :] for k in range(2))
-            nc.scalar.activation(v_decayed[j], v_got[j], ACT.Copy, scale=RHO)
+            if j > 0:
+                nc.scalar.activation(v_decayed[j], v_got[j], ACT.Copy, scale=RHO)
             nc.scalar.activation(dw_sq[j][:], dw[j][:], ACT.Square, scale=math.sqrt(1.0 - RHO))
             nc.vector.tensor_tensor(v_win[j][:].indirect(offsets[:]), v_decayed[j], dw_sq[j][:], ALU.add)
             nc.sync.dma_start(out_2[block(j), :], v_win[j][:])

@@ -2,7 +2,6 @@ import math
 from contextlib import ExitStack
 
 import concourse.mybir as mybir
-from concourse.masks import make_identity
 
 N, T, D, R = 512, 1024, 512, 1024
 LR, BETA, RHO, EPS = 0.1, 0.5, 0.9, 0.001
@@ -28,20 +27,24 @@ LIST_BAND = 16
 assert D == K_PASS and N == K_PASS and PASSES == 2
 assert BETA == 1.0 - BETA
 
-
-X_ON_SCALAR = (72, 64)
+W_ON_SCALAR = 192
+X_ON_SCALAR = (56, 48)
 HALF = N // 2
+V_ON_VECTOR = 3
+M_ON_VECTOR = 2
 
 
 def tile_attend_gsqh_adam_kernel(tc, xT, wT, y, wt, xm, mT, vT, offs, out_0, out_1, out_2):
     nc = tc.nc
     with ExitStack() as ctx:
         keep = ctx.enter_context(tc.tile_pool(name="keep", bufs=1))
-        laid = ctx.enter_context(tc.tile_pool(name="laid", bufs=1))
         psum = ctx.enter_context(tc.psum_pool(name="psum", bufs=1))
 
         def sbuf(shape, dtype, name, place=None):
             return keep.tile([P] + shape, dtype, name=name, tag=place or name, align_bytes=64)
+
+        def bank(place):
+            return psum.tile([P, N], F32, name=place, tag=place)
 
         def woven_view(woven, run=PACK):
             return woven.rearrange("p (c i t) -> p c t i", i=run, t=PACK)
@@ -61,21 +64,19 @@ def tile_attend_gsqh_adam_kernel(tc, xT, wT, y, wt, xm, mT, vT, offs, out_0, out
         def block(n):
             return slice(n * P, (n + 1) * P)
 
-        def half(h):
-            return slice(h * HALF, (h + 1) * HALF)
-
         offsets = keep.tile([P, N // LIST_BAND], U16, name="offsets")
+
+        def listed(tile, first=0, last=N):
+            return tile[:].indirect(offsets[:, first // LIST_BAND:last // LIST_BAND])
 
         w_planes = wT.rearrange("(p t) c -> t p c", t=PACK)
         w_tab = [sbuf([T], F32, "w_tab%d" % t) for t in range(PACK)]
         x_raw = [sbuf([PACK, K_PASS], F32, "x_raw%d" % g) for g in range(PASSES)]
         y_raw = [[sbuf([2, N], F32, "y_raw%d_%d" % (g, pair)) for pair in range(2)] for g in range(PASSES)]
-        xm_parts = (slice(0, P), slice(P, 2 * P), slice(2 * P, D))
-        xm_raw = [[sbuf([PACK, part.stop - part.start], F32, "xm_raw%d_%d" % (g, h)) for h, part in enumerate(xm_parts)]
-                  for g in range(PASSES)]
-        m_tab = [laid.tile([P, T], F32, name="m_tab0", offset=0, align_bytes=64)]
-        m_tab.extend(sbuf([T], F32, "m_tab%d" % j) for j in range(1, D_TILES))
+        xm_raw = [sbuf([PACK, D], F32, "xm_raw%d" % g) for g in range(PASSES)]
         v_tab = [sbuf([T], F32, "v_tab%d" % j) for j in range(D_TILES)]
+        m_tab = [sbuf([T], F32, "m_tab%d" % j) for j in range(D_TILES)]
+        v_win = [sbuf([T], F32, "v_win%d" % j) for j in range(D_TILES)]
         step_win = [sbuf([T], F32, "step_win%d" % j) for j in range(D_TILES)]
         wt_sb = keep.tile([P, PASSES, PACK], F32, name="wt_sb")
 
@@ -84,15 +85,10 @@ def tile_attend_gsqh_adam_kernel(tc, xT, wT, y, wt, xm, mT, vT, offs, out_0, out
 
         def load_y(g, pair):
             src = y[0, pass_rows(g), :].rearrange("(p t) n -> p t n", t=PACK)
-            planes = slice(2 * pair, 2 * pair + 2)
-            nc.sync.dma_start(y_raw[g][pair][:], src[:, planes, :])
+            nc.sync.dma_start(y_raw[g][pair][:], src[:, 2 * pair:2 * pair + 2, :])
 
         def y_plane(g, t):
             return y_raw[g][t // 2][:, t % 2, :]
-
-        def load_xm(g, h):
-            src = xm[0, pass_rows(g), :].rearrange("(p t) d -> p t d", t=PACK)
-            nc.sync.dma_start(xm_raw[g][h][:], src[:, :, xm_parts[h]])
 
         def load_table(tile, table, j):
             nc.sync.dma_start(tile[:], table[block(j), :])
@@ -102,197 +98,145 @@ def tile_attend_gsqh_adam_kernel(tc, xT, wT, y, wt, xm, mT, vT, offs, out_0, out
         nc.sync.dma_start(offsets[:], offs)
         for t in range(1, PACK):
             nc.sync.dma_start(w_tab[t][:], w_planes[t])
-        load_table(v_tab[0], vT, 0)
         for g in range(PASSES):
             load_x(g)
         for g in range(PASSES):
             load_y(g, 0)
             load_y(g, 1)
-        for j in range(1, D_TILES):
+        load_table(v_tab[0], vT, 0)
+        for g in range(PASSES):
+            nc.sync.dma_start(xm_raw[g][:], xm[0, pass_rows(g), :].rearrange("(p t) d -> p t d", t=PACK))
+        for j in (1, 2):
             load_table(v_tab[j], vT, j)
-        load_table(m_tab[0], mT, 0)
-        load_xm(0, 0)
-        load_xm(1, 0)
-        load_table(m_tab[1], mT, 1)
-        load_xm(0, 1)
-        load_xm(1, 1)
-        load_table(m_tab[2], mT, 2)
+        load_table(v_win[0], vT, 0)
+        load_table(v_tab[3], vT, 3)
+        for j in (1, 2, 3):
+            load_table(v_win[j], vT, j)
+        for j in range(D_TILES):
+            load_table(m_tab[j], mT, j)
 
         one = keep.tile([P, 1], F32, name="one")
         nc.vector.memset(one[:], 1.0)
         for j in range(D_TILES):
-            (nc.gpsimd if j % 2 else nc.vector).memset(step_win[j][:], 0.0)
-        minus_one = sbuf([N], F32, "minus_one")
-        nc.vector.memset(minus_one[:], -1.0)
-        ident = keep.tile([P, P], F32, name="ident")
-        make_identity(nc, ident[:])
+            nc.gpsimd.memset(step_win[j][:], 0.0)
         eps = keep.tile([P, 1], F32, name="eps")
-        nc.scalar.activation(eps[:], one[:], ACT.Copy, scale=EPS)
+        nc.scalar.activation(eps[:], one[:], ACT.Copy, scale=(EPS / (LR * BETA)) ** 2)
+        tiny = keep.tile([P, 1], F32, name="tiny")
+        nc.scalar.activation(tiny[:], one[:], ACT.Copy, scale=1e-24)
         neg_wt = keep.tile([P, PASSES, PACK], F32, name="neg_wt")
         nc.scalar.activation(neg_wt[:], wt_sb[:], ACT.Copy, scale=-1.0)
 
         w_got = sbuf([PACK, N], F32, "w_got")
-        for t in range(PACK - 1):
-            nc.vector.tensor_copy(w_got[:, t, :], w_tab[t][:].indirect(offsets[:]))
-        for h in range(2):
-            listed = offsets[:, h * HALF // LIST_BAND:(h + 1) * HALF // LIST_BAND]
-            nc.vector.tensor_copy(w_got[:, PACK - 1, half(h)], w_tab[PACK - 1][:].indirect(listed))
+        nc.vector.tensor_copy(w_got[:, 0, :], listed(w_tab[0]))
+        nc.scalar.activation(w_got[:, 1, :], listed(w_tab[1]), ACT.Copy)
+        nc.vector.tensor_copy(w_got[:, 2, :], listed(w_tab[2]))
+        nc.scalar.activation(w_got[:, 3, :W_ON_SCALAR], listed(w_tab[3], 0, W_ON_SCALAR), ACT.Copy)
+        nc.vector.tensor_copy(w_got[:, 3, W_ON_SCALAR:], listed(w_tab[3], W_ON_SCALAR, N))
         w_woven = sbuf([PACK * N], BF16, "w_woven")
-        nc.scalar.copy(woven_view(w_woven[:, :PACK * HALF]), planes_view(w_got[:, :, half(0)]))
-        nc.vector.tensor_copy(woven_view(w_woven[:, PACK * HALF:]), planes_view(w_got[:, :, half(1)]))
+        nc.scalar.copy(woven_view(w_woven[:, :PACK * W_ON_SCALAR]), planes_view(w_got[:, :, :W_ON_SCALAR]))
+        nc.vector.tensor_copy(woven_view(w_woven[:, PACK * W_ON_SCALAR:]), planes_view(w_got[:, :, W_ON_SCALAR:]))
         w_codes, w_scales = mx_tiles("w", N)
         quantize(w_codes[:], w_scales[:], w_woven[:], E4M3)
 
-        v_win = [sbuf([T], F32, "v_win%d" % j, "w_tab%d" % (D_TILES - 1 - j)) for j in range(D_TILES)]
-        nc.scalar.activation(v_win[0][:], v_tab[0][:], ACT.Copy)
-        load_table(v_win[1], vT, 1)
-        load_xm(0, 2)
-        load_xm(1, 2)
-        load_table(m_tab[3], mT, 3)
-        for j in range(2, D_TILES):
-            load_table(v_win[j], vT, j)
+        m_win = [sbuf([T], F32, "m_win%d" % j, "w_tab%d" % j) for j in range(D_TILES)]
+        for j in range(D_TILES):
+            load_table(m_win[j], mT, j)
 
-        def gather(table, name, place=None):
-            got = sbuf([N], F32, name, place)
-            nc.vector.tensor_copy(got[:], table[:].indirect(offsets[:]))
-            return got[:]
-
-        def weave_x(g, place=None):
-            woven = sbuf([PACK * K_PASS], BF16, "x_woven%d" % g, place)
-            dst = woven[:].rearrange("p (t s j) -> p s j t", t=PACK, j=PACK)
+        x_q = []
+        for g in range(PASSES):
+            x_woven = sbuf([PACK * K_PASS], BF16, "x_woven%d" % g)
+            dst = x_woven[:].rearrange("p (t s j) -> p s j t", t=PACK, j=PACK)
             src = x_raw[g][:].rearrange("p j (s t) -> p s j t", t=PACK)
             nc.scalar.copy(dst[:, :X_ON_SCALAR[g]], src[:, :X_ON_SCALAR[g]])
-            if X_ON_SCALAR[g] < P:
-                nc.vector.tensor_copy(dst[:, X_ON_SCALAR[g]:], src[:, X_ON_SCALAR[g]:])
-            return woven
-
-        def quantize_x(g, woven):
-            codes, scales = mx_tiles("x%d" % g, K_PASS)
-            quantize(codes[:], scales[:], woven[:], E4M3)
-            return codes, scales
-
-        def hinges(g, x_codes, x_scales, hinge):
+            nc.vector.tensor_copy(dst[:, X_ON_SCALAR[g]:], src[:, X_ON_SCALAR[g]:])
+            x_q.append(mx_tiles("x%d" % g, K_PASS))
+            quantize(x_q[g][0][:], x_q[g][1][:], x_woven[:], E4M3)
+        hinge = [sbuf([PACK, N], F32, "hinge0"), sbuf([PACK, N], F32, "hinge1", "w_got")]
+        weight = [sbuf([PACK, N], F32, "weight0", "x_raw0"), sbuf([PACK, N], F32, "weight1")]
+        for g in range(PASSES):
             for t in range(PACK):
-                bank = "bank_%s%d" % ("ad"[g], t)
-                scores = psum.tile([P, N], F32, name=bank, tag=bank)
-                nc.tensor.matmul_mx(out=scores[:], lhsT=x_codes[:, block(t)].bitcast(E4M3), lhsT_scale=x_scales[:, block(t)],
+                scores = bank("bank_%s%d" % ("ab"[g], t))
+                nc.tensor.matmul_mx(out=scores[:], lhsT=x_q[g][0][:, block(t)].bitcast(E4M3), lhsT_scale=x_q[g][1][:, block(t)],
                                     rhs=w_codes[:].bitcast(E4M3), rhs_scale=w_scales[:], start=True, stop=True)
-                nc.vector.tensor_tensor(hinge[:, t, :], scores[:], y_plane(g, t), ALU.mult)
-                nc.scalar.activation(hinge[:, t, :], hinge[:, t, :], ACT.Relu, bias=one[:], scale=-1.0)
+                nc.gpsimd.tensor_scalar(weight[g][:, t, :], y_plane(g, t), neg_wt[:, g, t:t + 1], 0.0, ALU.mult, ALU.add)
+                margin = sbuf([N], F32, "margin", "g_woven0")[:] if (g, t) == (PASSES - 1, PACK - 2) else hinge[g][:, t, :]
+                nc.vector.tensor_tensor(margin, scores[:], y_plane(g, t), ALU.mult)
+                nc.scalar.activation(hinge[g][:, t, :], margin, ACT.Relu, bias=one[:], scale=-1.0)
+        g_woven = []
+        for g in range(PASSES):
+            g_woven.append(sbuf([PACK * N], BF16, "g_woven%d" % g))
+            nc.vector.tensor_tensor(woven_view(g_woven[g][:], 2), planes_view(hinge[g][:], 2), planes_view(weight[g][:], 2), ALU.mult)
 
-        def weave_xm(woven, h, tiles):
+        def weave_xm(name, tiles, copies, place=None):
+            woven = sbuf([len(tiles) * PASSES, PACK * P], BF16, name + "_woven", place)
             for k, j in enumerate(tiles):
                 for g in range(PASSES):
-                    nc.scalar.copy(woven_view(woven[:, k * PASSES + g, :]), planes_view(xm_raw[g][h][:, :, block(j - h)]))
+                    copies[g](woven_view(woven[:, k * PASSES + g, :]), planes_view(xm_raw[g][:, :, block(j)]))
             return woven
 
         def quantize_xm(name, woven):
-            codes = sbuf([woven.shape[1], P], U32, name + "_codes")
-            scales = sbuf([woven.shape[1], P], U8, name + "_scales")
-            quantize(*(tile[:].rearrange("p k c -> p (k c)") for tile in (codes, scales, woven)), E4M3)
+            codes, scales = mx_tiles(name, woven.shape[1] * P)
+            quantize(codes[:], scales[:], woven[:].rearrange("p k c -> p (k c)"), E4M3)
             return codes, scales
 
-        v_got = [gather(v_tab[0], "v_got0")]
-        x_q0 = quantize_x(0, weave_x(0))
-        x_woven1 = weave_x(1)
-        hinge = [sbuf([PACK, N], F32, "hinge0"), sbuf([PACK, N], F32, "hinge1", "w_got")]
-        hinges(0, *x_q0, hinge[0])
-        hinges(1, *quantize_x(1, x_woven1), hinge[1])
+        g_q = [mx_tiles("g%d" % g, N) for g in range(PASSES)]
+        dw = [bank("bank_a%d" % j) for j in range(D_TILES)]
 
-        weight0 = sbuf([PACK, N], F32, "weight0")
-        g_planes0 = sbuf([PACK, N], BF16, "g_planes0")
-        for t in (0, 1):
-            nc.scalar.activation(weight0[:, t, :], y_plane(0, t), ACT.Copy, scale=neg_wt[:, 0, t:t + 1])
-        for t in (2, 3):
-            nc.gpsimd.tensor_scalar(weight0[:, t, :], y_plane(0, t), neg_wt[:, 0, t:t + 1], 0.0, ALU.mult, ALU.add)
-        for planes in (slice(0, 2), slice(2, 4)):
-            nc.gpsimd.tensor_tensor(g_planes0[:, planes, :], hinge[0][:, planes, :], weight0[:, planes, :], ALU.mult)
-        weight1 = sbuf([PACK, N], F32, "weight1", "x_raw1")
-        g_planes1 = laid.tile([P, PACK, HALF], BF16, name="g_planes1", offset=10 * N, align_bytes=64)
-        for h in (1, 0):
-            for t in range(PACK):
-                nc.scalar.activation(weight1[:, t, half(h)], y_plane(1, t)[:, half(h)], ACT.Copy, scale=neg_wt[:, 1, t:t + 1])
-        nc.gpsimd.tensor_tensor(g_planes1[:], hinge[1][:, :, half(1)], weight1[:, :, half(1)], ALU.mult)
-        v_got.extend(gather(v_tab[j], "v_got%d" % j) for j in range(1, D_TILES))
-        m_got = [gather(m_tab[0], "m_got0")]
-        g_woven0 = sbuf([PACK * N], BF16, "g_woven0")
-        nc.scalar.copy(woven_view(g_woven0[:]), planes_view(g_planes0[:]))
-        xm_woven = weave_xm(sbuf([PASSES, PACK * P], BF16, "xm_first"), 0, [0])
-        g_woven1 = [laid.tile([P, PACK * HALF], BF16, name="g_woven10", offset=0, align_bytes=64), sbuf([PACK * HALF], BF16, "g_woven11", "xm_raw1_0")]
-        nc.scalar.copy(woven_view(g_woven1[1][:]), planes_view(g_planes1[:]))
-        nc.vector.tensor_tensor(woven_view(g_woven1[0][:], 2), planes_view(hinge[1][:, :, half(0)], 2),
-                                planes_view(weight1[:, :, half(0)], 2), ALU.mult)
-        g_q = [(laid.tile([P, N], U32, name="g0_codes", offset=4 * N, align_bytes=64), sbuf([N], U8, "g0_scales")), mx_tiles("g1", N)]
-        quantize(g_q[0][0][:], g_q[0][1][:], g_woven0[:], E5M2)
-        quantize(g_q[1][0][:, half(0)], g_q[1][1][:, half(0)], g_woven1[0][:], E5M2)
-        m_got.append(gather(m_tab[1], "m_got1"))
-        xm_q = quantize_xm("xm_first", xm_woven)
-        quantize(g_q[1][0][:, half(1)], g_q[1][1][:, half(1)], g_woven1[1][:], E5M2)
-        first = laid.tile([P, N], F32, name="first", offset=8 * N, align_bytes=64)
-        m_got.append(gather(m_tab[2], "m_got2", "xm_raw1_0"))
-        v_decayed = [first[:]]
-        m_win = [sbuf([T], F32, "m_win%d" % j, place) for j, place in enumerate(("v_tab0", "v_tab1", "v_tab2", "v_tab3"))]
-        for j in range(D_TILES):
-            load_table(m_win[j], mT, j)
-        dw = [psum.tile([P, N], F32, name="bank_d%d" % j, tag="bank_d%d" % j) for j in range(D_TILES)]
+        def dw_pass(j, g, codes, scales, k):
+            nc.tensor.matmul_mx(out=dw[j][:], lhsT=codes[:, block(k)].bitcast(E4M3), lhsT_scale=scales[:, block(k)],
+                                rhs=g_q[g][0][:].bitcast(E5M2), rhs_scale=g_q[g][1][:],
+                                start=(g == 0), stop=(g == PASSES - 1))
 
-        def make_dw(tiles, codes, scales):
-            for jj, j in enumerate(tiles):
+        xm_woven = weave_xm("xm0", [0], (nc.scalar.copy, nc.scalar.copy))
+        quantize(g_q[0][0][:], g_q[0][1][:], g_woven[0][:], E5M2)
+        xm_q = quantize_xm("xm0", xm_woven)
+        dw_pass(0, 0, *xm_q, 0)
+        quantize(g_q[1][0][:], g_q[1][1][:], g_woven[1][:], E5M2)
+        dw_pass(0, 1, *xm_q, 1)
+        for name, tiles, copy, place in (("xm1", [1], nc.scalar.copy, None), ("xm2", [2, 3], nc.vector.tensor_copy, "g_woven1")):
+            xm_q = quantize_xm(name, weave_xm(name, tiles, (copy, copy), place))
+            for k, j in enumerate(tiles):
                 for g in range(PASSES):
-                    nc.tensor.matmul_mx(out=dw[j][:], lhsT=codes[:, jj * PASSES + g, :].bitcast(E4M3),
-                                        lhsT_scale=scales[:, jj * PASSES + g, :],
-                                        rhs=g_q[g][0][:].bitcast(E5M2), rhs_scale=g_q[g][1][:],
-                                        start=(g == 0), stop=(g == PASSES - 1))
+                    dw_pass(j, g, *xm_q, k * PASSES + g)
 
-        dw_sq = [sbuf([N], F32, "dw_sq%d" % j, "xm_raw1_2" if j == 1 else None) for j in range(D_TILES)]
-        dw_sb = sbuf([D_TILES, N], F32, "dw_sb", "xm_raw0_2")
-        nm_t = sbuf([D_TILES, N], F32, "nm_t", "x_raw1")
-        nm = sbuf([D_TILES, N], F32, "nm", "x_raw0")
-        rate = sbuf([D_TILES, N], F32, "rate", "hinge0")
+        def scatter_on_scalar(window, values, scale):
+            for first in range(0, N, HALF):
+                nc.scalar.activation(listed(window, first, first + HALF), values[:, first:first + HALF], ACT.Copy, scale=scale)
 
-        def turned_sum(j, first, second):
-            bank = psum.tile([P, N // P, P], F32, name="bank_a%d" % j, tag="bank_a%d" % j)
-            for b in range(N // P):
-                nc.tensor.matmul(bank[:, b, :], first[:, block(b)], ident[:], start=True, stop=False, is_transpose=True)
-                nc.tensor.matmul(bank[:, b, :], second[:, block(b)], ident[:], start=False, stop=True, is_transpose=True)
-            return bank[:].rearrange("p b d -> p (b d)")
-
-        def turn_back(j, turned):
-            bank = psum.tile([P, N], F32, name="bank_d%d" % j, tag="bank_d%d" % j)
-            for b in range(N // P):
-                nc.tensor.transpose(bank[:, block(b)], turned[:, j, block(b)], ident[:])
-            return bank[:]
-
+        nv = sbuf([D_TILES, N], F32, "nv")
         for j in range(D_TILES):
-            if j == 0:
-                make_dw([0], *xm_q)
-                nc.scalar.activation(v_decayed[0], v_got[0], ACT.Copy, scale=RHO)
-                second = laid.tile([P, PASSES, PACK * P], BF16, name="xm_second", offset=12 * N, align_bytes=64)
-                make_dw([1], *quantize_xm("xm_second", weave_xm(second, 1, [1])))
-            if j == 1:
-                v_decayed.append(sbuf([N], F32, "v_decayed1", "xm_second_codes")[:])
-                late = sbuf([2 * PASSES, PACK * P], BF16, "xm_late")
-                make_dw([2, 3], *quantize_xm("xm_late", weave_xm(late, 2, [2, 3])))
-                m_got.append(gather(m_tab[3], "m_got3"))
-            if j == 2:
-                later = sbuf([2, N], F32, "later", "xm_late_codes")
-                v_decayed.extend(later[:, k, :] for k in range(2))
-            if j > 0:
-                nc.scalar.activation(v_decayed[j], v_got[j], ACT.Copy, scale=RHO)
-            nc.scalar.activation(dw_sq[j][:], dw[j][:], ACT.Square, scale=math.sqrt(1.0 - RHO))
-            nc.vector.tensor_tensor(v_win[j][:].indirect(offsets[:]), v_decayed[j], dw_sq[j][:], ALU.add)
+            v_decayed = sbuf([N], F32, "v_decayed%d" % j)
+            nc.scalar.activation(v_decayed[:], listed(v_tab[j]), ACT.Copy, scale=RHO)
+            nc.scalar.activation(nv[:, j, :], dw[j][:], ACT.Square, scale=math.sqrt(1.0 - RHO))
+            nc.gpsimd.tensor_tensor(nv[:, j, :], nv[:, j, :], v_decayed[:], ALU.add)
+        denom = sbuf([D_TILES, N], F32, "denom", "xm2_codes")
+        for pair in (slice(0, 2), slice(2, 4)):
+            nc.scalar.activation(denom[:, pair, :], nv[:, pair, :], ACT.Abs_reciprocal_sqrt, scale=0.25 / EPS ** 2, bias=tiny[:])
+            factor = sbuf([2, N], F32, "factor", "v_decayed3")
+            nc.gpsimd.tensor_scalar(factor[:], denom[:, pair, :], 1.0, 1.0, ALU.mult, ALU.add)
+            nc.gpsimd.tensor_tensor(denom[:, pair, :], factor[:], nv[:, pair, :], ALU.mult)
+        for j in range(D_TILES):
+            if j < V_ON_VECTOR:
+                nc.vector.tensor_copy(listed(v_win[j]), nv[:, j, :])
+            else:
+                scatter_on_scalar(v_win[j], nv[:, j, :], 1.0)
             nc.sync.dma_start(out_2[block(j), :], v_win[j][:])
+        neg_nm = sbuf([D_TILES, N], F32, "neg_nm", "x_raw0")
+        m_got = sbuf([D_TILES, N], F32, "m_got", "weight1")
         for j in range(D_TILES):
-            nc.scalar.copy(dw_sb[:, j, :], dw[j][:])
-            nc.scalar.activation(nm_t[:, j, :], turned_sum(j, m_got[j], dw_sb[:, j, :]), ACT.Copy, scale=-BETA)
-            nc.scalar.copy(nm[:, j, :], turn_back(j, nm_t))
-            nc.vector.tensor_tensor(m_win[j][:].indirect(offsets[:]), nm[:, j, :], minus_one[:], ALU.mult)
-            nc.sync.dma_start(out_1[block(j), :], m_win[j][:])
-        denom_t = sbuf([D_TILES, N], F32, "denom_t", "xm_late")
+            if j >= M_ON_VECTOR:
+                nc.scalar.activation(m_got[:, j, :], listed(m_tab[j]), ACT.Copy)
+            else:
+                nc.vector.tensor_copy(m_got[:, j, :], listed(m_tab[j]))
+            nc.vector.scalar_tensor_tensor(neg_nm[:, j, :], dw[j][:], -1.0, m_got[:, j, :], ALU.mult, ALU.subtract)
+        rate = []
+        for pair in range(2):
+            rates = sbuf([2, N], F32, "rates%d" % pair, "m_tab%d" % (pair + 2))
+            rate.extend(rates[:, k, :] for k in range(2))
         for j in range(D_TILES):
-            nc.scalar.activation(denom_t[:, j, :], turned_sum(j, v_decayed[j], dw_sq[j]), ACT.Sqrt)
-        nc.scalar.activation(denom_t[:], denom_t[:], ACT.Square, bias=eps[:])
+            nc.scalar.activation(rate[j], denom[:, j, :], ACT.Abs_reciprocal_sqrt, scale=1.0 / (LR * BETA) ** 2, bias=eps[:])
         for j in range(D_TILES):
-            nc.scalar.activation(rate[:, j, :], turn_back(j, denom_t), ACT.Abs_reciprocal_sqrt, scale=1.0 / (LR * LR))
-            nc.vector.tensor_tensor(step_win[j][:].indirect(offsets[:]), nm[:, j, :], rate[:, j, :], ALU.mult)
+            nc.vector.tensor_tensor(listed(step_win[j]), neg_nm[:, j, :], rate[j], ALU.mult)
             nc.sync.dma_start(out_0[block(j), :], step_win[j][:])
+            scatter_on_scalar(m_win[j], neg_nm[:, j, :], -BETA)
+            nc.sync.dma_start(out_1[block(j), :], m_win[j][:])

@@ -31,7 +31,7 @@ W_ON_SCALAR = 192
 X_ON_SCALAR = (56, 48)
 HALF = N // 2
 V_ON_VECTOR = 3
-M_ON_VECTOR = 2
+M_ON_VECTOR = 1024
 
 
 def tile_attend_gsqh_adam_kernel(tc, xT, wT, y, wt, xm, mT, vT, offs, out_0, out_1, out_2):
@@ -106,13 +106,12 @@ def tile_attend_gsqh_adam_kernel(tc, xT, wT, y, wt, xm, mT, vT, offs, out_0, out
         load_table(v_tab[0], vT, 0)
         for g in range(PASSES):
             nc.sync.dma_start(xm_raw[g][:], xm[0, pass_rows(g), :].rearrange("(p t) d -> p t d", t=PACK))
-        for j in (1, 2):
-            load_table(v_tab[j], vT, j)
-        load_table(v_win[0], vT, 0)
-        load_table(v_tab[3], vT, 3)
         for j in (1, 2, 3):
-            load_table(v_win[j], vT, j)
+            load_table(v_tab[j], vT, j)
+        load_table(m_tab[0], mT, 0)
         for j in range(D_TILES):
+            load_table(v_win[j], vT, j)
+        for j in (1, 2, 3):
             load_table(m_tab[j], mT, j)
 
         one = keep.tile([P, 1], F32, name="one")
@@ -203,12 +202,13 @@ def tile_attend_gsqh_adam_kernel(tc, xT, wT, y, wt, xm, mT, vT, offs, out_0, out
             for first in range(0, N, HALF):
                 nc.scalar.activation(listed(window, first, first + HALF), values[:, first:first + HALF], ACT.Copy, scale=scale)
 
-        nv = sbuf([D_TILES, N], F32, "nv")
+        v_decayed = [sbuf([N], F32, "v_decayed%d" % j) for j in range(D_TILES)]
         for j in range(D_TILES):
-            v_decayed = sbuf([N], F32, "v_decayed%d" % j)
-            nc.scalar.activation(v_decayed[:], listed(v_tab[j]), ACT.Copy, scale=RHO)
+            nc.scalar.activation(v_decayed[j][:], listed(v_tab[j]), ACT.Copy, scale=RHO)
+        nv = sbuf([D_TILES, N], F32, "nv", "v_tab2")
+        for j in range(D_TILES):
             nc.scalar.activation(nv[:, j, :], dw[j][:], ACT.Square, scale=math.sqrt(1.0 - RHO))
-            nc.gpsimd.tensor_tensor(nv[:, j, :], nv[:, j, :], v_decayed[:], ALU.add)
+            nc.gpsimd.tensor_tensor(nv[:, j, :], nv[:, j, :], v_decayed[j][:], ALU.add)
         denom = sbuf([D_TILES, N], F32, "denom", "xm2_codes")
         for pair in (slice(0, 2), slice(2, 4)):
             nc.scalar.activation(denom[:, pair, :], nv[:, pair, :], ACT.Abs_reciprocal_sqrt, scale=0.25 / EPS ** 2, bias=tiny[:])
@@ -224,10 +224,11 @@ def tile_attend_gsqh_adam_kernel(tc, xT, wT, y, wt, xm, mT, vT, offs, out_0, out
         neg_nm = sbuf([D_TILES, N], F32, "neg_nm", "x_raw0")
         m_got = sbuf([D_TILES, N], F32, "m_got", "weight1")
         for j in range(D_TILES):
-            if j >= M_ON_VECTOR:
-                nc.scalar.activation(m_got[:, j, :], listed(m_tab[j]), ACT.Copy)
-            else:
-                nc.vector.tensor_copy(m_got[:, j, :], listed(m_tab[j]))
+            cut = min(max(M_ON_VECTOR - j * N, 0), N)
+            if cut > 0:
+                nc.vector.tensor_copy(m_got[:, j, :cut], listed(m_tab[j], 0, cut))
+            if cut < N:
+                nc.scalar.activation(m_got[:, j, cut:], listed(m_tab[j], cut, N), ACT.Copy)
             nc.vector.scalar_tensor_tensor(neg_nm[:, j, :], dw[j][:], -1.0, m_got[:, j, :], ALU.mult, ALU.subtract)
         rate = []
         for pair in range(2):

@@ -30,6 +30,7 @@ assert BETA == 1.0 - BETA
 W_ON_SCALAR = 192
 X_ON_SCALAR = (56, 48)
 HALF = N // 2
+WEIGHTS_ON_SCALAR = ((0, 0), (1, 3))
 V_ON_VECTOR = 3
 M_ON_VECTOR = 1024
 
@@ -157,8 +158,11 @@ def tile_attend_gsqh_adam_kernel(tc, xT, wT, y, wt, xm, mT, vT, offs, out_0, out
                 scores = bank("bank_%s%d" % ("ab"[g], t))
                 nc.tensor.matmul_mx(out=scores[:], lhsT=x_q[g][0][:, block(t)].bitcast(E4M3), lhsT_scale=x_q[g][1][:, block(t)],
                                     rhs=w_codes[:].bitcast(E4M3), rhs_scale=w_scales[:], start=True, stop=True)
-                nc.gpsimd.tensor_scalar(weight[g][:, t, :], y_plane(g, t), neg_wt[:, g, t:t + 1], 0.0, ALU.mult, ALU.add)
-                margin = sbuf([N], F32, "margin", "g_woven0")[:] if (g, t) == (PASSES - 1, PACK - 2) else hinge[g][:, t, :]
+                if (g, t) in WEIGHTS_ON_SCALAR:
+                    nc.scalar.activation(weight[g][:, t, :], y_plane(g, t), ACT.Copy, scale=neg_wt[:, g, t:t + 1])
+                else:
+                    nc.gpsimd.tensor_scalar(weight[g][:, t, :], y_plane(g, t), neg_wt[:, g, t:t + 1], 0.0, ALU.mult, ALU.add)
+                margin = sbuf([N], F32, "margin", "g_woven0")[:] if (g, t) == (PASSES - 1, PACK - 3) else hinge[g][:, t, :]
                 nc.vector.tensor_tensor(margin, scores[:], y_plane(g, t), ALU.mult)
                 nc.scalar.activation(hinge[g][:, t, :], margin, ACT.Relu, bias=one[:], scale=-1.0)
         g_woven = []

@@ -30,8 +30,7 @@ assert BETA == 1.0 - BETA
 W_ON_SCALAR = 192
 X_ON_SCALAR = (56, 48)
 HALF = N // 2
-WEIGHTS_ON_SCALAR = ((0, 0), (1, 3))
-V_ON_VECTOR = 3
+WEIGHTS_ON_SCALAR = ((0, 0), (0, 1), (1, 3))
 M_ON_VECTOR = 1024
 
 
@@ -78,6 +77,7 @@ def tile_attend_gsqh_adam_kernel(tc, xT, wT, y, wt, xm, mT, vT, offs, out_0, out
         v_tab = [sbuf([T], F32, "v_tab%d" % j) for j in range(D_TILES)]
         m_tab = [sbuf([T], F32, "m_tab%d" % j) for j in range(D_TILES)]
         v_win = [sbuf([T], F32, "v_win%d" % j) for j in range(D_TILES)]
+        m_win = [sbuf([T], F32, "m_win0")]
         step_win = [sbuf([T], F32, "step_win%d" % j) for j in range(D_TILES)]
         wt_sb = keep.tile([P, PASSES, PACK], F32, name="wt_sb")
 
@@ -112,7 +112,9 @@ def tile_attend_gsqh_adam_kernel(tc, xT, wT, y, wt, xm, mT, vT, offs, out_0, out
         load_table(m_tab[0], mT, 0)
         for j in range(D_TILES):
             load_table(v_win[j], vT, j)
-        for j in (1, 2, 3):
+        load_table(m_tab[1], mT, 1)
+        load_table(m_win[0], mT, 0)
+        for j in (2, 3):
             load_table(m_tab[j], mT, j)
 
         one = keep.tile([P, 1], F32, name="one")
@@ -138,8 +140,8 @@ def tile_attend_gsqh_adam_kernel(tc, xT, wT, y, wt, xm, mT, vT, offs, out_0, out
         w_codes, w_scales = mx_tiles("w", N)
         quantize(w_codes[:], w_scales[:], w_woven[:], E4M3)
 
-        m_win = [sbuf([T], F32, "m_win%d" % j, "w_tab%d" % j) for j in range(D_TILES)]
-        for j in range(D_TILES):
+        for j in range(1, D_TILES):
+            m_win.append(sbuf([T], F32, "m_win%d" % j, "w_tab%d" % j))
             load_table(m_win[j], mT, j)
 
         x_q = []
@@ -220,10 +222,7 @@ def tile_attend_gsqh_adam_kernel(tc, xT, wT, y, wt, xm, mT, vT, offs, out_0, out
             nc.gpsimd.tensor_scalar(factor[:], denom[:, pair, :], 1.0, 1.0, ALU.mult, ALU.add)
             nc.gpsimd.tensor_tensor(denom[:, pair, :], factor[:], nv[:, pair, :], ALU.mult)
         for j in range(D_TILES):
-            if j < V_ON_VECTOR:
-                nc.vector.tensor_copy(listed(v_win[j]), nv[:, j, :])
-            else:
-                scatter_on_scalar(v_win[j], nv[:, j, :], 1.0)
+            nc.vector.tensor_copy(listed(v_win[j]), nv[:, j, :])
             nc.sync.dma_start(out_2[block(j), :], v_win[j][:])
         neg_nm = sbuf([D_TILES, N], F32, "neg_nm", "x_raw0")
         m_got = sbuf([D_TILES, N], F32, "m_got", "weight1")
@@ -241,7 +240,12 @@ def tile_attend_gsqh_adam_kernel(tc, xT, wT, y, wt, xm, mT, vT, offs, out_0, out
         for j in range(D_TILES):
             nc.scalar.activation(rate[j], denom[:, j, :], ACT.Abs_reciprocal_sqrt, scale=1.0 / (LR * BETA) ** 2, bias=eps[:])
         for j in range(D_TILES):
-            nc.vector.tensor_tensor(listed(step_win[j]), neg_nm[:, j, :], rate[j], ALU.mult)
+            if j == 0:
+                step = sbuf([N], F32, "step", "v_decayed3")
+                nc.gpsimd.tensor_tensor(step[:], neg_nm[:, j, :], rate[j], ALU.mult)
+                scatter_on_scalar(step_win[j], step[:], 1.0)
+            else:
+                nc.vector.tensor_tensor(listed(step_win[j]), neg_nm[:, j, :], rate[j], ALU.mult)
             nc.sync.dma_start(out_0[block(j), :], step_win[j][:])
             scatter_on_scalar(m_win[j], neg_nm[:, j, :], -BETA)
             nc.sync.dma_start(out_1[block(j), :], m_win[j][:])

@@ -31,7 +31,7 @@ W_ON_SCALAR = 192
 X_ON_SCALAR = (56, 48)
 HALF = N // 2
 WEIGHTS_ON_SCALAR = ((0, 0), (0, 1), (1, 3))
-M_ON_VECTOR = 1024
+M_ON_VECTOR = 2
 
 
 def tile_attend_gsqh_adam_kernel(tc, xT, wT, y, wt, xm, mT, vT, offs, out_0, out_1, out_2):
@@ -55,8 +55,8 @@ def tile_attend_gsqh_adam_kernel(tc, xT, wT, y, wt, xm, mT, vT, offs, out_0, out
         def quantize(codes, scales, woven, fmt):
             nc.vector.quantize_mx(out=codes.bitcast(fmt), scales=scales, in_=woven)
 
-        def mx_tiles(name, width):
-            return sbuf([width], U32, name + "_codes"), sbuf([width], U8, name + "_scales")
+        def mx_tiles(name, width, place=None):
+            return sbuf([width], U32, name + "_codes", place), sbuf([width], U8, name + "_scales")
 
         def pass_rows(g):
             return slice(g * K_PASS, (g + 1) * K_PASS)
@@ -104,18 +104,18 @@ def tile_attend_gsqh_adam_kernel(tc, xT, wT, y, wt, xm, mT, vT, offs, out_0, out
         for g in range(PASSES):
             load_y(g, 0)
             load_y(g, 1)
-        load_table(v_tab[0], vT, 0)
         for g in range(PASSES):
             nc.sync.dma_start(xm_raw[g][:], xm[0, pass_rows(g), :].rearrange("(p t) d -> p t d", t=PACK))
-        for j in (1, 2, 3):
+        for j in range(D_TILES):
             load_table(v_tab[j], vT, j)
         load_table(m_tab[0], mT, 0)
-        for j in range(D_TILES):
+        load_table(v_win[0], vT, 0)
+        load_table(m_tab[2], mT, 2)
+        for j in range(1, D_TILES):
             load_table(v_win[j], vT, j)
         load_table(m_tab[1], mT, 1)
         load_table(m_win[0], mT, 0)
-        for j in (2, 3):
-            load_table(m_tab[j], mT, j)
+        load_table(m_tab[3], mT, 3)
 
         one = keep.tile([P, 1], F32, name="one")
         nc.vector.memset(one[:], 1.0)
@@ -172,37 +172,41 @@ def tile_attend_gsqh_adam_kernel(tc, xT, wT, y, wt, xm, mT, vT, offs, out_0, out
             g_woven.append(sbuf([PACK * N], BF16, "g_woven%d" % g))
             nc.vector.tensor_tensor(woven_view(g_woven[g][:], 2), planes_view(hinge[g][:], 2), planes_view(weight[g][:], 2), ALU.mult)
 
-        def weave_xm(name, tiles, copies, place=None):
-            woven = sbuf([len(tiles) * PASSES, PACK * P], BF16, name + "_woven", place)
-            for k, j in enumerate(tiles):
-                for g in range(PASSES):
-                    copies[g](woven_view(woven[:, k * PASSES + g, :]), planes_view(xm_raw[g][:, :, block(j)]))
+        def weave_xm(name, pieces, place=None):
+            woven = sbuf([len(pieces), PACK * P], BF16, name + "_woven", place)
+            for k, (j, g) in enumerate(pieces):
+                copy = nc.scalar.copy if j == 0 or g == 0 else nc.vector.tensor_copy
+                copy(woven_view(woven[:, k, :]), planes_view(xm_raw[g][:, :, block(j)]))
             return woven
 
-        def quantize_xm(name, woven):
-            codes, scales = mx_tiles(name, woven.shape[1] * P)
+        xm_q = {}
+
+        def quantize_xm(name, pieces, woven, place=None):
+            codes, scales = mx_tiles(name, len(pieces) * P, place)
             quantize(codes[:], scales[:], woven[:].rearrange("p k c -> p (k c)"), E4M3)
-            return codes, scales
+            for k, piece in enumerate(pieces):
+                xm_q[piece] = (codes[:, block(k)], scales[:, block(k)])
 
         g_q = [mx_tiles("g%d" % g, N) for g in range(PASSES)]
         dw = [bank("bank_a%d" % j) for j in range(D_TILES)]
 
-        def dw_pass(j, g, codes, scales, k):
-            nc.tensor.matmul_mx(out=dw[j][:], lhsT=codes[:, block(k)].bitcast(E4M3), lhsT_scale=scales[:, block(k)],
+        def dw_pass(j, g):
+            nc.tensor.matmul_mx(out=dw[j][:], lhsT=xm_q[j, g][0].bitcast(E4M3), lhsT_scale=xm_q[j, g][1],
                                 rhs=g_q[g][0][:].bitcast(E5M2), rhs_scale=g_q[g][1][:],
                                 start=(g == 0), stop=(g == PASSES - 1))
 
-        xm_woven = weave_xm("xm0", [0], (nc.scalar.copy, nc.scalar.copy))
+        first, middle, last = [(0, 0), (0, 1)], [(1, 0), (2, 0), (3, 0), (1, 1)], [(2, 1), (3, 1)]
+        xm_woven = weave_xm("xm0", first)
         quantize(g_q[0][0][:], g_q[0][1][:], g_woven[0][:], E5M2)
-        xm_q = quantize_xm("xm0", xm_woven)
-        dw_pass(0, 0, *xm_q, 0)
+        quantize_xm("xm0", first, xm_woven)
+        dw_pass(0, 0)
         quantize(g_q[1][0][:], g_q[1][1][:], g_woven[1][:], E5M2)
-        dw_pass(0, 1, *xm_q, 1)
-        for name, tiles, copy, place in (("xm1", [1], nc.scalar.copy, None), ("xm2", [2, 3], nc.vector.tensor_copy, "g_woven1")):
-            xm_q = quantize_xm(name, weave_xm(name, tiles, (copy, copy), place))
-            for k, j in enumerate(tiles):
-                for g in range(PASSES):
-                    dw_pass(j, g, *xm_q, k * PASSES + g)
+        dw_pass(0, 1)
+        quantize_xm("xm1", middle, weave_xm("xm1", middle), "xm0_woven")
+        quantize_xm("xm2", last, weave_xm("xm2", last, "g_woven1"))
+        for j in range(1, D_TILES):
+            for g in range(PASSES):
+                dw_pass(j, g)
 
         def scatter_on_scalar(window, values, scale):
             for first in range(0, N, HALF):
@@ -215,37 +219,38 @@ def tile_attend_gsqh_adam_kernel(tc, xT, wT, y, wt, xm, mT, vT, offs, out_0, out
         for j in range(D_TILES):
             nc.scalar.activation(nv[:, j, :], dw[j][:], ACT.Square, scale=math.sqrt(1.0 - RHO))
             nc.gpsimd.tensor_tensor(nv[:, j, :], nv[:, j, :], v_decayed[j][:], ALU.add)
-        denom = sbuf([D_TILES, N], F32, "denom", "xm2_codes")
-        for pair in (slice(0, 2), slice(2, 4)):
-            nc.scalar.activation(denom[:, pair, :], nv[:, pair, :], ACT.Abs_reciprocal_sqrt, scale=0.25 / EPS ** 2, bias=tiny[:])
+        m_got = sbuf([D_TILES, N], F32, "m_got", "weight1")
+        for j in range(D_TILES):
+            if j < M_ON_VECTOR:
+                nc.vector.tensor_copy(m_got[:, j, :], listed(m_tab[j]))
+            else:
+                nc.scalar.activation(m_got[:, j, :], listed(m_tab[j]), ACT.Copy)
+        denom = []
+        for pair, place in ((slice(0, 2), "xm2_codes"), (slice(2, 4), "m_tab2")):
+            squared = sbuf([2, N], F32, "denom%d" % pair.start, place)
+            nc.scalar.activation(squared[:], nv[:, pair, :], ACT.Abs_reciprocal_sqrt, scale=0.25 / EPS ** 2, bias=tiny[:])
             factor = sbuf([2, N], F32, "factor", "v_decayed3")
-            nc.gpsimd.tensor_scalar(factor[:], denom[:, pair, :], 1.0, 1.0, ALU.mult, ALU.add)
-            nc.gpsimd.tensor_tensor(denom[:, pair, :], factor[:], nv[:, pair, :], ALU.mult)
+            nc.gpsimd.tensor_scalar(factor[:], squared[:], 1.0, 1.0, ALU.mult, ALU.add)
+            nc.gpsimd.tensor_tensor(squared[:], factor[:], nv[:, pair, :], ALU.mult)
+            denom.extend(squared[:, k, :] for k in range(2))
         for j in range(D_TILES):
             nc.vector.tensor_copy(listed(v_win[j]), nv[:, j, :])
             nc.sync.dma_start(out_2[block(j), :], v_win[j][:])
-        neg_nm = sbuf([D_TILES, N], F32, "neg_nm", "x_raw0")
-        m_got = sbuf([D_TILES, N], F32, "m_got", "weight1")
+        later_nm = sbuf([D_TILES - 1, N], F32, "later_nm", "m_tab1")
+        neg_nm = [sbuf([N], F32, "first_nm", "x_raw0")[:]] + [later_nm[:, k, :] for k in range(D_TILES - 1)]
         for j in range(D_TILES):
-            cut = min(max(M_ON_VECTOR - j * N, 0), N)
-            if cut > 0:
-                nc.vector.tensor_copy(m_got[:, j, :cut], listed(m_tab[j], 0, cut))
-            if cut < N:
-                nc.scalar.activation(m_got[:, j, cut:], listed(m_tab[j], cut, N), ACT.Copy)
-            nc.vector.scalar_tensor_tensor(neg_nm[:, j, :], dw[j][:], -1.0, m_got[:, j, :], ALU.mult, ALU.subtract)
-        rate = []
-        for pair in range(2):
-            rates = sbuf([2, N], F32, "rates%d" % pair, "m_tab%d" % (pair + 2))
-            rate.extend(rates[:, k, :] for k in range(2))
+            nc.vector.scalar_tensor_tensor(neg_nm[j], dw[j][:], -1.0, m_got[:, j, :], ALU.mult, ALU.subtract)
+        rates = sbuf([D_TILES, N], F32, "rates", "m_tab3")
+        rate = [rates[:, j, :] for j in range(D_TILES)]
         for j in range(D_TILES):
-            nc.scalar.activation(rate[j], denom[:, j, :], ACT.Abs_reciprocal_sqrt, scale=1.0 / (LR * BETA) ** 2, bias=eps[:])
+            nc.scalar.activation(rate[j], denom[j], ACT.Abs_reciprocal_sqrt, scale=1.0 / (LR * BETA) ** 2, bias=eps[:])
         for j in range(D_TILES):
             if j == 0:
                 step = sbuf([N], F32, "step", "v_decayed3")
-                nc.gpsimd.tensor_tensor(step[:], neg_nm[:, j, :], rate[j], ALU.mult)
+                nc.gpsimd.tensor_tensor(step[:], neg_nm[j], rate[j], ALU.mult)
                 scatter_on_scalar(step_win[j], step[:], 1.0)
             else:
-                nc.vector.tensor_tensor(listed(step_win[j]), neg_nm[:, j, :], rate[j], ALU.mult)
+                nc.vector.tensor_tensor(listed(step_win[j]), neg_nm[j], rate[j], ALU.mult)
             nc.sync.dma_start(out_0[block(j), :], step_win[j][:])
-            scatter_on_scalar(m_win[j], neg_nm[:, j, :], -BETA)
+            scatter_on_scalar(m_win[j], neg_nm[j], -BETA)
             nc.sync.dma_start(out_1[block(j), :], m_win[j][:])

@@ -29,7 +29,7 @@ assert BETA == 1.0 - BETA
 
 W_ON_SCALAR = 192
 X_ON_SCALAR = (56, 48)
-HALF = N // 2
+SHORT = 128
 WEIGHTS_ON_SCALAR = ((0, 0), (0, 1), (1, 3))
 M_ON_VECTOR = 2
 
@@ -111,9 +111,10 @@ def tile_attend_gsqh_adam_kernel(tc, xT, wT, y, wt, xm, mT, vT, offs, out_0, out
         load_table(m_tab[0], mT, 0)
         load_table(v_win[0], vT, 0)
         load_table(m_tab[2], mT, 2)
-        for j in range(1, D_TILES):
+        for j in (1, 2):
             load_table(v_win[j], vT, j)
         load_table(m_tab[1], mT, 1)
+        load_table(v_win[3], vT, 3)
         load_table(m_win[0], mT, 0)
         load_table(m_tab[3], mT, 3)
 
@@ -209,8 +210,8 @@ def tile_attend_gsqh_adam_kernel(tc, xT, wT, y, wt, xm, mT, vT, offs, out_0, out
                 dw_pass(j, g)
 
         def scatter_on_scalar(window, values, scale):
-            for first in range(0, N, HALF):
-                nc.scalar.activation(listed(window, first, first + HALF), values[:, first:first + HALF], ACT.Copy, scale=scale)
+            for first, last in ((0, SHORT), (SHORT, N)):
+                nc.scalar.activation(listed(window, first, last), values[:, first:last], ACT.Copy, scale=scale)
 
         v_decayed = [sbuf([N], F32, "v_decayed%d" % j) for j in range(D_TILES)]
         for j in range(D_TILES):

@@ -31,7 +31,7 @@ W_ON_SCALAR = 192
 X_ON_SCALAR = (56, 48)
 SHORT = 128
 WEIGHTS_ON_SCALAR = ((0, 0), (0, 1), (1, 3))
-M_ON_VECTOR = 2
+M_ON_VECTOR = 768
 
 
 def tile_attend_gsqh_adam_kernel(tc, xT, wT, y, wt, xm, mT, vT, offs, out_0, out_1, out_2):
@@ -77,7 +77,6 @@ def tile_attend_gsqh_adam_kernel(tc, xT, wT, y, wt, xm, mT, vT, offs, out_0, out
         v_tab = [sbuf([T], F32, "v_tab%d" % j) for j in range(D_TILES)]
         m_tab = [sbuf([T], F32, "m_tab%d" % j) for j in range(D_TILES)]
         v_win = [sbuf([T], F32, "v_win%d" % j) for j in range(D_TILES)]
-        m_win = [sbuf([T], F32, "m_win0")]
         step_win = [sbuf([T], F32, "step_win%d" % j) for j in range(D_TILES)]
         wt_sb = keep.tile([P, PASSES, PACK], F32, name="wt_sb")
 
@@ -111,12 +110,10 @@ def tile_attend_gsqh_adam_kernel(tc, xT, wT, y, wt, xm, mT, vT, offs, out_0, out
         load_table(m_tab[0], mT, 0)
         load_table(v_win[0], vT, 0)
         load_table(m_tab[2], mT, 2)
-        for j in (1, 2):
+        for j in range(1, D_TILES):
             load_table(v_win[j], vT, j)
-        load_table(m_tab[1], mT, 1)
-        load_table(v_win[3], vT, 3)
-        load_table(m_win[0], mT, 0)
-        load_table(m_tab[3], mT, 3)
+        for j in (1, 3):
+            load_table(m_tab[j], mT, j)
 
         one = keep.tile([P, 1], F32, name="one")
         nc.vector.memset(one[:], 1.0)
@@ -141,8 +138,8 @@ def tile_attend_gsqh_adam_kernel(tc, xT, wT, y, wt, xm, mT, vT, offs, out_0, out
         w_codes, w_scales = mx_tiles("w", N)
         quantize(w_codes[:], w_scales[:], w_woven[:], E4M3)
 
-        for j in range(1, D_TILES):
-            m_win.append(sbuf([T], F32, "m_win%d" % j, "w_tab%d" % j))
+        m_win = [sbuf([T], F32, "m_win%d" % j, "w_tab%d" % j) for j in range(D_TILES)]
+        for j in range(D_TILES):
             load_table(m_win[j], mT, j)
 
         x_q = []
@@ -222,10 +219,11 @@ def tile_attend_gsqh_adam_kernel(tc, xT, wT, y, wt, xm, mT, vT, offs, out_0, out
             nc.gpsimd.tensor_tensor(nv[:, j, :], nv[:, j, :], v_decayed[j][:], ALU.add)
         m_got = sbuf([D_TILES, N], F32, "m_got", "weight1")
         for j in range(D_TILES):
-            if j < M_ON_VECTOR:
-                nc.vector.tensor_copy(m_got[:, j, :], listed(m_tab[j]))
-            else:
-                nc.scalar.activation(m_got[:, j, :], listed(m_tab[j]), ACT.Copy)
+            cut = min(max(M_ON_VECTOR - j * N, 0), N)
+            if cut > 0:
+                nc.vector.tensor_copy(m_got[:, j, :cut], listed(m_tab[j], 0, cut))
+            if cut < N:
+                nc.scalar.activation(m_got[:, j, cut:], listed(m_tab[j], cut, N), ACT.Copy)
         denom = []
         for pair, place in ((slice(0, 2), "xm2_codes"), (slice(2, 4), "m_tab2")):
             squared = sbuf([2, N], F32, "denom%d" % pair.start, place)
@@ -235,7 +233,11 @@ def tile_attend_gsqh_adam_kernel(tc, xT, wT, y, wt, xm, mT, vT, offs, out_0, out
             nc.gpsimd.tensor_tensor(squared[:], factor[:], nv[:, pair, :], ALU.mult)
             denom.extend(squared[:, k, :] for k in range(2))
         for j in range(D_TILES):
-            nc.vector.tensor_copy(listed(v_win[j]), nv[:, j, :])
+            if j < D_TILES - 1:
+                nc.vector.tensor_copy(listed(v_win[j]), nv[:, j, :])
+            else:
+                nc.scalar.activation(listed(v_win[j], SHORT, N), nv[:, j, SHORT:], ACT.Copy)
+                nc.vector.tensor_copy(listed(v_win[j], 0, SHORT), nv[:, j, :SHORT])
             nc.sync.dma_start(out_2[block(j), :], v_win[j][:])
         later_nm = sbuf([D_TILES - 1, N], F32, "later_nm", "m_tab1")
         neg_nm = [sbuf([N], F32, "first_nm", "x_raw0")[:]] + [later_nm[:, k, :] for k in range(D_TILES - 1)]
@@ -246,12 +248,7 @@ def tile_attend_gsqh_adam_kernel(tc, xT, wT, y, wt, xm, mT, vT, offs, out_0, out
         for j in range(D_TILES):
             nc.scalar.activation(rate[j], denom[j], ACT.Abs_reciprocal_sqrt, scale=1.0 / (LR * BETA) ** 2, bias=eps[:])
         for j in range(D_TILES):
-            if j == 0:
-                step = sbuf([N], F32, "step", "v_decayed3")
-                nc.gpsimd.tensor_tensor(step[:], neg_nm[j], rate[j], ALU.mult)
-                scatter_on_scalar(step_win[j], step[:], 1.0)
-            else:
-                nc.vector.tensor_tensor(listed(step_win[j]), neg_nm[j], rate[j], ALU.mult)
+            nc.vector.tensor_tensor(listed(step_win[j]), neg_nm[j], rate[j], ALU.mult)
             nc.sync.dma_start(out_0[block(j), :], step_win[j][:])
             scatter_on_scalar(m_win[j], neg_nm[j], -BETA)
             nc.sync.dma_start(out_1[block(j), :], m_win[j][:])

@@ -31,7 +31,7 @@ W_ON_SCALAR = 192
 X_ON_SCALAR = (56, 48)
 SHORT = 128
 WEIGHTS_ON_SCALAR = ((0, 0), (0, 1), (1, 3))
-M_ON_VECTOR = 768
+M_ON_VECTOR = 672
 
 
 def tile_attend_gsqh_adam_kernel(tc, xT, wT, y, wt, xm, mT, vT, offs, out_0, out_1, out_2):

@@ -31,7 +31,7 @@ W_ON_SCALAR = 192
 X_ON_SCALAR = (56, 48)
 SHORT = 128
 WEIGHTS_ON_SCALAR = ((0, 0), (0, 1), (1, 3))
-M_ON_VECTOR = 672
+M_ON_VECTOR = 512
 
 
 def tile_attend_gsqh_adam_kernel(tc, xT, wT, y, wt, xm, mT, vT, offs, out_0, out_1, out_2):
@@ -119,10 +119,10 @@ def tile_attend_gsqh_adam_kernel(tc, xT, wT, y, wt, xm, mT, vT, offs, out_0, out
         nc.vector.memset(one[:], 1.0)
         for j in range(D_TILES):
             nc.gpsimd.memset(step_win[j][:], 0.0)
+        tiny = keep.tile([P, 1], F32, name="tiny")
+        nc.scalar.activation(tiny[:], one[:], ACT.Abs_reciprocal_sqrt, scale=1e28)
         eps = keep.tile([P, 1], F32, name="eps")
         nc.scalar.activation(eps[:], one[:], ACT.Copy, scale=(EPS / (LR * BETA)) ** 2)
-        tiny = keep.tile([P, 1], F32, name="tiny")
-        nc.scalar.activation(tiny[:], one[:], ACT.Copy, scale=1e-24)
         neg_wt = keep.tile([P, PASSES, PACK], F32, name="neg_wt")
         nc.scalar.activation(neg_wt[:], wt_sb[:], ACT.Copy, scale=-1.0)
 

@@ -213,7 +213,7 @@ def tile_attend_gsqh_adam_kernel(tc, xT, wT, y, wt, xm, mT, vT, offs, out_0, out
         v_decayed = [sbuf([N], F32, "v_decayed%d" % j) for j in range(D_TILES)]
         for j in range(D_TILES):
             nc.scalar.activation(v_decayed[j][:], listed(v_tab[j]), ACT.Copy, scale=RHO)
-        nv = sbuf([D_TILES, N], F32, "nv", "v_tab2")
+        nv = sbuf([D_TILES, N], F32, "nv", "v_tab1")
         for j in range(D_TILES):
             nc.scalar.activation(nv[:, j, :], dw[j][:], ACT.Square, scale=math.sqrt(1.0 - RHO))
             nc.gpsimd.tensor_tensor(nv[:, j, :], nv[:, j, :], v_decayed[j][:], ALU.add)
@@ -230,7 +230,11 @@ def tile_attend_gsqh_adam_kernel(tc, xT, wT, y, wt, xm, mT, vT, offs, out_0, out
             nc.scalar.activation(squared[:], nv[:, pair, :], ACT.Abs_reciprocal_sqrt, scale=0.25 / EPS ** 2, bias=tiny[:])
             factor = sbuf([2, N], F32, "factor", "v_decayed3")
             nc.gpsimd.tensor_scalar(factor[:], squared[:], 1.0, 1.0, ALU.mult, ALU.add)
-            nc.gpsimd.tensor_tensor(squared[:], factor[:], nv[:, pair, :], ALU.mult)
+            if pair.start == 0:
+                nc.gpsimd.tensor_tensor(squared[:], factor[:], nv[:, pair, :], ALU.mult)
+            else:
+                for k in range(2):
+                    nc.gpsimd.tensor_tensor(squared[:, k, :], factor[:, k, :], nv[:, pair.start + k, :], ALU.mult)
             denom.extend(squared[:, k, :] for k in range(2))
         for j in range(D_TILES):
             if j < D_TILES - 1:

@@ -31,7 +31,7 @@ W_ON_SCALAR = 192
 X_ON_SCALAR = (56, 48)
 SHORT = 128
 WEIGHTS_ON_SCALAR = ((0, 0), (0, 1), (1, 3))
-M_ON_VECTOR = 512
+M_ON_VECTOR = 384
 
 
 def tile_attend_gsqh_adam_kernel(tc, xT, wT, y, wt, xm, mT, vT, offs, out_0, out_1, out_2):
@@ -112,8 +112,6 @@ def tile_attend_gsqh_adam_kernel(tc, xT, wT, y, wt, xm, mT, vT, offs, out_0, out
         load_table(m_tab[2], mT, 2)
         for j in range(1, D_TILES):
             load_table(v_win[j], vT, j)
-        for j in (1, 3):
-            load_table(m_tab[j], mT, j)
 
         one = keep.tile([P, 1], F32, name="one")
         nc.vector.memset(one[:], 1.0)
@@ -140,6 +138,9 @@ def tile_attend_gsqh_adam_kernel(tc, xT, wT, y, wt, xm, mT, vT, offs, out_0, out
 
         m_win = [sbuf([T], F32, "m_win%d" % j, "w_tab%d" % j) for j in range(D_TILES)]
         for j in range(D_TILES):
+            if j == 2:
+                load_table(m_tab[1], mT, 1)
+                load_table(m_tab[3], mT, 3)
             load_table(m_win[j], mT, j)
 
         x_q = []
@@ -172,9 +173,13 @@ def tile_attend_gsqh_adam_kernel(tc, xT, wT, y, wt, xm, mT, vT, offs, out_0, out
 
         def weave_xm(name, pieces, place=None):
             woven = sbuf([len(pieces), PACK * P], BF16, name + "_woven", place)
-            for k, (j, g) in enumerate(pieces):
-                copy = nc.scalar.copy if j == 0 or g == 0 else nc.vector.tensor_copy
-                copy(woven_view(woven[:, k, :]), planes_view(xm_raw[g][:, :, block(j)]))
+            for g in range(PASSES):
+                ks = [k for k, piece in enumerate(pieces) if piece[1] == g]
+                if ks:
+                    j = pieces[ks[0]][0]
+                    copy = nc.scalar.copy if j == 0 or g == 0 else nc.vector.tensor_copy
+                    copy(woven_view(woven[:, ks[0]:ks[-1] + 1, :].rearrange("p k c -> p (k c)")),
+                         planes_view(xm_raw[g][:, :, j * P:(j + len(ks)) * P]))
             return woven
 
         xm_q = {}
@@ -206,53 +211,51 @@ def tile_attend_gsqh_adam_kernel(tc, xT, wT, y, wt, xm, mT, vT, offs, out_0, out
             for g in range(PASSES):
                 dw_pass(j, g)
 
-        def scatter_on_scalar(window, values, scale):
+        def scatter_on_scalar(tiles):
             for first, last in ((0, SHORT), (SHORT, N)):
-                nc.scalar.activation(listed(window, first, last), values[:, first:last], ACT.Copy, scale=scale)
+                for j in tiles:
+                    nc.scalar.activation(listed(m_win[j], first, last), neg_nm[:, j, first:last], ACT.Copy, scale=-BETA)
 
         v_decayed = [sbuf([N], F32, "v_decayed%d" % j) for j in range(D_TILES)]
         for j in range(D_TILES):
             nc.scalar.activation(v_decayed[j][:], listed(v_tab[j]), ACT.Copy, scale=RHO)
-        nv = sbuf([D_TILES, N], F32, "nv", "v_tab1")
-        for j in range(D_TILES):
-            nc.scalar.activation(nv[:, j, :], dw[j][:], ACT.Square, scale=math.sqrt(1.0 - RHO))
-            nc.gpsimd.tensor_tensor(nv[:, j, :], nv[:, j, :], v_decayed[j][:], ALU.add)
         m_got = sbuf([D_TILES, N], F32, "m_got", "weight1")
         for j in range(D_TILES):
-            cut = min(max(M_ON_VECTOR - j * N, 0), N)
-            if cut > 0:
+            cut = M_ON_VECTOR if j == 0 else 0
+            if cut:
                 nc.vector.tensor_copy(m_got[:, j, :cut], listed(m_tab[j], 0, cut))
-            if cut < N:
-                nc.scalar.activation(m_got[:, j, cut:], listed(m_tab[j], cut, N), ACT.Copy)
+            nc.scalar.activation(m_got[:, j, cut:], listed(m_tab[j], cut, N), ACT.Copy)
+        nv = sbuf([2, 2, N], F32, "nv", "v_tab1")
+        for j in range(D_TILES):
+            nv_j = nv[:, j // 2, j % 2, :]
+            nc.scalar.activation(nv_j, dw[j][:], ACT.Square, scale=math.sqrt(1.0 - RHO))
+            nc.gpsimd.tensor_tensor(nv_j, nv_j, v_decayed[j][:], ALU.add)
         denom = []
-        for pair, place in ((slice(0, 2), "xm2_codes"), (slice(2, 4), "m_tab2")):
-            squared = sbuf([2, N], F32, "denom%d" % pair.start, place)
-            nc.scalar.activation(squared[:], nv[:, pair, :], ACT.Abs_reciprocal_sqrt, scale=0.25 / EPS ** 2, bias=tiny[:])
+        for pair, place in ((0, "xm2_codes"), (1, "m_tab2")):
+            squared = sbuf([2, N], F32, "denom%d" % pair, place)
+            nc.scalar.activation(squared[:], nv[:, pair], ACT.Abs_reciprocal_sqrt, scale=0.25 / EPS ** 2, bias=tiny[:])
             factor = sbuf([2, N], F32, "factor", "v_decayed3")
             nc.gpsimd.tensor_scalar(factor[:], squared[:], 1.0, 1.0, ALU.mult, ALU.add)
-            if pair.start == 0:
-                nc.gpsimd.tensor_tensor(squared[:], factor[:], nv[:, pair, :], ALU.mult)
-            else:
-                for k in range(2):
-                    nc.gpsimd.tensor_tensor(squared[:, k, :], factor[:, k, :], nv[:, pair.start + k, :], ALU.mult)
-            denom.extend(squared[:, k, :] for k in range(2))
+            nc.gpsimd.tensor_tensor(squared[:], factor[:], nv[:, pair], ALU.mult)
+            denom.append(squared)
         for j in range(D_TILES):
+            nv_j = nv[:, j // 2, j % 2, :]
             if j < D_TILES - 1:
-                nc.vector.tensor_copy(listed(v_win[j]), nv[:, j, :])
+                nc.vector.tensor_copy(listed(v_win[j]), nv_j)
             else:
-                nc.scalar.activation(listed(v_win[j], SHORT, N), nv[:, j, SHORT:], ACT.Copy)
-                nc.vector.tensor_copy(listed(v_win[j], 0, SHORT), nv[:, j, :SHORT])
+                nc.scalar.activation(listed(v_win[j], SHORT, N), nv_j[:, SHORT:], ACT.Copy)
+                nc.vector.tensor_copy(listed(v_win[j], 0, SHORT), nv_j[:, :SHORT])
             nc.sync.dma_start(out_2[block(j), :], v_win[j][:])
-        later_nm = sbuf([D_TILES - 1, N], F32, "later_nm", "m_tab1")
-        neg_nm = [sbuf([N], F32, "first_nm", "x_raw0")[:]] + [later_nm[:, k, :] for k in range(D_TILES - 1)]
+        held = sbuf([D_TILES + 2, N], F32, "held", "m_tab1")
+        neg_nm, rate = held[:, :D_TILES, :], [held[:, D_TILES:, :], sbuf([2, N], F32, "rate23", "m_tab3")[:]]
         for j in range(D_TILES):
-            nc.vector.scalar_tensor_tensor(neg_nm[j], dw[j][:], -1.0, m_got[:, j, :], ALU.mult, ALU.subtract)
-        rates = sbuf([D_TILES, N], F32, "rates", "m_tab3")
-        rate = [rates[:, j, :] for j in range(D_TILES)]
-        for j in range(D_TILES):
-            nc.scalar.activation(rate[j], denom[j], ACT.Abs_reciprocal_sqrt, scale=1.0 / (LR * BETA) ** 2, bias=eps[:])
-        for j in range(D_TILES):
-            nc.vector.tensor_tensor(listed(step_win[j]), neg_nm[j], rate[j], ALU.mult)
-            nc.sync.dma_start(out_0[block(j), :], step_win[j][:])
-            scatter_on_scalar(m_win[j], neg_nm[j], -BETA)
-            nc.sync.dma_start(out_1[block(j), :], m_win[j][:])
+            nc.vector.scalar_tensor_tensor(neg_nm[:, j, :], dw[j][:], -1.0, m_got[:, j, :], ALU.mult, ALU.subtract)
+        for pair in range(2):
+            tiles = range(2 * pair, 2 * pair + 2)
+            nc.scalar.activation(rate[pair], denom[pair][:], ACT.Abs_reciprocal_sqrt,
+                                 scale=1.0 / (LR * BETA) ** 2, bias=eps[:])
+            scatter_on_scalar(tiles)
+            for j in tiles:
+                nc.vector.tensor_tensor(listed(step_win[j]), neg_nm[:, j, :], rate[pair][:, j % 2, :], ALU.mult)
+                nc.sync.dma_start(out_0[block(j), :], step_win[j][:])
+                nc.sync.dma_start(out_1[block(j), :], m_win[j][:])

@@ -28,10 +28,10 @@ assert D == K_PASS and N == K_PASS and PASSES == 2
 assert BETA == 1.0 - BETA
 
 W_ON_SCALAR = 192
-X_ON_SCALAR = (56, 48)
+X_ON_SCALAR = (56, 40, 20)
 SHORT = 128
 WEIGHTS_ON_SCALAR = ((0, 0), (0, 1), (1, 3))
-M_ON_VECTOR = 384
+M_ON_VECTOR = 512
 
 
 def tile_attend_gsqh_adam_kernel(tc, xT, wT, y, wt, xm, mT, vT, offs, out_0, out_1, out_2):
@@ -71,7 +71,8 @@ def tile_attend_gsqh_adam_kernel(tc, xT, wT, y, wt, xm, mT, vT, offs, out_0, out
 
         w_planes = wT.rearrange("(p t) c -> t p c", t=PACK)
         w_tab = [sbuf([T], F32, "w_tab%d" % t) for t in range(PACK)]
-        x_raw = [sbuf([PACK, K_PASS], F32, "x_raw%d" % g) for g in range(PASSES)]
+        x_parts = ((0, 0, P), (1, 0, P // 2), (1, P // 2, P))
+        x_raw = [sbuf([PACK, PACK * (last - first)], F32, "x_raw%d" % k) for k, (g, first, last) in enumerate(x_parts)]
         y_raw = [[sbuf([2, N], F32, "y_raw%d_%d" % (g, pair)) for pair in range(2)] for g in range(PASSES)]
         xm_raw = [sbuf([PACK, D], F32, "xm_raw%d" % g) for g in range(PASSES)]
         v_tab = [sbuf([T], F32, "v_tab%d" % j) for j in range(D_TILES)]
@@ -80,8 +81,10 @@ def tile_attend_gsqh_adam_kernel(tc, xT, wT, y, wt, xm, mT, vT, offs, out_0, out
         step_win = [sbuf([T], F32, "step_win%d" % j) for j in range(D_TILES)]
         wt_sb = keep.tile([P, PASSES, PACK], F32, name="wt_sb")
 
-        def load_x(g):
-            nc.sync.dma_start(x_raw[g][:], xT[0, :, pass_rows(g)].rearrange("(p j) r -> p j r", j=PACK))
+        def load_x(k):
+            g, first, last = x_parts[k]
+            rows = slice(g * K_PASS + PACK * first, g * K_PASS + PACK * last)
+            nc.sync.dma_start(x_raw[k][:], xT[0, :, rows].rearrange("(p j) r -> p j r", j=PACK))
 
         def load_y(g, pair):
             src = y[0, pass_rows(g), :].rearrange("(p t) n -> p t n", t=PACK)
@@ -98,8 +101,8 @@ def tile_attend_gsqh_adam_kernel(tc, xT, wT, y, wt, xm, mT, vT, offs, out_0, out
         nc.sync.dma_start(offsets[:], offs)
         for t in range(1, PACK):
             nc.sync.dma_start(w_tab[t][:], w_planes[t])
-        for g in range(PASSES):
-            load_x(g)
+        for k in range(len(x_parts)):
+            load_x(k)
         for g in range(PASSES):
             load_y(g, 0)
             load_y(g, 1)
@@ -147,9 +150,12 @@ def tile_attend_gsqh_adam_kernel(tc, xT, wT, y, wt, xm, mT, vT, offs, out_0, out
         for g in range(PASSES):
             x_woven = sbuf([PACK * K_PASS], BF16, "x_woven%d" % g)
             dst = x_woven[:].rearrange("p (t s j) -> p s j t", t=PACK, j=PACK)
-            src = x_raw[g][:].rearrange("p j (s t) -> p s j t", t=PACK)
-            nc.scalar.copy(dst[:, :X_ON_SCALAR[g]], src[:, :X_ON_SCALAR[g]])
-            nc.vector.tensor_copy(dst[:, X_ON_SCALAR[g]:], src[:, X_ON_SCALAR[g]:])
+            for k, (part_pass, first, last) in enumerate(x_parts):
+                if part_pass == g:
+                    src = x_raw[k][:].rearrange("p j (s t) -> p s j t", t=PACK)
+                    cut = X_ON_SCALAR[k]
+                    nc.scalar.copy(dst[:, first:first + cut], src[:, :cut])
+                    nc.vector.tensor_copy(dst[:, first + cut:last], src[:, cut:])
             x_q.append(mx_tiles("x%d" % g, K_PASS))
             quantize(x_q[g][0][:], x_q[g][1][:], x_woven[:], E4M3)
         hinge = [sbuf([PACK, N], F32, "hinge0"), sbuf([PACK, N], F32, "hinge1", "w_got")]
@@ -163,12 +169,12 @@ def tile_attend_gsqh_adam_kernel(tc, xT, wT, y, wt, xm, mT, vT, offs, out_0, out
                     nc.scalar.activation(weight[g][:, t, :], y_plane(g, t), ACT.Copy, scale=neg_wt[:, g, t:t + 1])
                 else:
                     nc.gpsimd.tensor_scalar(weight[g][:, t, :], y_plane(g, t), neg_wt[:, g, t:t + 1], 0.0, ALU.mult, ALU.add)
-                margin = sbuf([N], F32, "margin", "g_woven0")[:] if (g, t) == (PASSES - 1, PACK - 3) else hinge[g][:, t, :]
+                margin = hinge[g][:, t, :]
                 nc.vector.tensor_tensor(margin, scores[:], y_plane(g, t), ALU.mult)
                 nc.scalar.activation(hinge[g][:, t, :], margin, ACT.Relu, bias=one[:], scale=-1.0)
         g_woven = []
         for g in range(PASSES):
-            g_woven.append(sbuf([PACK * N], BF16, "g_woven%d" % g))
+            g_woven.append(sbuf([PACK * N], BF16, "g_woven%d" % g, ("y_raw1_1", None)[g]))
             nc.vector.tensor_tensor(woven_view(g_woven[g][:], 2), planes_view(hinge[g][:], 2), planes_view(weight[g][:], 2), ALU.mult)
 
         def weave_xm(name, pieces, place=None):
@@ -177,7 +183,7 @@ def tile_attend_gsqh_adam_kernel(tc, xT, wT, y, wt, xm, mT, vT, offs, out_0, out
                 ks = [k for k, piece in enumerate(pieces) if piece[1] == g]
                 if ks:
                     j = pieces[ks[0]][0]
-                    copy = nc.scalar.copy if j == 0 or g == 0 else nc.vector.tensor_copy
+                    copy = nc.scalar.copy if j <= 1 else nc.vector.tensor_copy
                     copy(woven_view(woven[:, ks[0]:ks[-1] + 1, :].rearrange("p k c -> p (k c)")),
                          planes_view(xm_raw[g][:, :, j * P:(j + len(ks)) * P]))
             return woven
@@ -224,7 +230,8 @@ def tile_attend_gsqh_adam_kernel(tc, xT, wT, y, wt, xm, mT, vT, offs, out_0, out
             cut = M_ON_VECTOR if j == 0 else 0
             if cut:
                 nc.vector.tensor_copy(m_got[:, j, :cut], listed(m_tab[j], 0, cut))
-            nc.scalar.activation(m_got[:, j, cut:], listed(m_tab[j], cut, N), ACT.Copy)
+            if cut < N:
+                nc.scalar.activation(m_got[:, j, cut:], listed(m_tab[j], cut, N), ACT.Copy)
         nv = sbuf([2, 2, N], F32, "nv", "v_tab1")
         for j in range(D_TILES):
             nv_j = nv[:, j // 2, j % 2, :]

@@ -73,39 +73,41 @@ def tile_attend_gsqh_adam_kernel(tc, xT, wT, y, wt, xm, mT, vT, offs, out_0, out
         w_tab = [sbuf([T], F32, "w_tab%d" % t) for t in range(PACK)]
         x_parts = ((0, 0, P), (1, 0, P // 2), (1, P // 2, P))
         x_raw = [sbuf([PACK, PACK * (last - first)], F32, "x_raw%d" % k) for k, (g, first, last) in enumerate(x_parts)]
-        y_raw = [[sbuf([2, N], F32, "y_raw%d_%d" % (g, pair)) for pair in range(2)] for g in range(PASSES)]
+        y_parts = ((0, 0, 2), (0, 2, 4), (1, 0, 2), (1, 2, 3), (1, 3, 4))
+        y_raw = [sbuf([last - first, N], F32, "y_raw%d" % k) for k, (g, first, last) in enumerate(y_parts)]
         xm_raw = [sbuf([PACK, D], F32, "xm_raw%d" % g) for g in range(PASSES)]
         v_tab = [sbuf([T], F32, "v_tab%d" % j) for j in range(D_TILES)]
         m_tab = [sbuf([T], F32, "m_tab%d" % j) for j in range(D_TILES)]
         v_win = [sbuf([T], F32, "v_win%d" % j) for j in range(D_TILES)]
         step_win = [sbuf([T], F32, "step_win%d" % j) for j in range(D_TILES)]
-        wt_sb = keep.tile([P, PASSES, PACK], F32, name="wt_sb")
+        wt_sb = keep.tile([P, PASSES, 2 * PACK], F32, name="wt_sb")[:, :, :PACK]
 
         def load_x(k):
             g, first, last = x_parts[k]
             rows = slice(g * K_PASS + PACK * first, g * K_PASS + PACK * last)
             nc.sync.dma_start(x_raw[k][:], xT[0, :, rows].rearrange("(p j) r -> p j r", j=PACK))
 
-        def load_y(g, pair):
+        def load_y(k):
+            g, first, last = y_parts[k]
             src = y[0, pass_rows(g), :].rearrange("(p t) n -> p t n", t=PACK)
-            nc.sync.dma_start(y_raw[g][pair][:], src[:, 2 * pair:2 * pair + 2, :])
+            nc.sync.dma_start(y_raw[k][:], src[:, first:last, :])
 
         def y_plane(g, t):
-            return y_raw[g][t // 2][:, t % 2, :]
+            k = [part[0] == g and part[1] <= t < part[2] for part in y_parts].index(True)
+            return y_raw[k][:, t - y_parts[k][1], :]
 
         def load_table(tile, table, j):
             nc.sync.dma_start(tile[:], table[block(j), :])
 
-        nc.scalar.dma_start(wt_sb[:], wt[0].rearrange("(g p t) o -> p g (t o)", p=P, t=PACK))
+        nc.scalar.dma_start(wt_sb, wt[0].rearrange("(g p t) o -> p g (t o)", p=P, t=PACK))
         nc.sync.dma_start(w_tab[0][:], w_planes[0])
         nc.sync.dma_start(offsets[:], offs)
         for t in range(1, PACK):
             nc.sync.dma_start(w_tab[t][:], w_planes[t])
         for k in range(len(x_parts)):
             load_x(k)
-        for g in range(PASSES):
-            load_y(g, 0)
-            load_y(g, 1)
+        for k in range(len(y_parts)):
+            load_y(k)
         for g in range(PASSES):
             nc.sync.dma_start(xm_raw[g][:], xm[0, pass_rows(g), :].rearrange("(p t) d -> p t d", t=PACK))
         for j in range(D_TILES):
@@ -125,7 +127,7 @@ def tile_attend_gsqh_adam_kernel(tc, xT, wT, y, wt, xm, mT, vT, offs, out_0, out
         eps = keep.tile([P, 1], F32, name="eps")
         nc.scalar.activation(eps[:], one[:], ACT.Copy, scale=(EPS / (LR * BETA)) ** 2)
         neg_wt = keep.tile([P, PASSES, PACK], F32, name="neg_wt")
-        nc.scalar.activation(neg_wt[:], wt_sb[:], ACT.Copy, scale=-1.0)
+        nc.scalar.activation(neg_wt[:], wt_sb, ACT.Copy, scale=-1.0)
 
         w_got = sbuf([PACK, N], F32, "w_got")
         nc.vector.tensor_copy(w_got[:, 0, :], listed(w_tab[0]))
@@ -174,7 +176,7 @@ def tile_attend_gsqh_adam_kernel(tc, xT, wT, y, wt, xm, mT, vT, offs, out_0, out
                 nc.scalar.activation(hinge[g][:, t, :], margin, ACT.Relu, bias=one[:], scale=-1.0)
         g_woven = []
         for g in range(PASSES):
-            g_woven.append(sbuf([PACK * N], BF16, "g_woven%d" % g, ("y_raw1_1", None)[g]))
+            g_woven.append(sbuf([PACK * N], BF16, "g_woven%d" % g, ("y_raw4", None)[g]))
             nc.vector.tensor_tensor(woven_view(g_woven[g][:], 2), planes_view(hinge[g][:], 2), planes_view(weight[g][:], 2), ALU.mult)
 
         def weave_xm(name, pieces, place=None):

import math
from contextlib import ExitStack

import concourse.mybir as mybir

N, T, D, R = 512, 1024, 512, 1024
LR, BETA, RHO, EPS = 0.1, 0.5, 0.9, 0.001
FLOPS = 2 * 2 * R * N * D

F32 = mybir.dt.float32
BF16 = mybir.dt.bfloat16
U32 = mybir.dt.uint32
U16 = mybir.dt.uint16
U8 = mybir.dt.uint8
E4M3 = mybir.dt.float8_e4m3fn_x4
E5M2 = mybir.dt.float8_e5m2_x4
ALU = mybir.AluOpType
ACT = mybir.ActivationFunctionType

P = 128
PACK = 4
K_PASS = P * PACK
PASSES = R // K_PASS
D_TILES = D // P
LIST_BAND = 16

assert D == K_PASS and N == K_PASS and PASSES == 2
assert BETA == 1.0 - BETA

W_ON_SCALAR = 192
X_ON_SCALAR = (56, 40, 20)
SHORT = 128
WEIGHTS_ON_SCALAR = ((0, 0), (0, 1), (1, 3))
M_ON_VECTOR = 512


def tile_attend_gsqh_adam_kernel(tc, xT, wT, y, wt, xm, mT, vT, offs, out_0, out_1, out_2):
    nc = tc.nc
    with ExitStack() as ctx:
        keep = ctx.enter_context(tc.tile_pool(name="keep", bufs=1))
        psum = ctx.enter_context(tc.psum_pool(name="psum", bufs=1))

        def sbuf(shape, dtype, name, place=None):
            return keep.tile([P] + shape, dtype, name=name, tag=place or name, align_bytes=64)

        def bank(place):
            return psum.tile([P, N], F32, name=place, tag=place)

        def woven_view(woven, run=PACK):
            return woven.rearrange("p (c i t) -> p c t i", i=run, t=PACK)

        def planes_view(planes, run=PACK):
            return planes.rearrange("p t (c i) -> p c t i", i=run)

        def quantize(codes, scales, woven, fmt):
            nc.vector.quantize_mx(out=codes.bitcast(fmt), scales=scales, in_=woven)

        def mx_tiles(name, width, place=None):
            return sbuf([width], U32, name + "_codes", place), sbuf([width], U8, name + "_scales")

        def pass_rows(g):
            return slice(g * K_PASS, (g + 1) * K_PASS)

        def block(n):
            return slice(n * P, (n + 1) * P)

        offsets = keep.tile([P, N // LIST_BAND], U16, name="offsets")

        def listed(tile, first=0, last=N):
            return tile[:].indirect(offsets[:, first // LIST_BAND:last // LIST_BAND])

        w_planes = wT.rearrange("(p t) c -> t p c", t=PACK)
        w_tab = [sbuf([T], F32, "w_tab%d" % t) for t in range(PACK)]
        x_parts = ((0, 0, P), (1, 0, P // 2), (1, P // 2, P))
        x_raw = [sbuf([PACK, PACK * (last - first)], F32, "x_raw%d" % k) for k, (g, first, last) in enumerate(x_parts)]
        y_parts = ((0, 0, 2), (0, 2, 4), (1, 0, 2), (1, 2, 3), (1, 3, 4))
        y_raw = [sbuf([last - first, N], F32, "y_raw%d" % k) for k, (g, first, last) in enumerate(y_parts)]
        xm_raw = [sbuf([PACK, D], F32, "xm_raw%d" % g) for g in range(PASSES)]
        v_tab = [sbuf([T], F32, "v_tab%d" % j) for j in range(D_TILES)]
        m_tab = [sbuf([T], F32, "m_tab%d" % j) for j in range(D_TILES)]
        v_win = [sbuf([T], F32, "v_win%d" % j) for j in range(D_TILES)]
        step_win = [sbuf([T], F32, "step_win%d" % j) for j in range(D_TILES)]
        wt_sb = keep.tile([P, PASSES, 2 * PACK], F32, name="wt_sb")[:, :, :PACK]

        def load_x(k):
            g, first, last = x_parts[k]
            rows = slice(g * K_PASS + PACK * first, g * K_PASS + PACK * last)
            nc.sync.dma_start(x_raw[k][:], xT[0, :, rows].rearrange("(p j) r -> p j r", j=PACK))

        def load_y(k):
            g, first, last = y_parts[k]
            src = y[0, pass_rows(g), :].rearrange("(p t) n -> p t n", t=PACK)
            nc.sync.dma_start(y_raw[k][:], src[:, first:last, :])

        def y_plane(g, t):
            k = [part[0] == g and part[1] <= t < part[2] for part in y_parts].index(True)
            return y_raw[k][:, t - y_parts[k][1], :]

        def load_table(tile, table, j):
            nc.sync.dma_start(tile[:], table[block(j), :])

        nc.scalar.dma_start(wt_sb, wt[0].rearrange("(g p t) o -> p g (t o)", p=P, t=PACK))
        nc.sync.dma_start(w_tab[0][:], w_planes[0])
        nc.sync.dma_start(offsets[:], offs)
        for t in range(1, PACK):
            nc.sync.dma_start(w_tab[t][:], w_planes[t])
        for k in range(len(x_parts)):
            load_x(k)
        for k in range(len(y_parts)):
            load_y(k)
        for g in range(PASSES):
            nc.sync.dma_start(xm_raw[g][:], xm[0, pass_rows(g), :].rearrange("(p t) d -> p t d", t=PACK))
        for j in range(D_TILES):
            load_table(v_tab[j], vT, j)
        load_table(m_tab[0], mT, 0)
        load_table(v_win[0], vT, 0)
        load_table(m_tab[2], mT, 2)
        for j in range(1, D_TILES):
            load_table(v_win[j], vT, j)

        one = keep.tile([P, 1], F32, name="one")
        nc.vector.memset(one[:], 1.0)
        for j in range(D_TILES):
            nc.gpsimd.memset(step_win[j][:], 0.0)
        tiny = keep.tile([P, 1], F32, name="tiny")
        nc.scalar.activation(tiny[:], one[:], ACT.Abs_reciprocal_sqrt, scale=1e28)
        eps = keep.tile([P, 1], F32, name="eps")
        nc.scalar.activation(eps[:], one[:], ACT.Copy, scale=(EPS / (LR * BETA)) ** 2)
        neg_wt = keep.tile([P, PASSES, PACK], F32, name="neg_wt")
        nc.scalar.activation(neg_wt[:], wt_sb, ACT.Copy, scale=-1.0)

        w_got = sbuf([PACK, N], F32, "w_got")
        nc.vector.tensor_copy(w_got[:, 0, :], listed(w_tab[0]))
        nc.scalar.activation(w_got[:, 1, :], listed(w_tab[1]), ACT.Copy)
        nc.vector.tensor_copy(w_got[:, 2, :], listed(w_tab[2]))
        nc.scalar.activation(w_got[:, 3, :W_ON_SCALAR], listed(w_tab[3], 0, W_ON_SCALAR), ACT.Copy)
        nc.vector.tensor_copy(w_got[:, 3, W_ON_SCALAR:], listed(w_tab[3], W_ON_SCALAR, N))
        w_woven = sbuf([PACK * N], BF16, "w_woven")
        nc.scalar.copy(woven_view(w_woven[:, :PACK * W_ON_SCALAR]), planes_view(w_got[:, :, :W_ON_SCALAR]))
        nc.vector.tensor_copy(woven_view(w_woven[:, PACK * W_ON_SCALAR:]), planes_view(w_got[:, :, W_ON_SCALAR:]))
        w_codes, w_scales = mx_tiles("w", N)
        quantize(w_codes[:], w_scales[:], w_woven[:], E4M3)

        m_win = [sbuf([T], F32, "m_win%d" % j, "w_tab%d" % j) for j in range(D_TILES)]
        for j in range(D_TILES):
            if j == 2:
                load_table(m_tab[1], mT, 1)
                load_table(m_tab[3], mT, 3)
            load_table(m_win[j], mT, j)

        x_q = []
        for g in range(PASSES):
            x_woven = sbuf([PACK * K_PASS], BF16, "x_woven%d" % g)
            dst = x_woven[:].rearrange("p (t s j) -> p s j t", t=PACK, j=PACK)
            for k, (part_pass, first, last) in enumerate(x_parts):
                if part_pass == g:
                    src = x_raw[k][:].rearrange("p j (s t) -> p s j t", t=PACK)
                    cut = X_ON_SCALAR[k]
                    nc.scalar.copy(dst[:, first:first + cut], src[:, :cut])
                    nc.vector.tensor_copy(dst[:, first + cut:last], src[:, cut:])
            x_q.append(mx_tiles("x%d" % g, K_PASS))
            quantize(x_q[g][0][:], x_q[g][1][:], x_woven[:], E4M3)
        hinge = [sbuf([PACK, N], F32, "hinge0"), sbuf([PACK, N], F32, "hinge1", "w_got")]
        weight = [sbuf([PACK, N], F32, "weight0", "x_raw0"), sbuf([PACK, N], F32, "weight1")]
        for g in range(PASSES):
            for t in range(PACK):
                scores = bank("bank_%s%d" % ("ab"[g], t))
                nc.tensor.matmul_mx(out=scores[:], lhsT=x_q[g][0][:, block(t)].bitcast(E4M3), lhsT_scale=x_q[g][1][:, block(t)],
                                    rhs=w_codes[:].bitcast(E4M3), rhs_scale=w_scales[:], start=True, stop=True)
                if (g, t) in WEIGHTS_ON_SCALAR:
                    nc.scalar.activation(weight[g][:, t, :], y_plane(g, t), ACT.Copy, scale=neg_wt[:, g, t:t + 1])
                else:
                    nc.gpsimd.tensor_scalar(weight[g][:, t, :], y_plane(g, t), neg_wt[:, g, t:t + 1], 0.0, ALU.mult, ALU.add)
                margin = hinge[g][:, t, :]
                nc.vector.tensor_tensor(margin, scores[:], y_plane(g, t), ALU.mult)
                nc.scalar.activation(hinge[g][:, t, :], margin, ACT.Relu, bias=one[:], scale=-1.0)
        g_woven = []
        for g in range(PASSES):
            g_woven.append(sbuf([PACK * N], BF16, "g_woven%d" % g, ("y_raw4", None)[g]))
            nc.vector.tensor_tensor(woven_view(g_woven[g][:], 2), planes_view(hinge[g][:], 2), planes_view(weight[g][:], 2), ALU.mult)

        def weave_xm(name, pieces, place=None):
            woven = sbuf([len(pieces), PACK * P], BF16, name + "_woven", place)
            for g in range(PASSES):
                ks = [k for k, piece in enumerate(pieces) if piece[1] == g]
                if ks:
                    j = pieces[ks[0]][0]
                    copy = nc.scalar.copy if j <= 1 else nc.vector.tensor_copy
                    copy(woven_view(woven[:, ks[0]:ks[-1] + 1, :].rearrange("p k c -> p (k c)")),
                         planes_view(xm_raw[g][:, :, j * P:(j + len(ks)) * P]))
            return woven

        xm_q = {}

        def quantize_xm(name, pieces, woven, place=None):
            codes, scales = mx_tiles(name, len(pieces) * P, place)
            quantize(codes[:], scales[:], woven[:].rearrange("p k c -> p (k c)"), E4M3)
            for k, piece in enumerate(pieces):
                xm_q[piece] = (codes[:, block(k)], scales[:, block(k)])

        g_q = [mx_tiles("g%d" % g, N) for g in range(PASSES)]
        dw = [bank("bank_a%d" % j) for j in range(D_TILES)]

        def dw_pass(j, g):
            nc.tensor.matmul_mx(out=dw[j][:], lhsT=xm_q[j, g][0].bitcast(E4M3), lhsT_scale=xm_q[j, g][1],
                                rhs=g_q[g][0][:].bitcast(E5M2), rhs_scale=g_q[g][1][:],
                                start=(g == 0), stop=(g == PASSES - 1))

        first, middle, last = [(0, 0), (0, 1)], [(1, 0), (2, 0), (3, 0), (1, 1)], [(2, 1), (3, 1)]
        xm_woven = weave_xm("xm0", first)
        quantize(g_q[0][0][:], g_q[0][1][:], g_woven[0][:], E5M2)
        quantize_xm("xm0", first, xm_woven)
        dw_pass(0, 0)
        quantize(g_q[1][0][:], g_q[1][1][:], g_woven[1][:], E5M2)
        dw_pass(0, 1)
        quantize_xm("xm1", middle, weave_xm("xm1", middle), "xm0_woven")
        quantize_xm("xm2", last, weave_xm("xm2", last, "g_woven1"))
        for j in range(1, D_TILES):
            for g in range(PASSES):
                dw_pass(j, g)

        def scatter_on_scalar(tiles):
            for first, last in ((0, SHORT), (SHORT, N)):
                for j in tiles:
                    nc.scalar.activation(listed(m_win[j], first, last), neg_nm[:, j, first:last], ACT.Copy, scale=-BETA)

        v_decayed = [sbuf([N], F32, "v_decayed%d" % j) for j in range(D_TILES)]
        for j in range(D_TILES):
            nc.scalar.activation(v_decayed[j][:], listed(v_tab[j]), ACT.Copy, scale=RHO)
        m_got = sbuf([D_TILES, N], F32, "m_got", "weight1")
        for j in range(D_TILES):
            cut = M_ON_VECTOR if j == 0 else 0
            if cut:
                nc.vector.tensor_copy(m_got[:, j, :cut], listed(m_tab[j], 0, cut))
            if cut < N:
                nc.scalar.activation(m_got[:, j, cut:], listed(m_tab[j], cut, N), ACT.Copy)
        nv = sbuf([2, 2, N], F32, "nv", "v_tab1")
        for j in range(D_TILES):
            nv_j = nv[:, j // 2, j % 2, :]
            nc.scalar.activation(nv_j, dw[j][:], ACT.Square, scale=math.sqrt(1.0 - RHO))
            nc.gpsimd.tensor_tensor(nv_j, nv_j, v_decayed[j][:], ALU.add)
        denom = []
        for pair, place in ((0, "xm2_codes"), (1, "m_tab2")):
            squared = sbuf([2, N], F32, "denom%d" % pair, place)
            nc.scalar.activation(squared[:], nv[:, pair], ACT.Abs_reciprocal_sqrt, scale=0.25 / EPS ** 2, bias=tiny[:])
            factor = sbuf([2, N], F32, "factor", "v_decayed3")
            nc.gpsimd.tensor_scalar(factor[:], squared[:], 1.0, 1.0, ALU.mult, ALU.add)
            nc.gpsimd.tensor_tensor(squared[:], factor[:], nv[:, pair], ALU.mult)
            denom.append(squared)
        for j in range(D_TILES):
            nv_j = nv[:, j // 2, j % 2, :]
            if j < D_TILES - 1:
                nc.vector.tensor_copy(listed(v_win[j]), nv_j)
            else:
                nc.scalar.activation(listed(v_win[j], SHORT, N), nv_j[:, SHORT:], ACT.Copy)
                nc.vector.tensor_copy(listed(v_win[j], 0, SHORT), nv_j[:, :SHORT])
            nc.sync.dma_start(out_2[block(j), :], v_win[j][:])
        held = sbuf([D_TILES + 2, N], F32, "held", "m_tab1")
        neg_nm, rate = held[:, :D_TILES, :], [held[:, D_TILES:, :], sbuf([2, N], F32, "rate23", "m_tab3")[:]]
        for j in range(D_TILES):
            nc.vector.scalar_tensor_tensor(neg_nm[:, j, :], dw[j][:], -1.0, m_got[:, j, :], ALU.mult, ALU.subtract)
        for pair in range(2):
            tiles = range(2 * pair, 2 * pair + 2)
            nc.scalar.activation(rate[pair], denom[pair][:], ACT.Abs_reciprocal_sqrt,
                                 scale=1.0 / (LR * BETA) ** 2, bias=eps[:])
            scatter_on_scalar(tiles)
            for j in tiles:
                nc.vector.tensor_tensor(listed(step_win[j]), neg_nm[:, j, :], rate[pair][:, j % 2, :], ALU.mult)
                nc.sync.dma_start(out_0[block(j), :], step_win[j][:])
                nc.sync.dma_start(out_1[block(j), :], m_win[j][:])
